import numpy as np
import ml_dtypes


def mxq(x, axis, fmt="e4m3"):
    dtype, down = {"e4m3": (ml_dtypes.float8_e4m3fn, 7), "e5m2": (ml_dtypes.float8_e5m2, 14)}[fmt]
    v = np.moveaxis(np.asarray(x, np.float32).astype(ml_dtypes.bfloat16).astype(np.float64), axis, -1)
    blocks = v.reshape(v.shape[:-1] + (-1, 32))
    amax = np.abs(blocks).max(-1, keepdims=True)
    byte = np.maximum(np.where(amax > 0, np.frexp(amax)[1] - 1 + 127, 0) - down, 1)
    scale = np.exp2(byte - 127.0)
    codes = (blocks / scale).astype(np.float32).astype(dtype).astype(np.float64)
    return np.moveaxis((codes * scale).reshape(v.shape), -1, axis)


WIDE = False


def mx_kscale(k):
    if not WIDE:
        return np.ones(k)
    levels = np.array([30, -30])
    if k % 512:
        return np.exp2(np.random.permutation(np.resize(levels, k // 32))).repeat(32)
    a = np.empty((k // 512, 16))
    for p in range(k // 512):
        a[p, :8] = np.random.permutation(np.resize(levels, 8))
        for g in range(8):
            far = levels[np.abs(levels - a[p, g]) >= 10]
            a[p, g + 8] = far[np.random.randint(len(far))]
    return np.exp2(a.ravel()).repeat(32)


def f64(x):
    return np.asarray(x).astype(np.float64)


def striped(idx):
    return np.tile(idx.reshape(-1, 16).T, (8, 1)).astype(np.uint16)


def unstriped(offs):
    return offs[:16].T.reshape(-1).astype(np.int64)


E2M1 = np.array([0.0, 0.5, 1.0, 1.5, 2.0, 3.0, 4.0, 6.0, -0.0, -0.5, -1.0, -1.5, -2.0, -3.0, -4.0, -6.0])


def pack_weight(w, fmt):
    k, n = w.shape
    w = f64(np.asarray(w, np.float32).astype(ml_dtypes.bfloat16)).reshape(k // 32, 32, n)
    amax = np.abs(w).max(1)
    if fmt == "e4m3":
        byte = np.frexp(amax)[1] - 1 + 127 - 7
    elif fmt == "e5m2":
        byte = np.frexp(amax)[1] - 1 + 127 - 14
    else:
        mant, ex = np.frexp(amax / 6.0)
        byte = np.where(mant > 0.5, ex, ex - 1) + 127
    byte = np.clip(np.where(amax > 0, byte, 1), 1, 254)
    scaled = (w * np.exp2(127.0 - byte)[:, None, :]).reshape(k, n).astype(np.float32)
    by_word = np.ascontiguousarray(scaled.reshape(k // 512, 128, 4, n).transpose(0, 1, 3, 2))
    if fmt == "e4m3":
        words = by_word.astype(ml_dtypes.float8_e4m3fn).view(np.uint8)
    elif fmt == "e5m2":
        words = by_word.astype(ml_dtypes.float8_e5m2).view(np.uint8)
    else:
        c = by_word.astype(ml_dtypes.float4_e2m1fn).view(np.uint8) & 0xF
        words = (c[..., 0::2] | (c[..., 1::2] << 4)).reshape(k // 512, 128, 2 * n)
    return np.ascontiguousarray(words), np.ascontiguousarray(byte.astype(np.uint8).reshape(k // 512, 16, n))


def unpack_weight(words, scales, fmt):
    g, _, n = scales.shape
    words = np.ascontiguousarray(words).reshape(g, 128, n, -1)
    if fmt == "e4m3":
        vals = words.view(ml_dtypes.float8_e4m3fn).astype(np.float64)
    elif fmt == "e5m2":
        vals = words.view(ml_dtypes.float8_e5m2).astype(np.float64)
    else:
        nib = np.empty((g, 128, n, 4), np.uint8)
        nib[..., 0::2] = words & 0xF
        nib[..., 1::2] = words >> 4
        vals = E2M1[nib]
    vals = vals * np.repeat(np.exp2(scales.astype(np.float64) - 127.0), 8, axis=1)[..., None]
    return vals.transpose(0, 1, 3, 2).reshape(g * 512, n)


def d_silu(v):
    s = 1.0 / (1.0 + np.exp(-np.maximum(v, -700.0)))
    return s * (1.0 + v * (1.0 - s))


K, T, E, C, H, N = 512, 1024, 4, 512, 512, 512


def by_expert(wq, xq):
    return np.concatenate([wq[e].T @ xq[:, e * C:(e + 1) * C] for e in range(E)], axis=1)


def setup_inputs():
    n = np.random.standard_normal
    v = mx_kscale(N)
    u = mx_kscale(H)
    first = np.random.permutation(np.repeat(np.arange(E), T // E))
    second = (first + 1 + np.random.permutation(np.repeat(np.arange(E - 1), -(-T // (E - 1)))[:T])) % E
    while np.bincount(second, minlength=E).max() != T // E:
        load = np.bincount(second, minlength=E); hi, lo = int(load.argmax()), int(load.argmin())
        t = np.flatnonzero((second == hi) & (first != lo))[0]; second[t] = lo
    slot_token = np.empty(E * C, np.int64); pos = np.empty((2, T), np.int64); fill = np.zeros(E, np.int64)
    place = np.stack([np.random.permutation(C) for _ in range(E)])
    for r, deal in enumerate((first, second)):
        for t in np.random.permutation(T):
            e = deal[t]; j = e * C + place[e, fill[e]]; fill[e] += 1; slot_token[j] = t; pos[r, t] = j
    g = np.random.uniform(0.2, 0.8, T)
    w_slot = np.empty(E * C); w_slot[pos[0]] = g; w_slot[pos[1]] = 1.0 - g
    dy = pack_weight(n((N, T)) * v[:, None], "e5m2")
    w2t = pack_weight(n((N, H)) / np.sqrt(N) / v[:, None] * u, "e2m1")
    w1t = [pack_weight(m, "e4m3") for m in n((E, H, K)) / np.sqrt(H) / u[None, :, None]]
    return {
        "dy_words": dy[0],
        "dy_scales": dy[1],
        "w2t_words": w2t[0],
        "w2t_scales": w2t[1],
        "w1t_words": np.stack([m[0] for m in w1t]),
        "w1t_scales": np.stack([m[1] for m in w1t]),
        "a": (n((H, E * C))).astype(np.float32),
        "gate": (np.tile(w_slot, (128, 1))).astype(np.float32),
        "offs": striped(slot_token),
        "pos1": striped(pos[0]),
        "pos2": striped(pos[1]),
    }


def reference(dy_words, dy_scales, w2t_words, w2t_scales, w1t_words, w1t_scales, a, gate, offs, pos1, pos2):
    w2t = unpack_weight(w2t_words, w2t_scales, "e2m1")
    w1t = np.stack([unpack_weight(w1t_words[e], w1t_scales[e], "e4m3") for e in range(E)])
    idx = unstriped(offs)
    dc = w2t.T @ unpack_weight(dy_words, dy_scales, "e5m2")
    da = f64(gate[:1]) * dc[:, idx] * d_silu(f64(a))
    dx = by_expert(w1t, mxq(da, 0, "e5m2"))
    out = dx[:, unstriped(pos1)] + dx[:, unstriped(pos2)]
    return out

@@ -1,0 +1,265 @@
+from contextlib import ExitStack
+
+import concourse.mybir as mybir
+from concourse.masks import make_identity
+
+K, T, E, C, H, N = 512, 1024, 4, 512, 512, 512
+S = E * C
+FLOPS = 2 * N * H * T + 2 * H * K * S
+
+F32 = mybir.dt.float32
+BF16 = mybir.dt.bfloat16
+I32 = mybir.dt.int32
+U32 = mybir.dt.uint32
+U16 = mybir.dt.uint16
+U8 = mybir.dt.uint8
+E2M1 = mybir.dt.float4_e2m1fn_x4
+E4M3 = mybir.dt.float8_e4m3fn_x4
+E5M2 = mybir.dt.float8_e5m2_x4
+ACT = mybir.ActivationFunctionType
+ALU = mybir.AluOpType
+
+P = 128
+PACK = 4
+BANK = 512
+BLOCKS = C // P
+PLAIN_EXPERTS = ()
+RUN = 2
+
+
+def tile_moe_sdb_silu_kernel(
+    tc, dy_words, dy_scales, w2t_words, w2t_scales, w1t_words, w1t_scales, a, gate, offs, pos1, pos2, out
+):
+    nc = tc.nc
+    with ExitStack() as ctx:
+        keep = ctx.enter_context(tc.tile_pool(name="keep", bufs=1))
+        ring = ctx.enter_context(tc.tile_pool(name="ring", bufs=2))
+        psum = ctx.enter_context(tc.psum_pool(name="psum", bufs=1))
+
+        offs_sb = keep.tile([P, S // 16], U16, name="offs_sb")
+        pos1_sb = keep.tile([P, T // 16], U16, name="pos1_sb")
+        pos2_sb = keep.tile([P, T // 16], U16, name="pos2_sb")
+
+        w2_raw = keep.tile([P, 2 * H], U8, name="w2_raw", align_bytes=64)
+        w2_sc_raw = keep.tile([P, H], U8, name="w2_sc_raw", align_bytes=64)
+        w2_codes = keep.tile([P, 2 * H], U8, name="w2_codes", align_bytes=64)
+        w2_sc = keep.tile([P, H], U8, name="w2_sc", align_bytes=64)
+        dy_codes = [keep.tile([P, 4 * BANK], U8, name="dy_codes%d" % h, align_bytes=64) for h in range(T // BANK)]
+        dy_sc = keep.tile([P, T], U8, name="dy_sc", align_bytes=64)
+        w1_codes = keep.tile([P, E, 4 * K], U8, name="w1_codes", align_bytes=64)
+        w1_sc = keep.tile([P, E * K], U8, name="w1_sc", align_bytes=64)
+        a_sb = [keep.tile([P, PACK, C], F32, name="a_sb%d" % e) for e in range(E)]
+        ident = keep.tile([P, P], F32, name="ident")
+        gate_rows = keep.tile([P, P], F32, name="gate_rows")
+
+        nc.vector.memset(w2_sc_raw[:].bitcast(I32), 0)
+        nc.vector.memset(dy_sc[:].bitcast(I32), 0)
+        nc.vector.memset(w1_sc[:].bitcast(I32), 0)
+        nc.gpsimd.memset(gate_rows[:], 0.0)
+        make_identity(nc, ident[:])
+
+        def load_scale_rows(plane, rows):
+            for r in range(4):
+                nc.sync.dma_start(out=plane[:].bitcast(I32)[r:P:32, :], in_=rows.bitcast(I32)[r:16:4, :])
+
+        a_rows = a.rearrange("(p t) j -> p t j", t=PACK)
+        dy_flat = dy_words[0].rearrange("p n d -> p (n d)").bitcast(I32)
+
+        nc.sync.dma_start(out=w2_raw[:].bitcast(I32), in_=w2t_words[0].bitcast(I32))
+        load_scale_rows(w2_sc_raw, w2t_scales[0])
+        load_scale_rows(dy_sc, dy_scales[0])
+        nc.sync.dma_start(out=dy_codes[0][:].bitcast(I32), in_=dy_flat[:, 0:BANK])
+        nc.sync.dma_start(out=a_sb[0][:, 0, :], in_=a_rows[:, 0, 0:C])
+        nc.sync.dma_start(out=dy_codes[1][:].bitcast(I32), in_=dy_flat[:, BANK:T])
+        nc.sync.dma_start(offs_sb[:], offs)
+        nc.sync.dma_start(out=a_sb[0][:, 1, :], in_=a_rows[:, 1, 0:C])
+        nc.sync.dma_start(out=a_sb[0][:, 2:PACK, :], in_=a_rows[:, 2:PACK, 0:C])
+        for e in range(1, E):
+            nc.sync.dma_start(out=a_sb[e][:], in_=a_rows[:, :, e * C : (e + 1) * C])
+        nc.sync.dma_start(out=gate_rows[0 : S // P, :], in_=gate[0].rearrange("(r c) -> r c", c=P))
+        gate_wide = {}
+        for e in PLAIN_EXPERTS:
+            gate_wide[e] = keep.tile([P, C], F32, name="gate_wide%d" % e)
+            nc.sync.dma_start(out=gate_wide[e][:], in_=gate[:, e * C : (e + 1) * C])
+        nc.sync.dma_start(
+            out=w1_codes[:].bitcast(I32), in_=w1t_words[:, 0].rearrange("e p k d -> p e (k d)").bitcast(I32)
+        )
+        w1_sc_rows = w1t_scales[:, 0].bitcast(I32).rearrange("e b k -> b e k")
+        w1_sc_view = w1_sc[:].bitcast(I32).rearrange("p (e k) -> p e k", e=E)
+        for r in range(4):
+            nc.sync.dma_start(out=w1_sc_view[r:P:32], in_=w1_sc_rows[r:16:4])
+        nc.sync.dma_start(pos1_sb[:], pos1)
+        nc.sync.dma_start(pos2_sb[:], pos2)
+
+        nc.vector.tensor_copy(
+            out=w2_codes[:].bitcast(U16).rearrange("p (t m) -> p t m", t=PACK),
+            in_=w2_raw[:].bitcast(U16).rearrange("p (m t) -> p t m", t=PACK),
+        )
+        nc.vector.tensor_copy(
+            out=w2_sc[:].rearrange("p (t m) -> p t m", t=PACK),
+            in_=w2_sc_raw[:].rearrange("p (m t) -> p t m", t=PACK),
+        )
+
+        sg = [keep.tile([P, PACK, C], F32, name="sg%d" % e) for e in range(E)]
+        dc = [keep.tile([P, T], F32, name="dc%d" % t) for t in range(PACK)]
+        for t in range(PACK):
+            nc.scalar.activation(out=sg[0][:, t, :], in_=a_sb[0][:, t, :], func=ACT.Sigmoid)
+            for h in range(T // BANK):
+                acc = psum.tile([P, BANK], F32, name="acc", tag="back", bufs=4)
+                nc.tensor.matmul_mx(
+                    out=acc[:],
+                    lhsT=w2_codes[:, 2 * P * t : 2 * P * (t + 1)].bitcast(E2M1),
+                    lhsT_scale=w2_sc[:, P * t : P * (t + 1)],
+                    rhs=dy_codes[h][:].bitcast(E5M2),
+                    rhs_scale=dy_sc[:, BANK * h : BANK * (h + 1)],
+                    start=True,
+                    stop=True,
+                )
+                if t < 3 and h == 0:
+                    nc.vector.tensor_copy(out=dc[t][:, BANK * h : BANK * (h + 1)], in_=acc[:])
+                else:
+                    nc.scalar.copy(out=dc[t][:, BANK * h : BANK * (h + 1)], in_=acc[:])
+        for e in range(1, E):
+            step = 2 if e == 1 else PACK
+            for t in range(0, PACK, step):
+                nc.scalar.activation(out=sg[e][:, t : t + step, :], in_=a_sb[e][:, t : t + step, :], func=ACT.Sigmoid)
+
+        gate_ps = psum.tile([P, BANK], F32, name="gate_ps", tag="turned", bufs=3)
+        nc.tensor.transpose(gate_ps[:, 0:P], gate_rows[:], ident[:])
+        g_col = keep.tile([P, S // P], F32, name="g_col")
+        neg_g_col = keep.tile([P, S // P], F32, name="neg_g_col")
+        nc.vector.tensor_copy(out=g_col[:], in_=gate_ps[:, 0 : S // P])
+        nc.vector.tensor_scalar(out=neg_g_col[:], in0=gate_ps[:, 0 : S // P], scalar1=-1.0, scalar2=None, op0=ALU.mult)
+
+        picked = {}
+        da_codes = [keep.tile([P, C], U32, name="da_codes%d" % e, align_bytes=64) for e in range(E)]
+        da_sc = [keep.tile([P, C], U8, name="da_sc%d" % e, align_bytes=64) for e in range(E)]
+        dx = [keep.tile([P, S], F32, name="dx%d" % m) for m in range(K // P)]
+
+        def gather_dc(e, factor):
+            picked[e] = ring.tile([P, PACK, C], F32, name="picked", tag="picked", bufs=3)
+            for t in range(PACK):
+                nc.vector.tensor_tensor(
+                    out=picked[e][:, t, :],
+                    in0=dc[t][:].indirect(offs_sb[:, e * C // 16 : (e + 1) * C // 16]),
+                    in1=factor[:, t, :],
+                    op=ALU.mult,
+                )
+
+        def woven(ap):
+            return ap.rearrange("p t (c i) -> p c t i", i=RUN)
+
+        def quantise(e, da, lo, hi):
+            nc.vector.quantize_mx(
+                out=da_codes[e][:, lo:hi].bitcast(E5M2),
+                scales=da_sc[e][:, lo:hi],
+                in_=da[:, lo:hi, :].rearrange("p j t -> p (j t)"),
+            )
+
+        def finish_turned(e):
+            da = ring.tile([P, C, PACK], BF16, name="da", tag="da", align_bytes=64)
+            for b in range(BLOCKS):
+                cols = slice(b * P, (b + 1) * P)
+                col = e * BLOCKS + b
+                turned = psum.tile([P, PACK, P], F32, name="turned", tag="turned", bufs=3)
+                for t in range(PACK):
+                    nc.tensor.transpose(turned[:, t, :], a_sb[e][:, t, cols], ident[:])
+                u = ring.tile([P, PACK, P], F32, name="u", tag="u", bufs=3)
+                nc.scalar.activation(out=u[:], in_=turned[:], func=ACT.Silu, scale=-1.0)
+                gw = ring.tile([P, PACK, P], F32, name="gw", tag="gw", bufs=6)
+                nc.scalar.activation(
+                    out=gw[:], in_=u[:], func=ACT.Identity, scale=neg_g_col[:, col : col + 1], bias=g_col[:, col : col + 1]
+                )
+                back = psum.tile([P, PACK, P], F32, name="back", tag="back", bufs=4)
+                for t in range(PACK):
+                    nc.tensor.transpose(back[:, t, :], gw[:, t, :], ident[:])
+                nc.vector.tensor_tensor(
+                    out=da[:, cols, :].rearrange("p (c i) t -> p c t i", i=RUN),
+                    in0=woven(picked[e][:, :, cols]),
+                    in1=woven(back[:]),
+                    op=ALU.mult,
+                )
+                if e == E - 1:
+                    quantise(e, da, b * P, (b + 1) * P)
+            if e != E - 1:
+                quantise(e, da, 0, C)
+
+        def plain_factor(e):
+            u_wide = ring.tile([P, PACK, C], F32, name="u_wide", tag="u_wide", bufs=1)
+            nc.scalar.activation(out=u_wide[:], in_=a_sb[e][:], func=ACT.Silu, scale=-1.0)
+            nc.vector.tensor_scalar(
+                out=gate_wide[e][:], in0=gate_wide[e][:], scalar1=-1.0, scalar2=None, op0=ALU.mult
+            )
+            nc.vector.scalar_tensor_tensor(
+                out=u_wide[:], in0=u_wide[:], scalar=1.0, in1=sg[e][:], op0=ALU.subtract, op1=ALU.mult
+            )
+            return u_wide
+
+        def finish_plain(e):
+            da = ring.tile([P, C, PACK], BF16, name="da", tag="da", align_bytes=64)
+            g_view = gate_wide[e][:].rearrange("p (c i) -> p c i", i=RUN).unsqueeze(2).to_broadcast([P, C // RUN, PACK, RUN])
+            nc.vector.tensor_tensor(
+                out=da[:].rearrange("p (c i) t -> p c t i", i=RUN), in0=woven(picked[e][:]), in1=g_view, op=ALU.mult
+            )
+            quantise(e, da, 0, C)
+
+        def expert_product(e, m):
+            if m == 0:
+                acc = psum.tile([P, BANK], F32, name="acc", tag="acc", bufs=1)
+            else:
+                acc = psum.tile([P, BANK], F32, name="acc", tag="turned", bufs=3)
+            nc.tensor.matmul_mx(
+                out=acc[:],
+                lhsT=w1_codes[:, e, 4 * P * m : 4 * P * (m + 1)].bitcast(E4M3),
+                lhsT_scale=w1_sc[:, e * K + P * m : e * K + P * (m + 1)],
+                rhs=da_codes[e][:].bitcast(E5M2),
+                rhs_scale=da_sc[e][:],
+                start=True,
+                stop=True,
+            )
+            if e == E - 1 and m == 0:
+                nc.vector.tensor_copy(out=dx[m][:, e * C : (e + 1) * C], in_=acc[:])
+            else:
+                nc.scalar.copy(out=dx[m][:, e * C : (e + 1) * C], in_=acc[:])
+
+        def start_expert(e):
+            gather_dc(e, plain_factor(e) if e in PLAIN_EXPERTS else sg[e])
+
+        def finish_expert(e):
+            if e in PLAIN_EXPERTS:
+                finish_plain(e)
+            else:
+                finish_turned(e)
+            expert_product(e, 0)
+
+        start_expert(0)
+        start_expert(1)
+        start_expert(2)
+        finish_expert(0)
+        start_expert(3)
+        finish_expert(1)
+        finish_expert(2)
+        finish_expert(3)
+
+        half = T // 2
+        for m in range(K // P):
+            if m + 1 < K // P:
+                for e in range(E):
+                    expert_product(e, m + 1)
+            first = ring.tile([P, T], F32, name="first", tag="first")
+            both = ring.tile([P, T], F32, name="both", tag="both")
+            for lo in range(0, T, half):
+                nc.vector.tensor_copy(
+                    out=first[:, lo : lo + half], in_=dx[m][:].indirect(pos1_sb[:, lo // 16 : (lo + half) // 16])
+                )
+            widths = (half, half) if m + 1 < K // P else (half, half // 2, half // 2)
+            lo = 0
+            for w in widths:
+                nc.vector.tensor_tensor(
+                    out=both[:, lo : lo + w],
+                    in0=dx[m][:].indirect(pos2_sb[:, lo // 16 : (lo + w) // 16]),
+                    in1=first[:, lo : lo + w],
+                    op=ALU.add,
+                )
+                nc.sync.dma_start(out=out[m * P : (m + 1) * P, lo : lo + w], in_=both[:, lo : lo + w])
+                lo = lo + w

@@ -23,7 +23,8 @@ P = 128
 PACK = 4
 BANK = 512
 BLOCKS = C // P
-PLAIN_EXPERTS = ()
+PLAIN_EXPERTS = (3,)
+LAST = 2
 RUN = 2
 
 
@@ -44,7 +45,7 @@ def tile_moe_sdb_silu_kernel(
         w2_sc_raw = keep.tile([P, H], U8, name="w2_sc_raw", align_bytes=64)
         w2_codes = keep.tile([P, 2 * H], U8, name="w2_codes", align_bytes=64)
         w2_sc = keep.tile([P, H], U8, name="w2_sc", align_bytes=64)
-        dy_codes = [keep.tile([P, 4 * BANK], U8, name="dy_codes%d" % h, align_bytes=64) for h in range(T // BANK)]
+        dy_codes = keep.tile([P, 4 * T], U8, name="dy_codes", align_bytes=64)
         dy_sc = keep.tile([P, T], U8, name="dy_sc", align_bytes=64)
         w1_codes = keep.tile([P, E, 4 * K], U8, name="w1_codes", align_bytes=64)
         w1_sc = keep.tile([P, E * K], U8, name="w1_sc", align_bytes=64)
@@ -52,25 +53,25 @@ def tile_moe_sdb_silu_kernel(
         ident = keep.tile([P, P], F32, name="ident")
         gate_rows = keep.tile([P, P], F32, name="gate_rows")
 
-        nc.vector.memset(w2_sc_raw[:].bitcast(I32), 0)
-        nc.vector.memset(dy_sc[:].bitcast(I32), 0)
+        nc.gpsimd.memset(w2_sc_raw[:].bitcast(I32), 0)
+        nc.gpsimd.memset(dy_sc[:].bitcast(I32), 0)
         nc.vector.memset(w1_sc[:].bitcast(I32), 0)
         nc.gpsimd.memset(gate_rows[:], 0.0)
         make_identity(nc, ident[:])
 
-        def load_scale_rows(plane, rows):
-            for r in range(4):
+        def load_scale_rows(plane, rows, lo, hi):
+            for r in range(lo, hi):
                 nc.sync.dma_start(out=plane[:].bitcast(I32)[r:P:32, :], in_=rows.bitcast(I32)[r:16:4, :])
 
         a_rows = a.rearrange("(p t) j -> p t j", t=PACK)
         dy_flat = dy_words[0].rearrange("p n d -> p (n d)").bitcast(I32)
 
         nc.sync.dma_start(out=w2_raw[:].bitcast(I32), in_=w2t_words[0].bitcast(I32))
-        load_scale_rows(w2_sc_raw, w2t_scales[0])
-        load_scale_rows(dy_sc, dy_scales[0])
-        nc.sync.dma_start(out=dy_codes[0][:].bitcast(I32), in_=dy_flat[:, 0:BANK])
+        load_scale_rows(w2_sc_raw, w2t_scales[0], 0, 1)
+        nc.sync.dma_start(out=dy_codes[:].bitcast(I32), in_=dy_flat)
+        load_scale_rows(w2_sc_raw, w2t_scales[0], 1, 4)
+        load_scale_rows(dy_sc, dy_scales[0], 0, 4)
         nc.sync.dma_start(out=a_sb[0][:, 0, :], in_=a_rows[:, 0, 0:C])
-        nc.sync.dma_start(out=dy_codes[1][:].bitcast(I32), in_=dy_flat[:, BANK:T])
         nc.sync.dma_start(offs_sb[:], offs)
         nc.sync.dma_start(out=a_sb[0][:, 1, :], in_=a_rows[:, 1, 0:C])
         nc.sync.dma_start(out=a_sb[0][:, 2:PACK, :], in_=a_rows[:, 2:PACK, 0:C])
@@ -102,6 +103,16 @@ def tile_moe_sdb_silu_kernel(
 
         sg = [keep.tile([P, PACK, C], F32, name="sg%d" % e) for e in range(E)]
         dc = [keep.tile([P, T], F32, name="dc%d" % t) for t in range(PACK)]
+        picked = [keep.tile([P, PACK, C], F32, name="picked%d" % e) for e in range(E)]
+
+        def gather_plane(e, t, factor):
+            nc.vector.tensor_tensor(
+                out=picked[e][:, t, :],
+                in0=dc[t][:].indirect(offs_sb[:, e * C // 16 : (e + 1) * C // 16]),
+                in1=factor[:, t, :],
+                op=ALU.mult,
+            )
+
         for t in range(PACK):
             nc.scalar.activation(out=sg[0][:, t, :], in_=a_sb[0][:, t, :], func=ACT.Sigmoid)
             for h in range(T // BANK):
@@ -110,15 +121,16 @@ def tile_moe_sdb_silu_kernel(
                     out=acc[:],
                     lhsT=w2_codes[:, 2 * P * t : 2 * P * (t + 1)].bitcast(E2M1),
                     lhsT_scale=w2_sc[:, P * t : P * (t + 1)],
-                    rhs=dy_codes[h][:].bitcast(E5M2),
+                    rhs=dy_codes[:, 4 * BANK * h : 4 * BANK * (h + 1)].bitcast(E5M2),
                     rhs_scale=dy_sc[:, BANK * h : BANK * (h + 1)],
                     start=True,
                     stop=True,
                 )
-                if t < 3 and h == 0:
+                if t < 2 and h == 0:
                     nc.vector.tensor_copy(out=dc[t][:, BANK * h : BANK * (h + 1)], in_=acc[:])
                 else:
                     nc.scalar.copy(out=dc[t][:, BANK * h : BANK * (h + 1)], in_=acc[:])
+            gather_plane(0, t, sg[0])
         for e in range(1, E):
             step = 2 if e == 1 else PACK
             for t in range(0, PACK, step):
@@ -131,20 +143,13 @@ def tile_moe_sdb_silu_kernel(
         nc.vector.tensor_copy(out=g_col[:], in_=gate_ps[:, 0 : S // P])
         nc.vector.tensor_scalar(out=neg_g_col[:], in0=gate_ps[:, 0 : S // P], scalar1=-1.0, scalar2=None, op0=ALU.mult)
 
-        picked = {}
         da_codes = [keep.tile([P, C], U32, name="da_codes%d" % e, align_bytes=64) for e in range(E)]
         da_sc = [keep.tile([P, C], U8, name="da_sc%d" % e, align_bytes=64) for e in range(E)]
         dx = [keep.tile([P, S], F32, name="dx%d" % m) for m in range(K // P)]
 
         def gather_dc(e, factor):
-            picked[e] = ring.tile([P, PACK, C], F32, name="picked", tag="picked", bufs=3)
             for t in range(PACK):
-                nc.vector.tensor_tensor(
-                    out=picked[e][:, t, :],
-                    in0=dc[t][:].indirect(offs_sb[:, e * C // 16 : (e + 1) * C // 16]),
-                    in1=factor[:, t, :],
-                    op=ALU.mult,
-                )
+                gather_plane(e, t, factor)
 
         def woven(ap):
             return ap.rearrange("p t (c i) -> p c t i", i=RUN)
@@ -179,13 +184,13 @@ def tile_moe_sdb_silu_kernel(
                     in1=woven(back[:]),
                     op=ALU.mult,
                 )
-                if e == E - 1:
+                if e == LAST:
                     quantise(e, da, b * P, (b + 1) * P)
-            if e != E - 1:
+            if e != LAST:
                 quantise(e, da, 0, C)
 
         def plain_factor(e):
-            u_wide = ring.tile([P, PACK, C], F32, name="u_wide", tag="u_wide", bufs=1)
+            u_wide = a_sb[e]
             nc.scalar.activation(out=u_wide[:], in_=a_sb[e][:], func=ACT.Silu, scale=-1.0)
             nc.vector.tensor_scalar(
                 out=gate_wide[e][:], in0=gate_wide[e][:], scalar1=-1.0, scalar2=None, op0=ALU.mult
@@ -217,7 +222,7 @@ def tile_moe_sdb_silu_kernel(
                 start=True,
                 stop=True,
             )
-            if e == E - 1 and m == 0:
+            if e == LAST and m == 0:
                 nc.vector.tensor_copy(out=dx[m][:, e * C : (e + 1) * C], in_=acc[:])
             else:
                 nc.scalar.copy(out=dx[m][:, e * C : (e + 1) * C], in_=acc[:])
@@ -232,14 +237,13 @@ def tile_moe_sdb_silu_kernel(
                 finish_turned(e)
             expert_product(e, 0)
 
-        start_expert(0)
         start_expert(1)
         start_expert(2)
-        finish_expert(0)
         start_expert(3)
+        finish_expert(0)
+        finish_expert(3)
         finish_expert(1)
         finish_expert(2)
-        finish_expert(3)
 
         half = T // 2
         for m in range(K // P):

@@ -4,8 +4,8 @@ import concourse.mybir as mybir
 from concourse.masks import make_identity
 
 K, T, E, C, H, N = 512, 1024, 4, 512, 512, 512
-S = E * C
-FLOPS = 2 * N * H * T + 2 * H * K * S
+SLOTS = E * C
+FLOPS = 2 * N * H * T + 2 * H * K * SLOTS
 
 F32 = mybir.dt.float32
 BF16 = mybir.dt.bfloat16
@@ -23,9 +23,19 @@ P = 128
 PACK = 4
 BANK = 512
 BLOCKS = C // P
-PLAIN_EXPERTS = (3,)
-LAST = 2
-RUN = 2
+ROW_BLOCKS = K // P
+PER_COLUMN = 16
+QUADRANT = 32
+GROUP = 4
+SCALE_ROWS = 16
+RUN = 4
+
+PLAIN = 3
+TURNED = (0, 1, 2)
+LAST = TURNED[-1]
+
+OUT_OF_BANKS, AHEAD_BANKS = 4, 3
+VECTOR_DC_PLANES = 2
 
 
 def tile_moe_sdb_silu_kernel(
@@ -37,17 +47,17 @@ def tile_moe_sdb_silu_kernel(
         ring = ctx.enter_context(tc.tile_pool(name="ring", bufs=2))
         psum = ctx.enter_context(tc.psum_pool(name="psum", bufs=1))
 
-        offs_sb = keep.tile([P, S // 16], U16, name="offs_sb")
-        pos1_sb = keep.tile([P, T // 16], U16, name="pos1_sb")
-        pos2_sb = keep.tile([P, T // 16], U16, name="pos2_sb")
+        offs_sb = keep.tile([P, SLOTS // PER_COLUMN], U16, name="offs_sb")
+        pos1_sb = keep.tile([P, T // PER_COLUMN], U16, name="pos1_sb")
+        pos2_sb = keep.tile([P, T // PER_COLUMN], U16, name="pos2_sb")
 
         w2_raw = keep.tile([P, 2 * H], U8, name="w2_raw", align_bytes=64)
         w2_sc_raw = keep.tile([P, H], U8, name="w2_sc_raw", align_bytes=64)
         w2_codes = keep.tile([P, 2 * H], U8, name="w2_codes", align_bytes=64)
         w2_sc = keep.tile([P, H], U8, name="w2_sc", align_bytes=64)
-        dy_codes = keep.tile([P, 4 * T], U8, name="dy_codes", align_bytes=64)
+        dy_codes = keep.tile([P, PACK * T], U8, name="dy_codes", align_bytes=64)
         dy_sc = keep.tile([P, T], U8, name="dy_sc", align_bytes=64)
-        w1_codes = keep.tile([P, E, 4 * K], U8, name="w1_codes", align_bytes=64)
+        w1_codes = keep.tile([P, E, PACK * K], U8, name="w1_codes", align_bytes=64)
         w1_sc = keep.tile([P, E * K], U8, name="w1_sc", align_bytes=64)
         a_sb = [keep.tile([P, PACK, C], F32, name="a_sb%d" % e) for e in range(E)]
         ident = keep.tile([P, P], F32, name="ident")
@@ -59,36 +69,33 @@ def tile_moe_sdb_silu_kernel(
         nc.gpsimd.memset(gate_rows[:], 0.0)
         make_identity(nc, ident[:])
 
-        def load_scale_rows(plane, rows, lo, hi):
-            for r in range(lo, hi):
-                nc.sync.dma_start(out=plane[:].bitcast(I32)[r:P:32, :], in_=rows.bitcast(I32)[r:16:4, :])
+        def load_scale_rows(plane, rows, first, last):
+            for r in range(first, last):
+                nc.sync.dma_start(out=plane[r:P:QUADRANT], in_=rows[r:SCALE_ROWS:GROUP])
 
-        a_rows = a.rearrange("(p t) j -> p t j", t=PACK)
-        dy_flat = dy_words[0].rearrange("p n d -> p (n d)").bitcast(I32)
-
+        a_planes = a.rearrange("(p t) j -> p t j", t=PACK)
+        dy_sc_rows = dy_scales[0].bitcast(I32)
         nc.sync.dma_start(out=w2_raw[:].bitcast(I32), in_=w2t_words[0].bitcast(I32))
-        load_scale_rows(w2_sc_raw, w2t_scales[0], 0, 1)
-        nc.sync.dma_start(out=dy_codes[:].bitcast(I32), in_=dy_flat)
-        load_scale_rows(w2_sc_raw, w2t_scales[0], 1, 4)
-        load_scale_rows(dy_sc, dy_scales[0], 0, 4)
-        nc.sync.dma_start(out=a_sb[0][:, 0, :], in_=a_rows[:, 0, 0:C])
+        load_scale_rows(w2_sc_raw[:].bitcast(I32), w2t_scales[0].bitcast(I32), 0, GROUP)
+        load_scale_rows(dy_sc[:].bitcast(I32), dy_sc_rows, 0, GROUP // 2)
+        nc.sync.dma_start(out=dy_codes[:].bitcast(I32), in_=dy_words[0].rearrange("p n d -> p (n d)").bitcast(I32))
+        load_scale_rows(dy_sc[:].bitcast(I32), dy_sc_rows, GROUP // 2, GROUP)
+        nc.sync.dma_start(out=a_sb[0][:, 0, :], in_=a_planes[:, 0, 0:C])
         nc.sync.dma_start(offs_sb[:], offs)
-        nc.sync.dma_start(out=a_sb[0][:, 1, :], in_=a_rows[:, 1, 0:C])
-        nc.sync.dma_start(out=a_sb[0][:, 2:PACK, :], in_=a_rows[:, 2:PACK, 0:C])
+        nc.sync.dma_start(out=a_sb[0][:, 1, :], in_=a_planes[:, 1, 0:C])
+        nc.sync.dma_start(out=a_sb[0][:, 2:PACK, :], in_=a_planes[:, 2:PACK, 0:C])
         for e in range(1, E):
-            nc.sync.dma_start(out=a_sb[e][:], in_=a_rows[:, :, e * C : (e + 1) * C])
-        nc.sync.dma_start(out=gate_rows[0 : S // P, :], in_=gate[0].rearrange("(r c) -> r c", c=P))
-        gate_wide = {}
-        for e in PLAIN_EXPERTS:
-            gate_wide[e] = keep.tile([P, C], F32, name="gate_wide%d" % e)
-            nc.sync.dma_start(out=gate_wide[e][:], in_=gate[:, e * C : (e + 1) * C])
+            nc.sync.dma_start(out=a_sb[e][:], in_=a_planes[:, :, e * C : (e + 1) * C])
+        nc.sync.dma_start(out=gate_rows[0 : SLOTS // P, :], in_=gate[0].rearrange("(r c) -> r c", c=P))
         nc.sync.dma_start(
             out=w1_codes[:].bitcast(I32), in_=w1t_words[:, 0].rearrange("e p k d -> p e (k d)").bitcast(I32)
         )
-        w1_sc_rows = w1t_scales[:, 0].bitcast(I32).rearrange("e b k -> b e k")
-        w1_sc_view = w1_sc[:].bitcast(I32).rearrange("p (e k) -> p e k", e=E)
-        for r in range(4):
-            nc.sync.dma_start(out=w1_sc_view[r:P:32], in_=w1_sc_rows[r:16:4])
+        load_scale_rows(
+            w1_sc[:].bitcast(I32).rearrange("p (e k) -> p e k", e=E),
+            w1t_scales[:, 0].bitcast(I32).rearrange("e b k -> b e k"),
+            0,
+            GROUP,
+        )
         nc.sync.dma_start(pos1_sb[:], pos1)
         nc.sync.dma_start(pos2_sb[:], pos2)
 
@@ -105,10 +112,13 @@ def tile_moe_sdb_silu_kernel(
         dc = [keep.tile([P, T], F32, name="dc%d" % t) for t in range(PACK)]
         picked = [keep.tile([P, PACK, C], F32, name="picked%d" % e) for e in range(E)]
 
+        def entries(list_sb, first, count):
+            return list_sb[:, first // PER_COLUMN : (first + count) // PER_COLUMN]
+
         def gather_plane(e, t, factor):
             nc.vector.tensor_tensor(
                 out=picked[e][:, t, :],
-                in0=dc[t][:].indirect(offs_sb[:, e * C // 16 : (e + 1) * C // 16]),
+                in0=dc[t][:].indirect(entries(offs_sb, e * C, C)),
                 in1=factor[:, t, :],
                 op=ALU.mult,
             )
@@ -116,43 +126,56 @@ def tile_moe_sdb_silu_kernel(
         for t in range(PACK):
             nc.scalar.activation(out=sg[0][:, t, :], in_=a_sb[0][:, t, :], func=ACT.Sigmoid)
             for h in range(T // BANK):
-                acc = psum.tile([P, BANK], F32, name="acc", tag="back", bufs=4)
+                tokens = slice(BANK * h, BANK * (h + 1))
+                dc_ps = psum.tile([P, BANK], F32, name="dc_ps", tag="out_of", bufs=OUT_OF_BANKS)
                 nc.tensor.matmul_mx(
-                    out=acc[:],
+                    out=dc_ps[:],
                     lhsT=w2_codes[:, 2 * P * t : 2 * P * (t + 1)].bitcast(E2M1),
                     lhsT_scale=w2_sc[:, P * t : P * (t + 1)],
-                    rhs=dy_codes[:, 4 * BANK * h : 4 * BANK * (h + 1)].bitcast(E5M2),
-                    rhs_scale=dy_sc[:, BANK * h : BANK * (h + 1)],
+                    rhs=dy_codes[:, PACK * BANK * h : PACK * BANK * (h + 1)].bitcast(E5M2),
+                    rhs_scale=dy_sc[:, tokens],
                     start=True,
                     stop=True,
                 )
-                if t < 2 and h == 0:
-                    nc.vector.tensor_copy(out=dc[t][:, BANK * h : BANK * (h + 1)], in_=acc[:])
+                if t < VECTOR_DC_PLANES and h == 0:
+                    nc.vector.tensor_copy(out=dc[t][:, tokens], in_=dc_ps[:])
                 else:
-                    nc.scalar.copy(out=dc[t][:, BANK * h : BANK * (h + 1)], in_=acc[:])
+                    nc.scalar.copy(out=dc[t][:, tokens], in_=dc_ps[:])
             gather_plane(0, t, sg[0])
-        for e in range(1, E):
-            step = 2 if e == 1 else PACK
-            for t in range(0, PACK, step):
-                nc.scalar.activation(out=sg[e][:, t : t + step, :], in_=a_sb[e][:, t : t + step, :], func=ACT.Sigmoid)
 
-        gate_ps = psum.tile([P, BANK], F32, name="gate_ps", tag="turned", bufs=3)
+        for e in range(1, E):
+            planes = PACK // 2 if e == 1 else PACK
+            for t in range(0, PACK, planes):
+                nc.scalar.activation(
+                    out=sg[e][:, t : t + planes, :], in_=a_sb[e][:, t : t + planes, :], func=ACT.Sigmoid
+                )
+
+        gate_ps = psum.tile([P, BANK], F32, name="gate_ps", tag="ahead", bufs=AHEAD_BANKS)
         nc.tensor.transpose(gate_ps[:, 0:P], gate_rows[:], ident[:])
-        g_col = keep.tile([P, S // P], F32, name="g_col")
-        neg_g_col = keep.tile([P, S // P], F32, name="neg_g_col")
-        nc.vector.tensor_copy(out=g_col[:], in_=gate_ps[:, 0 : S // P])
-        nc.vector.tensor_scalar(out=neg_g_col[:], in0=gate_ps[:, 0 : S // P], scalar1=-1.0, scalar2=None, op0=ALU.mult)
+        g_col = keep.tile([P, SLOTS // P], F32, name="g_col")
+        neg_g_col = keep.tile([P, SLOTS // P], F32, name="neg_g_col")
+        nc.vector.tensor_copy(out=g_col[:], in_=gate_ps[:, 0 : SLOTS // P])
+        nc.vector.tensor_scalar(
+            out=neg_g_col[:], in0=gate_ps[:, 0 : SLOTS // P], scalar1=-1.0, scalar2=None, op0=ALU.mult
+        )
 
         da_codes = [keep.tile([P, C], U32, name="da_codes%d" % e, align_bytes=64) for e in range(E)]
         da_sc = [keep.tile([P, C], U8, name="da_sc%d" % e, align_bytes=64) for e in range(E)]
-        dx = [keep.tile([P, S], F32, name="dx%d" % m) for m in range(K // P)]
+        dx = [keep.tile([P, SLOTS], F32, name="dx%d" % m) for m in range(ROW_BLOCKS)]
 
-        def gather_dc(e, factor):
-            for t in range(PACK):
-                gather_plane(e, t, factor)
+        def in_runs(planes_ap):
+            return planes_ap.rearrange("p t (c i) -> p c t i", i=RUN)
 
-        def woven(ap):
-            return ap.rearrange("p t (c i) -> p c t i", i=RUN)
+        def round_block(da, e, cols, factor_in_runs):
+            nc.vector.tensor_tensor(
+                out=da[:, cols, :].rearrange("p (c i) t -> p c t i", i=RUN),
+                in0=in_runs(picked[e][:, :, cols]),
+                in1=factor_in_runs,
+                op=ALU.mult,
+            )
+
+        def new_da():
+            return ring.tile([P, C, PACK], BF16, name="da", tag="da", bufs=3, align_bytes=64)
 
         def quantise(e, da, lo, hi):
             nc.vector.quantize_mx(
@@ -161,109 +184,114 @@ def tile_moe_sdb_silu_kernel(
                 in_=da[:, lo:hi, :].rearrange("p j t -> p (j t)"),
             )
 
-        def finish_turned(e):
-            da = ring.tile([P, C, PACK], BF16, name="da", tag="da", align_bytes=64)
+        def turned_block(da, e, b):
+            cols = slice(b * P, (b + 1) * P)
+            r = e * BLOCKS + b
+            a_turned = psum.tile([P, PACK, P], F32, name="a_turned", tag="ahead", bufs=AHEAD_BANKS)
+            for t in range(PACK):
+                nc.tensor.transpose(a_turned[:, t, :], a_sb[e][:, t, cols], ident[:])
+            u = ring.tile([P, PACK, P], F32, name="u", tag="u", bufs=3)
+            nc.scalar.activation(out=u[:], in_=a_turned[:], func=ACT.Silu, scale=-1.0)
+            gw = ring.tile([P, PACK, P], F32, name="gw", tag="gw", bufs=6)
+            nc.scalar.activation(
+                out=gw[:], in_=u[:], func=ACT.Identity, scale=neg_g_col[:, r : r + 1], bias=g_col[:, r : r + 1]
+            )
+            gw_back = psum.tile([P, PACK, P], F32, name="gw_back", tag="out_of", bufs=OUT_OF_BANKS)
+            for t in range(PACK):
+                nc.tensor.transpose(gw_back[:, t, :], gw[:, t, :], ident[:])
+            round_block(da, e, cols, in_runs(gw_back[:]))
+
+        def plain_factor():
+            for t in range(0, PACK, PACK // 2):
+                part = a_sb[PLAIN][:, t : t + PACK // 2, :]
+                nc.scalar.activation(out=part, in_=part, func=ACT.Silu, scale=-1.0)
+                nc.vector.scalar_tensor_tensor(
+                    out=part,
+                    in0=part,
+                    scalar=1.0,
+                    in1=sg[PLAIN][:, t : t + PACK // 2, :],
+                    op0=ALU.subtract,
+                    op1=ALU.mult,
+                )
+            return a_sb[PLAIN]
+
+        def finish_plain(da):
+            neg_g = psum.tile([P, C], F32, name="neg_g", tag="single", bufs=1)
+            for b in range(BLOCKS):
+                r = PLAIN * BLOCKS + b
+                nc.tensor.transpose(
+                    neg_g[:, b * P : (b + 1) * P], neg_g_col[:, r : r + 1].to_broadcast([P, P]), ident[:]
+                )
             for b in range(BLOCKS):
                 cols = slice(b * P, (b + 1) * P)
-                col = e * BLOCKS + b
-                turned = psum.tile([P, PACK, P], F32, name="turned", tag="turned", bufs=3)
-                for t in range(PACK):
-                    nc.tensor.transpose(turned[:, t, :], a_sb[e][:, t, cols], ident[:])
-                u = ring.tile([P, PACK, P], F32, name="u", tag="u", bufs=3)
-                nc.scalar.activation(out=u[:], in_=turned[:], func=ACT.Silu, scale=-1.0)
-                gw = ring.tile([P, PACK, P], F32, name="gw", tag="gw", bufs=6)
-                nc.scalar.activation(
-                    out=gw[:], in_=u[:], func=ACT.Identity, scale=neg_g_col[:, col : col + 1], bias=g_col[:, col : col + 1]
-                )
-                back = psum.tile([P, PACK, P], F32, name="back", tag="back", bufs=4)
-                for t in range(PACK):
-                    nc.tensor.transpose(back[:, t, :], gw[:, t, :], ident[:])
-                nc.vector.tensor_tensor(
-                    out=da[:, cols, :].rearrange("p (c i) t -> p c t i", i=RUN),
-                    in0=woven(picked[e][:, :, cols]),
-                    in1=woven(back[:]),
-                    op=ALU.mult,
-                )
-                if e == LAST:
-                    quantise(e, da, b * P, (b + 1) * P)
-            if e != LAST:
-                quantise(e, da, 0, C)
-
-        def plain_factor(e):
-            u_wide = a_sb[e]
-            nc.scalar.activation(out=u_wide[:], in_=a_sb[e][:], func=ACT.Silu, scale=-1.0)
-            nc.vector.tensor_scalar(
-                out=gate_wide[e][:], in0=gate_wide[e][:], scalar1=-1.0, scalar2=None, op0=ALU.mult
-            )
-            nc.vector.scalar_tensor_tensor(
-                out=u_wide[:], in0=u_wide[:], scalar=1.0, in1=sg[e][:], op0=ALU.subtract, op1=ALU.mult
-            )
-            return u_wide
-
-        def finish_plain(e):
-            da = ring.tile([P, C, PACK], BF16, name="da", tag="da", align_bytes=64)
-            g_view = gate_wide[e][:].rearrange("p (c i) -> p c i", i=RUN).unsqueeze(2).to_broadcast([P, C // RUN, PACK, RUN])
-            nc.vector.tensor_tensor(
-                out=da[:].rearrange("p (c i) t -> p c t i", i=RUN), in0=woven(picked[e][:]), in1=g_view, op=ALU.mult
-            )
-            quantise(e, da, 0, C)
+                neg_g_runs = neg_g[:, cols].rearrange("p (c i) -> p c i", i=RUN).unsqueeze(2)
+                round_block(da, PLAIN, cols, neg_g_runs.to_broadcast([P, P // RUN, PACK, RUN]))
 
         def expert_product(e, m):
-            if m == 0:
-                acc = psum.tile([P, BANK], F32, name="acc", tag="acc", bufs=1)
+            awaited = e == LAST and m == 0
+            if awaited:
+                dx_ps = psum.tile([P, BANK], F32, name="dx_ps", tag="single", bufs=1)
             else:
-                acc = psum.tile([P, BANK], F32, name="acc", tag="turned", bufs=3)
+                dx_ps = psum.tile([P, BANK], F32, name="dx_ps", tag="ahead", bufs=AHEAD_BANKS)
             nc.tensor.matmul_mx(
-                out=acc[:],
-                lhsT=w1_codes[:, e, 4 * P * m : 4 * P * (m + 1)].bitcast(E4M3),
+                out=dx_ps[:],
+                lhsT=w1_codes[:, e, PACK * P * m : PACK * P * (m + 1)].bitcast(E4M3),
                 lhsT_scale=w1_sc[:, e * K + P * m : e * K + P * (m + 1)],
                 rhs=da_codes[e][:].bitcast(E5M2),
                 rhs_scale=da_sc[e][:],
                 start=True,
                 stop=True,
             )
-            if e == LAST and m == 0:
-                nc.vector.tensor_copy(out=dx[m][:, e * C : (e + 1) * C], in_=acc[:])
+            if awaited:
+                nc.vector.tensor_copy(out=dx[m][:, e * C : (e + 1) * C], in_=dx_ps[:])
             else:
-                nc.scalar.copy(out=dx[m][:, e * C : (e + 1) * C], in_=acc[:])
+                nc.scalar.copy(out=dx[m][:, e * C : (e + 1) * C], in_=dx_ps[:])
 
-        def start_expert(e):
-            gather_dc(e, plain_factor(e) if e in PLAIN_EXPERTS else sg[e])
+        for e in range(1, E):
+            factor = plain_factor() if e == PLAIN else sg[e]
+            for t in range(PACK):
+                gather_plane(e, t, factor)
 
-        def finish_expert(e):
-            if e in PLAIN_EXPERTS:
-                finish_plain(e)
-            else:
-                finish_turned(e)
-            expert_product(e, 0)
-
-        start_expert(1)
-        start_expert(2)
-        start_expert(3)
-        finish_expert(0)
-        finish_expert(3)
-        finish_expert(1)
-        finish_expert(2)
+        da_first = new_da()
+        for b in range(BLOCKS):
+            turned_block(da_first, TURNED[0], b)
+        da_plain = new_da()
+        finish_plain(da_plain)
+        quantise(TURNED[0], da_first, 0, C)
+        waiting, da_waiting = PLAIN, da_plain
+        for e in TURNED[1:]:
+            da = new_da()
+            for b in range(BLOCKS):
+                turned_block(da, e, b)
+                if b == 0:
+                    quantise(waiting, da_waiting, 0, C)
+                if e == LAST and b == BLOCKS - 2:
+                    quantise(e, da, 0, b * P)
+            waiting, da_waiting = e, da
+        for b in range(BLOCKS - 2, BLOCKS):
+            quantise(LAST, da_waiting, b * P, (b + 1) * P)
+        for e in range(E):
+            if e != LAST:
+                expert_product(e, 0)
+        expert_product(LAST, 0)
 
         half = T // 2
-        for m in range(K // P):
-            if m + 1 < K // P:
+        for m in range(ROW_BLOCKS):
+            final = m + 1 == ROW_BLOCKS
+            if not final:
                 for e in range(E):
                     expert_product(e, m + 1)
             first = ring.tile([P, T], F32, name="first", tag="first")
             both = ring.tile([P, T], F32, name="both", tag="both")
             for lo in range(0, T, half):
-                nc.vector.tensor_copy(
-                    out=first[:, lo : lo + half], in_=dx[m][:].indirect(pos1_sb[:, lo // 16 : (lo + half) // 16])
-                )
-            widths = (half, half) if m + 1 < K // P else (half, half // 2, half // 2)
+                nc.vector.tensor_copy(out=first[:, lo : lo + half], in_=dx[m][:].indirect(entries(pos1_sb, lo, half)))
             lo = 0
-            for w in widths:
+            for width in (half, half // 2, half // 2) if final else (half, half):
                 nc.vector.tensor_tensor(
-                    out=both[:, lo : lo + w],
-                    in0=dx[m][:].indirect(pos2_sb[:, lo // 16 : (lo + w) // 16]),
-                    in1=first[:, lo : lo + w],
+                    out=both[:, lo : lo + width],
+                    in0=dx[m][:].indirect(entries(pos2_sb, lo, width)),
+                    in1=first[:, lo : lo + width],
                     op=ALU.add,
                 )
-                nc.sync.dma_start(out=out[m * P : (m + 1) * P, lo : lo + w], in_=both[:, lo : lo + w])
-                lo = lo + w
+                nc.sync.dma_start(out=out[m * P : (m + 1) * P, lo : lo + width], in_=both[:, lo : lo + width])
+                lo = lo + width

@@ -34,7 +34,7 @@ PLAIN = 3
 TURNED = (0, 1, 2)
 LAST = TURNED[-1]
 
-OUT_OF_BANKS, AHEAD_BANKS = 4, 3
+OUT_OF_BANKS, AHEAD_BANKS = 3, 4
 VECTOR_DC_PLANES = 2
 
 
@@ -193,9 +193,19 @@ def tile_moe_sdb_silu_kernel(
             u = ring.tile([P, PACK, P], F32, name="u", tag="u", bufs=3)
             nc.scalar.activation(out=u[:], in_=a_turned[:], func=ACT.Silu, scale=-1.0)
             gw = ring.tile([P, PACK, P], F32, name="gw", tag="gw", bufs=6)
-            nc.scalar.activation(
-                out=gw[:], in_=u[:], func=ACT.Identity, scale=neg_g_col[:, r : r + 1], bias=g_col[:, r : r + 1]
-            )
+            if e != LAST:
+                nc.scalar.activation(
+                    out=gw[:], in_=u[:], func=ACT.Identity, scale=neg_g_col[:, r : r + 1], bias=g_col[:, r : r + 1]
+                )
+            else:
+                nc.gpsimd.tensor_scalar(
+                    out=gw[:],
+                    in0=u[:],
+                    scalar1=neg_g_col[:, r : r + 1],
+                    scalar2=g_col[:, r : r + 1],
+                    op0=ALU.mult,
+                    op1=ALU.add,
+                )
             gw_back = psum.tile([P, PACK, P], F32, name="gw_back", tag="out_of", bufs=OUT_OF_BANKS)
             for t in range(PACK):
                 nc.tensor.transpose(gw_back[:, t, :], gw[:, t, :], ident[:])

@@ -30,11 +30,14 @@ GROUP = 4
 SCALE_ROWS = 16
 RUN = 4
 
+BANKS = 8
 PLAIN = 3
 TURNED = (0, 1, 2)
-LAST = TURNED[-1]
-
-OUT_OF_BANKS, AHEAD_BANKS = 3, 4
+FINISH_ORDER = (PLAIN,) + TURNED
+GATE_BANK = 7
+BACK_BANKS = (5, 6, 0, 1)
+PRODUCT_BANKS = (7, 2, 3, 4)
+SCALAR_GATES = 4
 VECTOR_DC_PLANES = 2
 
 
@@ -44,7 +47,6 @@ def tile_moe_sdb_silu_kernel(
     nc = tc.nc
     with ExitStack() as ctx:
         keep = ctx.enter_context(tc.tile_pool(name="keep", bufs=1))
-        ring = ctx.enter_context(tc.tile_pool(name="ring", bufs=2))
         psum = ctx.enter_context(tc.psum_pool(name="psum", bufs=1))
 
         offs_sb = keep.tile([P, SLOTS // PER_COLUMN], U16, name="offs_sb")
@@ -110,16 +112,19 @@ def tile_moe_sdb_silu_kernel(
 
         sg = [keep.tile([P, PACK, C], F32, name="sg%d" % e) for e in range(E)]
         dc = [keep.tile([P, T], F32, name="dc%d" % t) for t in range(PACK)]
-        picked = [keep.tile([P, PACK, C], F32, name="picked%d" % e) for e in range(E)]
+        picked_flat = [keep.tile([P, PACK * C], F32, name="picked%d" % e) for e in range(E)]
+        picked = [x[:].rearrange("p (t j) -> p t j", t=PACK) for x in picked_flat]
+        u_tiles = [keep.tile([P, PACK * P], F32, name="u%d" % n) for n in range(len(TURNED) * BLOCKS)]
+        bank = [psum.tile([P, BANK], F32, name="bank%d" % n) for n in range(BANKS)]
 
         def entries(list_sb, first, count):
             return list_sb[:, first // PER_COLUMN : (first + count) // PER_COLUMN]
 
-        def gather_plane(e, t, factor):
+        def gather_plane(e, t):
             nc.vector.tensor_tensor(
-                out=picked[e][:, t, :],
+                out=picked_flat[e][:, t * C : (t + 1) * C],
                 in0=dc[t][:].indirect(entries(offs_sb, e * C, C)),
-                in1=factor[:, t, :],
+                in1=(a_sb if e == PLAIN else sg)[e][:, t, :],
                 op=ALU.mult,
             )
 
@@ -127,7 +132,7 @@ def tile_moe_sdb_silu_kernel(
             nc.scalar.activation(out=sg[0][:, t, :], in_=a_sb[0][:, t, :], func=ACT.Sigmoid)
             for h in range(T // BANK):
                 tokens = slice(BANK * h, BANK * (h + 1))
-                dc_ps = psum.tile([P, BANK], F32, name="dc_ps", tag="out_of", bufs=OUT_OF_BANKS)
+                dc_ps = bank[2 * t + h]
                 nc.tensor.matmul_mx(
                     out=dc_ps[:],
                     lhsT=w2_codes[:, 2 * P * t : 2 * P * (t + 1)].bitcast(E2M1),
@@ -141,7 +146,7 @@ def tile_moe_sdb_silu_kernel(
                     nc.vector.tensor_copy(out=dc[t][:, tokens], in_=dc_ps[:])
                 else:
                     nc.scalar.copy(out=dc[t][:, tokens], in_=dc_ps[:])
-            gather_plane(0, t, sg[0])
+            gather_plane(0, t)
 
         for e in range(1, E):
             planes = PACK // 2 if e == 1 else PACK
@@ -149,159 +154,162 @@ def tile_moe_sdb_silu_kernel(
                 nc.scalar.activation(
                     out=sg[e][:, t : t + planes, :], in_=a_sb[e][:, t : t + planes, :], func=ACT.Sigmoid
                 )
+            for t in range(PACK):
+                if e == PLAIN:
+                    part = a_sb[e][:, t, :]
+                    nc.scalar.activation(out=part, in_=part, func=ACT.Silu, scale=-1.0)
+                    nc.vector.scalar_tensor_tensor(
+                        out=part, in0=part, scalar=1.0, in1=sg[e][:, t, :], op0=ALU.subtract, op1=ALU.mult
+                    )
+                gather_plane(e, t)
 
-        gate_ps = psum.tile([P, BANK], F32, name="gate_ps", tag="ahead", bufs=AHEAD_BANKS)
+        gate_ps = bank[GATE_BANK]
         nc.tensor.transpose(gate_ps[:, 0:P], gate_rows[:], ident[:])
         g_col = keep.tile([P, SLOTS // P], F32, name="g_col")
         neg_g_col = keep.tile([P, SLOTS // P], F32, name="neg_g_col")
-        nc.vector.tensor_copy(out=g_col[:], in_=gate_ps[:, 0 : SLOTS // P])
-        nc.vector.tensor_scalar(
-            out=neg_g_col[:], in0=gate_ps[:, 0 : SLOTS // P], scalar1=-1.0, scalar2=None, op0=ALU.mult
-        )
+        nc.scalar.copy(out=g_col[:], in_=gate_ps[:, 0 : SLOTS // P])
+        nc.scalar.mul(out=neg_g_col[:], in_=gate_ps[:, 0 : SLOTS // P], mul=-1.0)
 
         da_codes = [keep.tile([P, C], U32, name="da_codes%d" % e, align_bytes=64) for e in range(E)]
         da_sc = [keep.tile([P, C], U8, name="da_sc%d" % e, align_bytes=64) for e in range(E)]
+        da = [keep.tile([P, C, PACK], BF16, name="da%d" % e, align_bytes=64) for e in range(E)]
         dx = [keep.tile([P, SLOTS], F32, name="dx%d" % m) for m in range(ROW_BLOCKS)]
 
         def in_runs(planes_ap):
             return planes_ap.rearrange("p t (c i) -> p c t i", i=RUN)
 
-        def round_block(da, e, cols, factor_in_runs):
-            nc.vector.tensor_tensor(
-                out=da[:, cols, :].rearrange("p (c i) t -> p c t i", i=RUN),
-                in0=in_runs(picked[e][:, :, cols]),
-                in1=factor_in_runs,
-                op=ALU.mult,
-            )
+        def planes_of(bank_tile):
+            return bank_tile[:].rearrange("p (t s) -> p t s", t=PACK)
 
-        def new_da():
-            return ring.tile([P, C, PACK], BF16, name="da", tag="da", bufs=3, align_bytes=64)
-
-        def quantise(e, da, lo, hi):
+        def quantise(e, lo, hi):
             nc.vector.quantize_mx(
                 out=da_codes[e][:, lo:hi].bitcast(E5M2),
                 scales=da_sc[e][:, lo:hi],
-                in_=da[:, lo:hi, :].rearrange("p j t -> p (j t)"),
+                in_=da[e][:, lo:hi, :].rearrange("p j t -> p (j t)"),
             )
 
-        def turned_block(da, e, b):
+        def turned_block(n):
+            e, b = TURNED[n // BLOCKS], n % BLOCKS
             cols = slice(b * P, (b + 1) * P)
-            r = e * BLOCKS + b
-            a_turned = psum.tile([P, PACK, P], F32, name="a_turned", tag="ahead", bufs=AHEAD_BANKS)
+            a_bank = bank[n % GATE_BANK]
+            a_turned = planes_of(a_bank)
             for t in range(PACK):
                 nc.tensor.transpose(a_turned[:, t, :], a_sb[e][:, t, cols], ident[:])
-            u = ring.tile([P, PACK, P], F32, name="u", tag="u", bufs=3)
-            nc.scalar.activation(out=u[:], in_=a_turned[:], func=ACT.Silu, scale=-1.0)
-            gw = ring.tile([P, PACK, P], F32, name="gw", tag="gw", bufs=6)
-            if e != LAST:
+            u = u_tiles[n][:]
+            nc.scalar.activation(out=u, in_=a_bank[:], func=ACT.Silu, scale=-1.0)
+
+        def gate_block(n):
+            e, b = TURNED[n // BLOCKS], n % BLOCKS
+            r = e * BLOCKS + b
+            u = u_tiles[n][:]
+            if n < SCALAR_GATES:
+                gw = u
                 nc.scalar.activation(
-                    out=gw[:], in_=u[:], func=ACT.Identity, scale=neg_g_col[:, r : r + 1], bias=g_col[:, r : r + 1]
+                    out=gw, in_=u, func=ACT.Identity, scale=neg_g_col[:, r : r + 1], bias=g_col[:, r : r + 1]
                 )
             else:
-                nc.gpsimd.tensor_scalar(
-                    out=gw[:],
-                    in0=u[:],
+                gw = u
+                nc.vector.tensor_scalar(
+                    out=gw,
+                    in0=u,
                     scalar1=neg_g_col[:, r : r + 1],
                     scalar2=g_col[:, r : r + 1],
                     op0=ALU.mult,
                     op1=ALU.add,
                 )
-            gw_back = psum.tile([P, PACK, P], F32, name="gw_back", tag="out_of", bufs=OUT_OF_BANKS)
+            return gw
+
+        def back_block(n, gw):
+            e, b = TURNED[n // BLOCKS], n % BLOCKS
+            gw_back = planes_of(bank[BACK_BANKS[n % len(BACK_BANKS)]])
             for t in range(PACK):
-                nc.tensor.transpose(gw_back[:, t, :], gw[:, t, :], ident[:])
-            round_block(da, e, cols, in_runs(gw_back[:]))
+                nc.tensor.transpose(gw_back[:, t, :], gw[:, t * P : (t + 1) * P], ident[:])
+            round_block(e, b, in_runs(gw_back))
 
-        def plain_factor():
-            for t in range(0, PACK, PACK // 2):
-                part = a_sb[PLAIN][:, t : t + PACK // 2, :]
-                nc.scalar.activation(out=part, in_=part, func=ACT.Silu, scale=-1.0)
-                nc.vector.scalar_tensor_tensor(
-                    out=part,
-                    in0=part,
-                    scalar=1.0,
-                    in1=sg[PLAIN][:, t : t + PACK // 2, :],
-                    op0=ALU.subtract,
-                    op1=ALU.mult,
-                )
-            return a_sb[PLAIN]
+        def round_block(e, b, factor_in_runs):
+            cols = slice(b * P, (b + 1) * P)
+            nc.vector.tensor_tensor(
+                out=da[e][:, cols, :].rearrange("p (c i) t -> p c t i", i=RUN),
+                in0=in_runs(picked[e][:, :, cols]),
+                in1=factor_in_runs,
+                op=ALU.mult,
+            )
 
-        def finish_plain(da):
-            neg_g = psum.tile([P, C], F32, name="neg_g", tag="single", bufs=1)
+        def finish_plain():
+            neg_g = bank[GATE_BANK]
             for b in range(BLOCKS):
                 r = PLAIN * BLOCKS + b
                 nc.tensor.transpose(
                     neg_g[:, b * P : (b + 1) * P], neg_g_col[:, r : r + 1].to_broadcast([P, P]), ident[:]
                 )
-            for b in range(BLOCKS):
-                cols = slice(b * P, (b + 1) * P)
-                neg_g_runs = neg_g[:, cols].rearrange("p (c i) -> p c i", i=RUN).unsqueeze(2)
-                round_block(da, PLAIN, cols, neg_g_runs.to_broadcast([P, P // RUN, PACK, RUN]))
+            runs = neg_g[:].rearrange("p (c i) -> p c i", i=RUN).unsqueeze(2)
+            nc.vector.tensor_tensor(
+                out=da[PLAIN][:].rearrange("p (c i) t -> p c t i", i=RUN),
+                in0=in_runs(picked[PLAIN]),
+                in1=runs.to_broadcast([P, C // RUN, PACK, RUN]),
+                op=ALU.mult,
+            )
 
-        def expert_product(e, m):
-            awaited = e == LAST and m == 0
-            if awaited:
-                dx_ps = psum.tile([P, BANK], F32, name="dx_ps", tag="single", bufs=1)
-            else:
-                dx_ps = psum.tile([P, BANK], F32, name="dx_ps", tag="ahead", bufs=AHEAD_BANKS)
+        def expert_product(e, m, lo, hi, on_vector):
+            dx_ps = bank[PRODUCT_BANKS[m]]
             nc.tensor.matmul_mx(
-                out=dx_ps[:],
+                out=dx_ps[:, lo:hi],
                 lhsT=w1_codes[:, e, PACK * P * m : PACK * P * (m + 1)].bitcast(E4M3),
                 lhsT_scale=w1_sc[:, e * K + P * m : e * K + P * (m + 1)],
-                rhs=da_codes[e][:].bitcast(E5M2),
-                rhs_scale=da_sc[e][:],
+                rhs=da_codes[e][:, lo:hi].bitcast(E5M2),
+                rhs_scale=da_sc[e][:, lo:hi],
                 start=True,
                 stop=True,
             )
-            if awaited:
-                nc.vector.tensor_copy(out=dx[m][:, e * C : (e + 1) * C], in_=dx_ps[:])
+            if on_vector:
+                nc.vector.tensor_copy(out=dx[m][:, e * C + lo : e * C + hi], in_=dx_ps[:, lo:hi])
             else:
-                nc.scalar.copy(out=dx[m][:, e * C : (e + 1) * C], in_=dx_ps[:])
+                nc.scalar.copy(out=dx[m][:, e * C + lo : e * C + hi], in_=dx_ps[:, lo:hi])
 
-        for e in range(1, E):
-            factor = plain_factor() if e == PLAIN else sg[e]
-            for t in range(PACK):
-                gather_plane(e, t, factor)
-
-        da_first = new_da()
-        for b in range(BLOCKS):
-            turned_block(da_first, TURNED[0], b)
-        da_plain = new_da()
-        finish_plain(da_plain)
-        quantise(TURNED[0], da_first, 0, C)
-        waiting, da_waiting = PLAIN, da_plain
-        for e in TURNED[1:]:
-            da = new_da()
-            for b in range(BLOCKS):
-                turned_block(da, e, b)
-                if b == 0:
-                    quantise(waiting, da_waiting, 0, C)
-                if e == LAST and b == BLOCKS - 2:
-                    quantise(e, da, 0, b * P)
-            waiting, da_waiting = e, da
-        for b in range(BLOCKS - 2, BLOCKS):
-            quantise(LAST, da_waiting, b * P, (b + 1) * P)
-        for e in range(E):
-            if e != LAST:
-                expert_product(e, 0)
-        expert_product(LAST, 0)
+        last = FINISH_ORDER[-1]
+        turned_blocks = len(TURNED) * BLOCKS
+        finish_plain()
+        gated = {}
+        for n in range(turned_blocks):
+            turned_block(n)
+            if n < SCALAR_GATES:
+                gated[n] = gate_block(n)
+        for n in range(turned_blocks):
+            back_block(n, gated[n] if n in gated else gate_block(n))
+            if n % BLOCKS == 0:
+                quantise(FINISH_ORDER[n // BLOCKS], 0, C)
+            if n == turned_blocks - 2:
+                quantise(last, 0, C // 2)
+        quantise(last, C // 2, C)
+        for e in FINISH_ORDER[:-1]:
+            for m in range(ROW_BLOCKS):
+                expert_product(e, m, 0, C, False)
+        for m in range(ROW_BLOCKS):
+            expert_product(last, m, 0, C // 2, False)
+        for m in range(2):
+            expert_product(last, m, C // 2, C, m == 0)
 
         half = T // 2
+        first = [picked_flat[m][:, 0:T] for m in range(ROW_BLOCKS)]
+        both = [picked_flat[m][:, T : 2 * T] for m in range(ROW_BLOCKS)]
         for m in range(ROW_BLOCKS):
             final = m + 1 == ROW_BLOCKS
-            if not final:
-                for e in range(E):
-                    expert_product(e, m + 1)
-            first = ring.tile([P, T], F32, name="first", tag="first")
-            both = ring.tile([P, T], F32, name="both", tag="both")
-            for lo in range(0, T, half):
-                nc.vector.tensor_copy(out=first[:, lo : lo + half], in_=dx[m][:].indirect(entries(pos1_sb, lo, half)))
+            piece = half
+            for lo in range(0, T, piece):
+                window = dx[m][:].indirect(entries(pos1_sb, lo, piece))
+                if m == 0 and lo == 0:
+                    nc.vector.tensor_copy(out=first[m][:, lo : lo + piece], in_=window)
+                else:
+                    nc.scalar.activation(out=first[m][:, lo : lo + piece], in_=window, func=ACT.Copy)
+                if lo == 0 and 0 < m < ROW_BLOCKS - 1:
+                    expert_product(last, m + 1, C // 2, C, False)
             lo = 0
             for width in (half, half // 2, half // 2) if final else (half, half):
                 nc.vector.tensor_tensor(
-                    out=both[:, lo : lo + width],
+                    out=both[m][:, lo : lo + width],
                     in0=dx[m][:].indirect(entries(pos2_sb, lo, width)),
-                    in1=first[:, lo : lo + width],
+                    in1=first[m][:, lo : lo + width],
                     op=ALU.add,
                 )
-                nc.sync.dma_start(out=out[m * P : (m + 1) * P, lo : lo + width], in_=both[:, lo : lo + width])
+                nc.sync.dma_start(out=out[m * P : (m + 1) * P, lo : lo + width], in_=both[m][:, lo : lo + width])
                 lo = lo + width

@@ -33,11 +33,12 @@ RUN = 4
 BANKS = 8
 PLAIN = 3
 TURNED = (0, 1, 2)
-FINISH_ORDER = (PLAIN,) + TURNED
+PLAIN_AFTER = 8
 GATE_BANK = 7
 BACK_BANKS = (5, 6, 0, 1)
 PRODUCT_BANKS = (7, 2, 3, 4)
 SCALAR_GATES = 4
+VECTOR_FIRST = 512
 VECTOR_DC_PLANES = 2
 
 
@@ -181,6 +182,9 @@ def tile_moe_sdb_silu_kernel(
         def planes_of(bank_tile):
             return bank_tile[:].rearrange("p (t s) -> p t s", t=PACK)
 
+        def back_bank(turn):
+            return bank[BACK_BANKS[turn % len(BACK_BANKS)]]
+
         def quantise(e, lo, hi):
             nc.vector.quantize_mx(
                 out=da_codes[e][:, lo:hi].bitcast(E5M2),
@@ -208,8 +212,9 @@ def tile_moe_sdb_silu_kernel(
                     out=gw, in_=u, func=ACT.Identity, scale=neg_g_col[:, r : r + 1], bias=g_col[:, r : r + 1]
                 )
             else:
-                gw = u
-                nc.vector.tensor_scalar(
+                place = n - SCALAR_GATES
+                gw = dc[PACK - 1 - place // 2][:, BANK * (place % 2) : BANK * (place % 2 + 1)]
+                nc.gpsimd.tensor_scalar(
                     out=gw,
                     in0=u,
                     scalar1=neg_g_col[:, r : r + 1],
@@ -221,7 +226,7 @@ def tile_moe_sdb_silu_kernel(
 
         def back_block(n, gw):
             e, b = TURNED[n // BLOCKS], n % BLOCKS
-            gw_back = planes_of(bank[BACK_BANKS[n % len(BACK_BANKS)]])
+            gw_back = planes_of(back_bank(n + (n >= PLAIN_AFTER)))
             for t in range(PACK):
                 nc.tensor.transpose(gw_back[:, t, :], gw[:, t * P : (t + 1) * P], ident[:])
             round_block(e, b, in_runs(gw_back))
@@ -236,7 +241,7 @@ def tile_moe_sdb_silu_kernel(
             )
 
         def finish_plain():
-            neg_g = bank[GATE_BANK]
+            neg_g = back_bank(PLAIN_AFTER)
             for b in range(BLOCKS):
                 r = PLAIN * BLOCKS + b
                 nc.tensor.transpose(
@@ -250,8 +255,9 @@ def tile_moe_sdb_silu_kernel(
                 op=ALU.mult,
             )
 
-        def expert_product(e, m, lo, hi, on_vector):
-            dx_ps = bank[PRODUCT_BANKS[m]]
+        def expert_product(e, m, lo, hi, on_vector, dx_ps=None):
+            if dx_ps is None:
+                dx_ps = bank[PRODUCT_BANKS[m]]
             nc.tensor.matmul_mx(
                 out=dx_ps[:, lo:hi],
                 lhsT=w1_codes[:, e, PACK * P * m : PACK * P * (m + 1)].bitcast(E4M3),
@@ -266,43 +272,56 @@ def tile_moe_sdb_silu_kernel(
             else:
                 nc.scalar.copy(out=dx[m][:, e * C + lo : e * C + hi], in_=dx_ps[:, lo:hi])
 
-        last = FINISH_ORDER[-1]
+        last = TURNED[-1]
         turned_blocks = len(TURNED) * BLOCKS
-        finish_plain()
         gated = {}
         for n in range(turned_blocks):
             turned_block(n)
             if n < SCALAR_GATES:
                 gated[n] = gate_block(n)
+        waiting = None
         for n in range(turned_blocks):
+            if n == PLAIN_AFTER:
+                finish_plain()
+                quantise(waiting, 0, C)
+                for m in range(ROW_BLOCKS):
+                    expert_product(waiting, m, 0, C, False)
+                waiting = PLAIN
             back_block(n, gated[n] if n in gated else gate_block(n))
-            if n % BLOCKS == 0:
-                quantise(FINISH_ORDER[n // BLOCKS], 0, C)
+            if waiting is not None:
+                if n % BLOCKS == 0:
+                    quantise(waiting, 0, C)
+                if n < turned_blocks - 2:
+                    expert_product(waiting, n % BLOCKS, 0, C, False)
             if n == turned_blocks - 2:
                 quantise(last, 0, C // 2)
+                expert_product(last, 0, 0, C // 2, False, back_bank(turned_blocks + 1))
+            if n % BLOCKS == BLOCKS - 1:
+                waiting = TURNED[n // BLOCKS]
         quantise(last, C // 2, C)
-        for e in FINISH_ORDER[:-1]:
-            for m in range(ROW_BLOCKS):
-                expert_product(e, m, 0, C, False)
-        for m in range(ROW_BLOCKS):
-            expert_product(last, m, 0, C // 2, False)
-        for m in range(2):
-            expert_product(last, m, C // 2, C, m == 0)
+        expert_product(last, 0, C // 2, C, True, back_bank(turned_blocks + 2))
+        expert_product(last, 1, 0, C, False, back_bank(turned_blocks + 3))
 
         half = T // 2
         first = [picked_flat[m][:, 0:T] for m in range(ROW_BLOCKS)]
         both = [picked_flat[m][:, T : 2 * T] for m in range(ROW_BLOCKS)]
         for m in range(ROW_BLOCKS):
             final = m + 1 == ROW_BLOCKS
-            piece = half
-            for lo in range(0, T, piece):
-                window = dx[m][:].indirect(entries(pos1_sb, lo, piece))
+            if m == 0:
+                cuts = (0, VECTOR_FIRST, T)
+            elif final:
+                cuts = (0, half, half + half // 2, T)
+            else:
+                cuts = (0, half, T)
+            for lo, hi in zip(cuts, cuts[1:]):
+                window = dx[m][:].indirect(entries(pos1_sb, lo, hi - lo))
                 if m == 0 and lo == 0:
-                    nc.vector.tensor_copy(out=first[m][:, lo : lo + piece], in_=window)
+                    nc.vector.tensor_copy(out=first[m][:, lo:hi], in_=window)
                 else:
-                    nc.scalar.activation(out=first[m][:, lo : lo + piece], in_=window, func=ACT.Copy)
+                    nc.scalar.activation(out=first[m][:, lo:hi], in_=window, func=ACT.Copy)
                 if lo == 0 and 0 < m < ROW_BLOCKS - 1:
-                    expert_product(last, m + 1, C // 2, C, False)
+                    expert_product(PLAIN, m + 1, 0, C, False)
+                    expert_product(last, m + 1, 0, C, False, bank[PRODUCT_BANKS[m - 1]])
             lo = 0
             for width in (half, half // 2, half // 2) if final else (half, half):
                 nc.vector.tensor_tensor(

@@ -33,12 +33,12 @@ RUN = 4
 BANKS = 8
 PLAIN = 3
 TURNED = (0, 1, 2)
-PLAIN_AFTER = 8
 GATE_BANK = 7
-BACK_BANKS = (5, 6, 0, 1)
-PRODUCT_BANKS = (7, 2, 3, 4)
+BACK_BANKS = (0, 1, 2, 3)
+PRODUCT_BANKS = (4, 5, 6, 7)
+SCALAR_PLANES = 2
 SCALAR_GATES = 4
-VECTOR_FIRST = 512
+VECTOR_FIRST = 384
 VECTOR_DC_PLANES = 2
 
 
@@ -62,7 +62,8 @@ def tile_moe_sdb_silu_kernel(
         dy_sc = keep.tile([P, T], U8, name="dy_sc", align_bytes=64)
         w1_codes = keep.tile([P, E, PACK * K], U8, name="w1_codes", align_bytes=64)
         w1_sc = keep.tile([P, E * K], U8, name="w1_sc", align_bytes=64)
-        a_sb = [keep.tile([P, PACK, C], F32, name="a_sb%d" % e) for e in range(E)]
+        a_flat = [keep.tile([P, PACK * C], F32, name="a_sb%d" % e) for e in range(E)]
+        a_sb = [x[:].rearrange("p (t j) -> p t j", t=PACK) for x in a_flat]
         ident = keep.tile([P, P], F32, name="ident")
         gate_rows = keep.tile([P, P], F32, name="gate_rows")
 
@@ -88,7 +89,7 @@ def tile_moe_sdb_silu_kernel(
         nc.sync.dma_start(out=a_sb[0][:, 1, :], in_=a_planes[:, 1, 0:C])
         nc.sync.dma_start(out=a_sb[0][:, 2:PACK, :], in_=a_planes[:, 2:PACK, 0:C])
         for e in range(1, E):
-            nc.sync.dma_start(out=a_sb[e][:], in_=a_planes[:, :, e * C : (e + 1) * C])
+            nc.sync.dma_start(out=a_sb[e], in_=a_planes[:, :, e * C : (e + 1) * C])
         nc.sync.dma_start(out=gate_rows[0 : SLOTS // P, :], in_=gate[0].rearrange("(r c) -> r c", c=P))
         nc.sync.dma_start(
             out=w1_codes[:].bitcast(I32), in_=w1t_words[:, 0].rearrange("e p k d -> p e (k d)").bitcast(I32)
@@ -125,7 +126,7 @@ def tile_moe_sdb_silu_kernel(
             nc.vector.tensor_tensor(
                 out=picked_flat[e][:, t * C : (t + 1) * C],
                 in0=dc[t][:].indirect(entries(offs_sb, e * C, C)),
-                in1=(a_sb if e == PLAIN else sg)[e][:, t, :],
+                in1=sg[e][:, t, :],
                 op=ALU.mult,
             )
 
@@ -155,13 +156,7 @@ def tile_moe_sdb_silu_kernel(
                 nc.scalar.activation(
                     out=sg[e][:, t : t + planes, :], in_=a_sb[e][:, t : t + planes, :], func=ACT.Sigmoid
                 )
-            for t in range(PACK):
-                if e == PLAIN:
-                    part = a_sb[e][:, t, :]
-                    nc.scalar.activation(out=part, in_=part, func=ACT.Silu, scale=-1.0)
-                    nc.vector.scalar_tensor_tensor(
-                        out=part, in0=part, scalar=1.0, in1=sg[e][:, t, :], op0=ALU.subtract, op1=ALU.mult
-                    )
+            for t in range(PACK - SCALAR_PLANES if e == PLAIN else PACK):
                 gather_plane(e, t)
 
         gate_ps = bank[GATE_BANK]
@@ -195,7 +190,7 @@ def tile_moe_sdb_silu_kernel(
         def turned_block(n):
             e, b = TURNED[n // BLOCKS], n % BLOCKS
             cols = slice(b * P, (b + 1) * P)
-            a_bank = bank[n % GATE_BANK]
+            a_bank = bank[n if n < BANKS else n - len(PRODUCT_BANKS)]
             a_turned = planes_of(a_bank)
             for t in range(PACK):
                 nc.tensor.transpose(a_turned[:, t, :], a_sb[e][:, t, cols], ident[:])
@@ -213,7 +208,9 @@ def tile_moe_sdb_silu_kernel(
                 )
             else:
                 place = n - SCALAR_GATES
-                gw = dc[PACK - 1 - place // 2][:, BANK * (place % 2) : BANK * (place % 2 + 1)]
+                places = [sg[PLAIN][:, t, :] for t in reversed(range(fused))]
+                places = places + [sg[x][:, t, :] for x in reversed(TURNED) for t in reversed(range(PACK))]
+                gw = places[place]
                 nc.gpsimd.tensor_scalar(
                     out=gw,
                     in0=u,
@@ -226,7 +223,7 @@ def tile_moe_sdb_silu_kernel(
 
         def back_block(n, gw):
             e, b = TURNED[n // BLOCKS], n % BLOCKS
-            gw_back = planes_of(back_bank(n + (n >= PLAIN_AFTER)))
+            gw_back = planes_of(back_bank(n))
             for t in range(PACK):
                 nc.tensor.transpose(gw_back[:, t, :], gw[:, t * P : (t + 1) * P], ident[:])
             round_block(e, b, in_runs(gw_back))
@@ -240,18 +237,45 @@ def tile_moe_sdb_silu_kernel(
                 op=ALU.mult,
             )
 
-        def finish_plain():
-            neg_g = back_bank(PLAIN_AFTER)
+        fused = PACK - SCALAR_PLANES
+
+        def plain_on_scalar():
+            nc.scalar.activation(out=a_flat[PLAIN][:], in_=a_flat[PLAIN][:], func=ACT.Silu, scale=-1.0)
+            for t in range(fused, PACK):
+                nc.scalar.activation(
+                    out=picked_flat[PLAIN][:, t * C : (t + 1) * C],
+                    in_=dc[t][:].indirect(entries(offs_sb, PLAIN * C, C)),
+                    func=ACT.Copy,
+                )
+
+        def plain_factor():
+            u, rest = a_sb[PLAIN], picked[PLAIN]
+            nc.vector.scalar_tensor_tensor(
+                out=rest[:, 0:fused, :], in0=u[:, 0:fused, :], scalar=1.0, in1=rest[:, 0:fused, :],
+                op0=ALU.subtract, op1=ALU.mult,
+            )
+            nc.vector.scalar_tensor_tensor(
+                out=u[:, fused:PACK, :], in0=u[:, fused:PACK, :], scalar=1.0, in1=sg[PLAIN][:, fused:PACK, :],
+                op0=ALU.subtract, op1=ALU.mult,
+            )
+
+        def plain_gathers():
+            rest = picked[PLAIN][:, fused:PACK, :]
+            nc.vector.tensor_tensor(out=rest, in0=rest, in1=a_sb[PLAIN][:, fused:PACK, :], op=ALU.mult)
+
+        def spread_gate(neg_g):
             for b in range(BLOCKS):
                 r = PLAIN * BLOCKS + b
                 nc.tensor.transpose(
                     neg_g[:, b * P : (b + 1) * P], neg_g_col[:, r : r + 1].to_broadcast([P, P]), ident[:]
                 )
-            runs = neg_g[:].rearrange("p (c i) -> p c i", i=RUN).unsqueeze(2)
+
+        def round_plain(neg_g, lo, hi):
+            runs = neg_g[:, lo:hi].rearrange("p (c i) -> p c i", i=RUN).unsqueeze(2)
             nc.vector.tensor_tensor(
-                out=da[PLAIN][:].rearrange("p (c i) t -> p c t i", i=RUN),
-                in0=in_runs(picked[PLAIN]),
-                in1=runs.to_broadcast([P, C // RUN, PACK, RUN]),
+                out=da[PLAIN][:, lo:hi, :].rearrange("p (c i) t -> p c t i", i=RUN),
+                in0=in_runs(picked[PLAIN][:, :, lo:hi]),
+                in1=runs.to_broadcast([P, (hi - lo) // RUN, PACK, RUN]),
                 op=ALU.mult,
             )
 
@@ -272,43 +296,47 @@ def tile_moe_sdb_silu_kernel(
             else:
                 nc.scalar.copy(out=dx[m][:, e * C + lo : e * C + hi], in_=dx_ps[:, lo:hi])
 
-        last = TURNED[-1]
+        last = PLAIN
         turned_blocks = len(TURNED) * BLOCKS
         gated = {}
         for n in range(turned_blocks):
             turned_block(n)
             if n < SCALAR_GATES:
                 gated[n] = gate_block(n)
-        waiting = None
+        plain_on_scalar()
         for n in range(turned_blocks):
-            if n == PLAIN_AFTER:
-                finish_plain()
-                quantise(waiting, 0, C)
-                for m in range(ROW_BLOCKS):
-                    expert_product(waiting, m, 0, C, False)
-                waiting = PLAIN
             back_block(n, gated[n] if n in gated else gate_block(n))
-            if waiting is not None:
+            if n >= BLOCKS:
                 if n % BLOCKS == 0:
-                    quantise(waiting, 0, C)
-                if n < turned_blocks - 2:
-                    expert_product(waiting, n % BLOCKS, 0, C, False)
-            if n == turned_blocks - 2:
-                quantise(last, 0, C // 2)
-                expert_product(last, 0, 0, C // 2, False, back_bank(turned_blocks + 1))
-            if n % BLOCKS == BLOCKS - 1:
-                waiting = TURNED[n // BLOCKS]
-        quantise(last, C // 2, C)
-        expert_product(last, 0, C // 2, C, True, back_bank(turned_blocks + 2))
-        expert_product(last, 1, 0, C, False, back_bank(turned_blocks + 3))
+                    quantise(TURNED[n // BLOCKS - 1], 0, C)
+                expert_product(TURNED[n // BLOCKS - 1], n % BLOCKS, 0, C, False)
+        neg_g = back_bank(turned_blocks)
+        spread_gate(neg_g)
+        plain_factor()
+        quantise(TURNED[-1], 0, C)
+        for m in range(ROW_BLOCKS):
+            expert_product(TURNED[-1], m, 0, C, False)
+        plain_gathers()
+        round_plain(neg_g, 0, C // 2)
+        round_plain(neg_g, C // 2, C - P)
+        quantise(last, 0, C // 2)
+        expert_product(last, 0, 0, C // 2, False, back_bank(turned_blocks + 1))
+        round_plain(neg_g, C - P, C)
+        quantise(last, C // 2, C - P)
+        quantise(last, C - P, C)
+        expert_product(last, 0, C // 2, C - P, False, bank[PRODUCT_BANKS[3]])
+        expert_product(last, 0, C - P, C, True, back_bank(turned_blocks + 2))
+        for m in range(1, ROW_BLOCKS):
+            expert_product(last, m, 0, C // 2, False, bank[PRODUCT_BANKS[m - 1]])
+        expert_product(last, 1, C // 2, C, False, back_bank(turned_blocks + 3))
 
         half = T // 2
-        first = [picked_flat[m][:, 0:T] for m in range(ROW_BLOCKS)]
-        both = [picked_flat[m][:, T : 2 * T] for m in range(ROW_BLOCKS)]
+        first = [a_flat[m][:, 0:T] for m in range(ROW_BLOCKS)]
+        both = [a_flat[m][:, T : 2 * T] for m in range(ROW_BLOCKS)]
         for m in range(ROW_BLOCKS):
             final = m + 1 == ROW_BLOCKS
             if m == 0:
-                cuts = (0, VECTOR_FIRST, T)
+                cuts = (0, VECTOR_FIRST, half, T)
             elif final:
                 cuts = (0, half, half + half // 2, T)
             else:
@@ -320,10 +348,9 @@ def tile_moe_sdb_silu_kernel(
                 else:
                     nc.scalar.activation(out=first[m][:, lo:hi], in_=window, func=ACT.Copy)
                 if lo == 0 and 0 < m < ROW_BLOCKS - 1:
-                    expert_product(PLAIN, m + 1, 0, C, False)
-                    expert_product(last, m + 1, 0, C, False, bank[PRODUCT_BANKS[m - 1]])
+                    expert_product(last, m + 1, C // 2, C, False, bank[PRODUCT_BANKS[m + 1]] if m == 2 else neg_g)
             lo = 0
-            for width in (half, half // 2, half // 2) if final else (half, half):
+            for width in (half, half // 2, half // 2) if final else (VECTOR_FIRST, half - VECTOR_FIRST, half) if m == 0 else (half, half):
                 nc.vector.tensor_tensor(
                     out=both[m][:, lo : lo + width],
                     in0=dx[m][:].indirect(entries(pos2_sb, lo, width)),

@@ -38,6 +38,7 @@ BACK_BANKS = (0, 1, 2, 3)
 PRODUCT_BANKS = (4, 5, 6, 7)
 SCALAR_PLANES = 2
 SCALAR_GATES = 4
+SCALAR_LAST_GATES = 1
 VECTOR_FIRST = 384
 VECTOR_DC_PLANES = 2
 
@@ -114,9 +115,9 @@ def tile_moe_sdb_silu_kernel(
 
         sg = [keep.tile([P, PACK, C], F32, name="sg%d" % e) for e in range(E)]
         dc = [keep.tile([P, T], F32, name="dc%d" % t) for t in range(PACK)]
-        picked_flat = [keep.tile([P, PACK * C], F32, name="picked%d" % e) for e in range(E)]
+        picked_flat = [keep.tile([P, PACK * C], F32, name="picked%d" % e, align_bytes=64) for e in range(E)]
         picked = [x[:].rearrange("p (t j) -> p t j", t=PACK) for x in picked_flat]
-        u_tiles = [keep.tile([P, PACK * P], F32, name="u%d" % n) for n in range(len(TURNED) * BLOCKS)]
+        u_tiles = [keep.tile([P, PACK * P], F32, name="u%d" % n, tag="u%d" % n, align_bytes=64) for n in range(len(TURNED) * BLOCKS)]
         bank = [psum.tile([P, BANK], F32, name="bank%d" % n) for n in range(BANKS)]
 
         def entries(list_sb, first, count):
@@ -166,7 +167,7 @@ def tile_moe_sdb_silu_kernel(
         nc.scalar.copy(out=g_col[:], in_=gate_ps[:, 0 : SLOTS // P])
         nc.scalar.mul(out=neg_g_col[:], in_=gate_ps[:, 0 : SLOTS // P], mul=-1.0)
 
-        da_codes = [keep.tile([P, C], U32, name="da_codes%d" % e, align_bytes=64) for e in range(E)]
+        da_codes = {e: keep.tile([P, C], U32, name="da_codes%d" % e, align_bytes=64) for e in range(2, E)}
         da_sc = [keep.tile([P, C], U8, name="da_sc%d" % e, align_bytes=64) for e in range(E)]
         da = [keep.tile([P, C, PACK], BF16, name="da%d" % e, align_bytes=64) for e in range(E)]
         dx = [keep.tile([P, SLOTS], F32, name="dx%d" % m) for m in range(ROW_BLOCKS)]
@@ -201,7 +202,7 @@ def tile_moe_sdb_silu_kernel(
             e, b = TURNED[n // BLOCKS], n % BLOCKS
             r = e * BLOCKS + b
             u = u_tiles[n][:]
-            if n < SCALAR_GATES:
+            if n < SCALAR_GATES or n >= len(TURNED) * BLOCKS - SCALAR_LAST_GATES:
                 gw = u
                 nc.scalar.activation(
                     out=gw, in_=u, func=ACT.Identity, scale=neg_g_col[:, r : r + 1], bias=g_col[:, r : r + 1]
@@ -301,21 +302,22 @@ def tile_moe_sdb_silu_kernel(
         gated = {}
         for n in range(turned_blocks):
             turned_block(n)
-            if n < SCALAR_GATES:
+            if n < SCALAR_GATES or n >= turned_blocks - SCALAR_LAST_GATES:
                 gated[n] = gate_block(n)
         plain_on_scalar()
         for n in range(turned_blocks):
             back_block(n, gated[n] if n in gated else gate_block(n))
-            if n >= BLOCKS:
-                if n % BLOCKS == 0:
-                    quantise(TURNED[n // BLOCKS - 1], 0, C)
-                expert_product(TURNED[n // BLOCKS - 1], n % BLOCKS, 0, C, False)
         neg_g = back_bank(turned_blocks)
         spread_gate(neg_g)
-        plain_factor()
-        quantise(TURNED[-1], 0, C)
-        for m in range(ROW_BLOCKS):
-            expert_product(TURNED[-1], m, 0, C, False)
+        for e in TURNED:
+            if e == TURNED[-1]:
+                plain_factor()
+            else:
+                tag = "u%d" % (turned_blocks - 1 - e)
+                da_codes[e] = keep.tile([P, C], U32, name="da_codes%d" % e, tag=tag, align_bytes=64)
+            quantise(e, 0, C)
+            for m in range(ROW_BLOCKS):
+                expert_product(e, m, 0, C, False)
         plain_gathers()
         round_plain(neg_g, 0, C // 2)
         round_plain(neg_g, C // 2, C - P)

@@ -38,7 +38,8 @@ BACK_BANKS = (0, 1, 2, 3)
 PRODUCT_BANKS = (4, 5, 6, 7)
 SCALAR_PLANES = 2
 SCALAR_GATES = 4
-SCALAR_LAST_GATES = 1
+SCALAR_LAST_GATES = 0
+FIRST_QUANTISE = 9
 VECTOR_FIRST = 384
 VECTOR_DC_PLANES = 2
 
@@ -208,10 +209,7 @@ def tile_moe_sdb_silu_kernel(
                     out=gw, in_=u, func=ACT.Identity, scale=neg_g_col[:, r : r + 1], bias=g_col[:, r : r + 1]
                 )
             else:
-                place = n - SCALAR_GATES
-                places = [sg[PLAIN][:, t, :] for t in reversed(range(fused))]
-                places = places + [sg[x][:, t, :] for x in reversed(TURNED) for t in reversed(range(PACK))]
-                gw = places[place]
+                gw = sg[PLAIN][:, fused - 1, :] if n == SCALAR_GATES else u
                 nc.gpsimd.tensor_scalar(
                     out=gw,
                     in0=u,
@@ -297,6 +295,10 @@ def tile_moe_sdb_silu_kernel(
             else:
                 nc.scalar.copy(out=dx[m][:, e * C + lo : e * C + hi], in_=dx_ps[:, lo:hi])
 
+        def late_quantise(e, n):
+            da_codes[e] = keep.tile([P, C], U32, name="da_codes%d" % e, tag="u%d" % n, align_bytes=64)
+            quantise(e, 0, C)
+
         last = PLAIN
         turned_blocks = len(TURNED) * BLOCKS
         gated = {}
@@ -307,15 +309,16 @@ def tile_moe_sdb_silu_kernel(
         plain_on_scalar()
         for n in range(turned_blocks):
             back_block(n, gated[n] if n in gated else gate_block(n))
+            if n == FIRST_QUANTISE:
+                late_quantise(TURNED[0], n)
         neg_g = back_bank(turned_blocks)
         spread_gate(neg_g)
         for e in TURNED:
             if e == TURNED[-1]:
                 plain_factor()
-            else:
-                tag = "u%d" % (turned_blocks - 1 - e)
-                da_codes[e] = keep.tile([P, C], U32, name="da_codes%d" % e, tag=tag, align_bytes=64)
-            quantise(e, 0, C)
+                quantise(e, 0, C)
+            elif e != TURNED[0]:
+                late_quantise(e, turned_blocks - 1)
             for m in range(ROW_BLOCKS):
                 expert_product(e, m, 0, C, False)
         plain_gathers()

@@ -31,8 +31,8 @@ SCALE_ROWS = 16
 RUN = 4
 
 BANKS = 8
-PLAIN = 3
-TURNED = (0, 1, 2)
+PLAIN = 1
+TURNED = (2, 3, 0)
 GATE_BANK = 7
 BACK_BANKS = (0, 1, 2, 3)
 PRODUCT_BANKS = (4, 5, 6, 7)
@@ -64,8 +64,9 @@ def tile_moe_sdb_silu_kernel(
         dy_sc = keep.tile([P, T], U8, name="dy_sc", align_bytes=64)
         w1_codes = keep.tile([P, E, PACK * K], U8, name="w1_codes", align_bytes=64)
         w1_sc = keep.tile([P, E * K], U8, name="w1_sc", align_bytes=64)
-        a_flat = [keep.tile([P, PACK * C], F32, name="a_sb%d" % e) for e in range(E)]
-        a_sb = [x[:].rearrange("p (t j) -> p t j", t=PACK) for x in a_flat]
+        a_flat = [keep.tile([P, PACK * 2 * C], F32, name="a_pair%d" % x) for x in range(E // 2)]
+        a_pair = [x[:].rearrange("p (t j) -> p t j", t=PACK) for x in a_flat]
+        a_sb = [a_pair[e // 2][:, :, (e % 2) * C : (e % 2 + 1) * C] for e in range(E)]
         ident = keep.tile([P, P], F32, name="ident")
         gate_rows = keep.tile([P, P], F32, name="gate_rows")
 
@@ -86,12 +87,14 @@ def tile_moe_sdb_silu_kernel(
         load_scale_rows(dy_sc[:].bitcast(I32), dy_sc_rows, 0, GROUP // 2)
         nc.sync.dma_start(out=dy_codes[:].bitcast(I32), in_=dy_words[0].rearrange("p n d -> p (n d)").bitcast(I32))
         load_scale_rows(dy_sc[:].bitcast(I32), dy_sc_rows, GROUP // 2, GROUP)
-        nc.sync.dma_start(out=a_sb[0][:, 0, :], in_=a_planes[:, 0, 0:C])
-        nc.sync.dma_start(offs_sb[:], offs)
-        nc.sync.dma_start(out=a_sb[0][:, 1, :], in_=a_planes[:, 1, 0:C])
-        nc.sync.dma_start(out=a_sb[0][:, 2:PACK, :], in_=a_planes[:, 2:PACK, 0:C])
-        for e in range(1, E):
-            nc.sync.dma_start(out=a_sb[e], in_=a_planes[:, :, e * C : (e + 1) * C])
+        for x in range(E // 2):
+            for t in range(PACK):
+                if x == 0 and t == 0:
+                    nc.sync.dma_start(out=a_sb[0][:, 0, :], in_=a_planes[:, 0, 0:C])
+                    nc.sync.dma_start(offs_sb[:], offs)
+                    nc.sync.dma_start(out=a_sb[1][:, 0, :], in_=a_planes[:, 0, C : 2 * C])
+                else:
+                    nc.sync.dma_start(out=a_pair[x][:, t, :], in_=a_planes[:, t, 2 * C * x : 2 * C * (x + 1)])
         nc.sync.dma_start(out=gate_rows[0 : SLOTS // P, :], in_=gate[0].rearrange("(r c) -> r c", c=P))
         nc.sync.dma_start(
             out=w1_codes[:].bitcast(I32), in_=w1t_words[:, 0].rearrange("e p k d -> p e (k d)").bitcast(I32)
@@ -114,7 +117,8 @@ def tile_moe_sdb_silu_kernel(
             in_=w2_sc_raw[:].rearrange("p (m t) -> p t m", t=PACK),
         )
 
-        sg = [keep.tile([P, PACK, C], F32, name="sg%d" % e) for e in range(E)]
+        sg_pair = [keep.tile([P, PACK, 2 * C], F32, name="sg_pair%d" % x) for x in range(E // 2)]
+        sg = [sg_pair[e // 2][:, :, (e % 2) * C : (e % 2 + 1) * C] for e in range(E)]
         dc = [keep.tile([P, T], F32, name="dc%d" % t) for t in range(PACK)]
         picked_flat = [keep.tile([P, PACK * C], F32, name="picked%d" % e, align_bytes=64) for e in range(E)]
         picked = [x[:].rearrange("p (t j) -> p t j", t=PACK) for x in picked_flat]
@@ -133,7 +137,11 @@ def tile_moe_sdb_silu_kernel(
             )
 
         for t in range(PACK):
-            nc.scalar.activation(out=sg[0][:, t, :], in_=a_sb[0][:, t, :], func=ACT.Sigmoid)
+            if t == 0:
+                for e in range(2):
+                    nc.scalar.activation(out=sg[e][:, t, :], in_=a_sb[e][:, t, :], func=ACT.Sigmoid)
+            else:
+                nc.scalar.activation(out=sg_pair[0][:, t, :], in_=a_pair[0][:, t, :], func=ACT.Sigmoid)
             for h in range(T // BANK):
                 tokens = slice(BANK * h, BANK * (h + 1))
                 dc_ps = bank[2 * t + h]
@@ -151,15 +159,13 @@ def tile_moe_sdb_silu_kernel(
                 else:
                     nc.scalar.copy(out=dc[t][:, tokens], in_=dc_ps[:])
             gather_plane(0, t)
+            if t < PACK - SCALAR_PLANES:
+                gather_plane(PLAIN, t)
 
-        for e in range(1, E):
-            planes = PACK // 2 if e == 1 else PACK
-            for t in range(0, PACK, planes):
-                nc.scalar.activation(
-                    out=sg[e][:, t : t + planes, :], in_=a_sb[e][:, t : t + planes, :], func=ACT.Sigmoid
-                )
-            for t in range(PACK - SCALAR_PLANES if e == PLAIN else PACK):
-                gather_plane(e, t)
+        for t in range(PACK):
+            nc.scalar.activation(out=sg_pair[1][:, t, :], in_=a_pair[1][:, t, :], func=ACT.Sigmoid)
+            gather_plane(2, t)
+            gather_plane(3, t)
 
         gate_ps = bank[GATE_BANK]
         nc.tensor.transpose(gate_ps[:, 0:P], gate_rows[:], ident[:])
@@ -168,7 +174,7 @@ def tile_moe_sdb_silu_kernel(
         nc.scalar.copy(out=g_col[:], in_=gate_ps[:, 0 : SLOTS // P])
         nc.scalar.mul(out=neg_g_col[:], in_=gate_ps[:, 0 : SLOTS // P], mul=-1.0)
 
-        da_codes = {e: keep.tile([P, C], U32, name="da_codes%d" % e, align_bytes=64) for e in range(2, E)}
+        da_codes = {e: keep.tile([P, C], U32, name="da_codes%d" % e, align_bytes=64) for e in (TURNED[-1], PLAIN)}
         da_sc = [keep.tile([P, C], U8, name="da_sc%d" % e, align_bytes=64) for e in range(E)]
         da = [keep.tile([P, C, PACK], BF16, name="da%d" % e, align_bytes=64) for e in range(E)]
         dx = [keep.tile([P, SLOTS], F32, name="dx%d" % m) for m in range(ROW_BLOCKS)]
@@ -209,7 +215,7 @@ def tile_moe_sdb_silu_kernel(
                     out=gw, in_=u, func=ACT.Identity, scale=neg_g_col[:, r : r + 1], bias=g_col[:, r : r + 1]
                 )
             else:
-                gw = sg[PLAIN][:, fused - 1, :] if n == SCALAR_GATES else u
+                gw = sg[E - 1][:, PACK - 1, :] if n == SCALAR_GATES else u
                 nc.gpsimd.tensor_scalar(
                     out=gw,
                     in0=u,
@@ -239,7 +245,7 @@ def tile_moe_sdb_silu_kernel(
         fused = PACK - SCALAR_PLANES
 
         def plain_on_scalar():
-            nc.scalar.activation(out=a_flat[PLAIN][:], in_=a_flat[PLAIN][:], func=ACT.Silu, scale=-1.0)
+            nc.scalar.activation(out=a_sb[PLAIN], in_=a_sb[PLAIN], func=ACT.Silu, scale=-1.0)
             for t in range(fused, PACK):
                 nc.scalar.activation(
                     out=picked_flat[PLAIN][:, t * C : (t + 1) * C],
@@ -304,8 +310,10 @@ def tile_moe_sdb_silu_kernel(
         gated = {}
         for n in range(turned_blocks):
             turned_block(n)
-            if n < SCALAR_GATES or n >= turned_blocks - SCALAR_LAST_GATES:
+            if n < SCALAR_GATES - 1:
                 gated[n] = gate_block(n)
+            if n == SCALAR_GATES:
+                gated[n - 1] = gate_block(n - 1)
         plain_on_scalar()
         for n in range(turned_blocks):
             back_block(n, gated[n] if n in gated else gate_block(n))
@@ -336,8 +344,8 @@ def tile_moe_sdb_silu_kernel(
         expert_product(last, 1, C // 2, C, False, back_bank(turned_blocks + 3))
 
         half = T // 2
-        first = [a_flat[m][:, 0:T] for m in range(ROW_BLOCKS)]
-        both = [a_flat[m][:, T : 2 * T] for m in range(ROW_BLOCKS)]
+        first = [a_pair[0][:, m, :] for m in range(ROW_BLOCKS)]
+        both = [a_pair[1][:, m, :] for m in range(ROW_BLOCKS)]
         for m in range(ROW_BLOCKS):
             final = m + 1 == ROW_BLOCKS
             if m == 0:

@@ -31,17 +31,21 @@ SCALE_ROWS = 16
 RUN = 4
 
 BANKS = 8
-PLAIN = 1
-TURNED = (2, 3, 0)
+EARLY = 256
+LATE = 2
+TURNED = (
+    [(e, b) for e in (3, 1) for b in range(BLOCKS)]
+    + [(0, b) for b in range(EARLY // P, BLOCKS)]
+    + [(LATE, b) for b in range(BLOCKS)]
+)
+SILU_BANKS = (0, 1, 2, 3, 4, 5, 6, 7, 0, 1, 5, 7, 3, 0)
 GATE_BANK = 7
-BACK_BANKS = (0, 1, 2, 3)
-PRODUCT_BANKS = (4, 5, 6, 7)
-SCALAR_PLANES = 2
-SCALAR_GATES = 4
-SCALAR_LAST_GATES = 0
-FIRST_QUANTISE = 9
-VECTOR_FIRST = 384
-VECTOR_DC_PLANES = 2
+SPREAD_BANK = 2
+BACK_BANKS = (3, 4, 6, 2, 4, 6, 2, 1, 5, 4, 2, 1, 5, 4)
+PRODUCT_BANKS = (7, 3, 0, 6)
+SCALAR_GATES = (0, 1, 7, 8, 12)
+PACE_BLOCK = 1
+VECTOR_FIRST = 512
 
 
 def tile_moe_sdb_silu_kernel(
@@ -64,9 +68,8 @@ def tile_moe_sdb_silu_kernel(
         dy_sc = keep.tile([P, T], U8, name="dy_sc", align_bytes=64)
         w1_codes = keep.tile([P, E, PACK * K], U8, name="w1_codes", align_bytes=64)
         w1_sc = keep.tile([P, E * K], U8, name="w1_sc", align_bytes=64)
-        a_flat = [keep.tile([P, PACK * 2 * C], F32, name="a_pair%d" % x) for x in range(E // 2)]
-        a_pair = [x[:].rearrange("p (t j) -> p t j", t=PACK) for x in a_flat]
-        a_sb = [a_pair[e // 2][:, :, (e % 2) * C : (e % 2 + 1) * C] for e in range(E)]
+        a_sb = keep.tile([P, PACK, SLOTS], F32, name="a_sb")
+        sg = keep.tile([P, PACK, SLOTS], F32, name="sg")
         ident = keep.tile([P, P], F32, name="ident")
         gate_rows = keep.tile([P, P], F32, name="gate_rows")
 
@@ -76,25 +79,30 @@ def tile_moe_sdb_silu_kernel(
         nc.gpsimd.memset(gate_rows[:], 0.0)
         make_identity(nc, ident[:])
 
-        def load_scale_rows(plane, rows, first, last):
-            for r in range(first, last):
+        def load_scale_rows(plane, rows):
+            for r in range(GROUP):
                 nc.sync.dma_start(out=plane[r:P:QUADRANT], in_=rows[r:SCALE_ROWS:GROUP])
 
         a_planes = a.rearrange("(p t) j -> p t j", t=PACK)
-        dy_sc_rows = dy_scales[0].bitcast(I32)
+        nc.sync.dma_start(out=a_sb[:, 0:2, 0:EARLY], in_=a_planes[:, 0:2, 0:EARLY])
         nc.sync.dma_start(out=w2_raw[:].bitcast(I32), in_=w2t_words[0].bitcast(I32))
-        load_scale_rows(w2_sc_raw[:].bitcast(I32), w2t_scales[0].bitcast(I32), 0, GROUP)
-        load_scale_rows(dy_sc[:].bitcast(I32), dy_sc_rows, 0, GROUP // 2)
+        load_scale_rows(w2_sc_raw[:].bitcast(I32), w2t_scales[0].bitcast(I32))
+        nc.sync.dma_start(out=a_sb[:, 2:4, 0:EARLY], in_=a_planes[:, 2:4, 0:EARLY])
         nc.sync.dma_start(out=dy_codes[:].bitcast(I32), in_=dy_words[0].rearrange("p n d -> p (n d)").bitcast(I32))
-        load_scale_rows(dy_sc[:].bitcast(I32), dy_sc_rows, GROUP // 2, GROUP)
-        for x in range(E // 2):
-            for t in range(PACK):
-                if x == 0 and t == 0:
-                    nc.sync.dma_start(out=a_sb[0][:, 0, :], in_=a_planes[:, 0, 0:C])
+        load_scale_rows(dy_sc[:].bitcast(I32), dy_scales[0].bitcast(I32))
+
+        def pieces(t):
+            cuts = (EARLY, 2 * C, 3 * C) if t < 2 else (EARLY, 2 * C)
+            return list(zip(cuts, cuts[1:]))
+
+        for t in range(PACK):
+            for lo, hi in pieces(t) if t != 1 else [(EARLY, 3 * C)]:
+                nc.sync.dma_start(out=a_sb[:, t, lo:hi], in_=a_planes[:, t, lo:hi])
+                if t == 0 and lo == EARLY:
                     nc.sync.dma_start(offs_sb[:], offs)
-                    nc.sync.dma_start(out=a_sb[1][:, 0, :], in_=a_planes[:, 0, C : 2 * C])
-                else:
-                    nc.sync.dma_start(out=a_pair[x][:, t, :], in_=a_planes[:, t, 2 * C * x : 2 * C * (x + 1)])
+        nc.sync.dma_start(out=a_sb[:, 2:4, 2 * C : 3 * C], in_=a_planes[:, 2:4, 2 * C : 3 * C])
+        for t in range(0, PACK, 2):
+            nc.sync.dma_start(out=a_sb[:, t : t + 2, 3 * C : SLOTS], in_=a_planes[:, t : t + 2, 3 * C : SLOTS])
         nc.sync.dma_start(out=gate_rows[0 : SLOTS // P, :], in_=gate[0].rearrange("(r c) -> r c", c=P))
         nc.sync.dma_start(
             out=w1_codes[:].bitcast(I32), in_=w1t_words[:, 0].rearrange("e p k d -> p e (k d)").bitcast(I32)
@@ -102,8 +110,6 @@ def tile_moe_sdb_silu_kernel(
         load_scale_rows(
             w1_sc[:].bitcast(I32).rearrange("p (e k) -> p e k", e=E),
             w1t_scales[:, 0].bitcast(I32).rearrange("e b k -> b e k"),
-            0,
-            GROUP,
         )
         nc.sync.dma_start(pos1_sb[:], pos1)
         nc.sync.dma_start(pos2_sb[:], pos2)
@@ -117,54 +123,73 @@ def tile_moe_sdb_silu_kernel(
             in_=w2_sc_raw[:].rearrange("p (m t) -> p t m", t=PACK),
         )
 
-        sg_pair = [keep.tile([P, PACK, 2 * C], F32, name="sg_pair%d" % x) for x in range(E // 2)]
-        sg = [sg_pair[e // 2][:, :, (e % 2) * C : (e % 2 + 1) * C] for e in range(E)]
-        dc = [keep.tile([P, T], F32, name="dc%d" % t) for t in range(PACK)]
-        picked_flat = [keep.tile([P, PACK * C], F32, name="picked%d" % e, align_bytes=64) for e in range(E)]
+        dc = [keep.tile([P, T], F32, name="dc%d" % t, tag="dc%d" % t, align_bytes=64) for t in range(PACK)]
+        picked_flat = [keep.tile([P, PACK * C], F32, name="picked%d" % e) for e in range(E)]
         picked = [x[:].rearrange("p (t j) -> p t j", t=PACK) for x in picked_flat]
-        u_tiles = [keep.tile([P, PACK * P], F32, name="u%d" % n, tag="u%d" % n, align_bytes=64) for n in range(len(TURNED) * BLOCKS)]
+        late_dc = keep.tile([P, 2, C], F32, name="late_dc")
+        places = {
+            PACE_BLOCK: picked[3][:, 1, :],
+            7: late_dc[:, 0, :],
+            8: late_dc[:, 1, :],
+            9: picked[LATE][:, 3, :],
+            10: picked[LATE][:, 2, :],
+        }
+        own = [keep.tile([P, PACK * P], F32, name="u%d" % n)[:] for n in range(len(TURNED)) if n not in (9, 10)]
+        own = own[:9] + [None, None] + own[9:]
+        u_at = [places.get(n, own[n]) for n in range(len(TURNED))]
         bank = [psum.tile([P, BANK], F32, name="bank%d" % n) for n in range(BANKS)]
 
         def entries(list_sb, first, count):
             return list_sb[:, first // PER_COLUMN : (first + count) // PER_COLUMN]
 
-        def gather_plane(e, t):
+        for x in range(2):
+            a_x, s_x = a_sb[:, 2 * x : 2 * x + 2, 0:EARLY], sg[:, 2 * x : 2 * x + 2, 0:EARLY]
+            nc.scalar.activation(out=s_x, in_=a_x, func=ACT.Sigmoid)
+            nc.vector.scalar_tensor_tensor(out=a_x, in0=s_x, scalar=1.0, in1=a_x, op0=ALU.subtract, op1=ALU.mult)
+            nc.vector.scalar_tensor_tensor(out=s_x, in0=a_x, scalar=1.0, in1=s_x, op0=ALU.subtract, op1=ALU.mult)
+
+        def gather_plane(e, t, lo=0, hi=C):
             nc.vector.tensor_tensor(
-                out=picked_flat[e][:, t * C : (t + 1) * C],
-                in0=dc[t][:].indirect(entries(offs_sb, e * C, C)),
-                in1=sg[e][:, t, :],
+                out=picked_flat[e][:, t * C + lo : t * C + hi],
+                in0=dc[t][:].indirect(entries(offs_sb, e * C + lo, hi - lo)),
+                in1=sg[:, t, e * C + lo : e * C + hi],
                 op=ALU.mult,
             )
 
         for t in range(PACK):
+            for x, (lo, hi) in enumerate(pieces(t)):
+                if x == 0:
+                    for h in range(T // BANK):
+                        tokens = slice(BANK * h, BANK * (h + 1))
+                        dc_ps = bank[2 * t + h]
+                        nc.tensor.matmul_mx(
+                            out=dc_ps[:],
+                            lhsT=w2_codes[:, 2 * P * t : 2 * P * (t + 1)].bitcast(E2M1),
+                            lhsT_scale=w2_sc[:, P * t : P * (t + 1)],
+                            rhs=dy_codes[:, PACK * BANK * h : PACK * BANK * (h + 1)].bitcast(E5M2),
+                            rhs_scale=dy_sc[:, tokens],
+                            start=True,
+                            stop=True,
+                        )
+                        if (t, h) == (0, 1):
+                            nc.vector.tensor_copy(out=dc[t][:, tokens], in_=dc_ps[:])
+                        else:
+                            nc.scalar.copy(out=dc[t][:, tokens], in_=dc_ps[:])
+                nc.scalar.activation(out=sg[:, t, lo:hi], in_=a_sb[:, t, lo:hi], func=ACT.Sigmoid)
             if t == 0:
-                for e in range(2):
-                    nc.scalar.activation(out=sg[e][:, t, :], in_=a_sb[e][:, t, :], func=ACT.Sigmoid)
+                gather_plane(0, t, 0, EARLY)
+                gather_plane(0, t, EARLY, C)
             else:
-                nc.scalar.activation(out=sg_pair[0][:, t, :], in_=a_pair[0][:, t, :], func=ACT.Sigmoid)
-            for h in range(T // BANK):
-                tokens = slice(BANK * h, BANK * (h + 1))
-                dc_ps = bank[2 * t + h]
-                nc.tensor.matmul_mx(
-                    out=dc_ps[:],
-                    lhsT=w2_codes[:, 2 * P * t : 2 * P * (t + 1)].bitcast(E2M1),
-                    lhsT_scale=w2_sc[:, P * t : P * (t + 1)],
-                    rhs=dy_codes[:, PACK * BANK * h : PACK * BANK * (h + 1)].bitcast(E5M2),
-                    rhs_scale=dy_sc[:, tokens],
-                    start=True,
-                    stop=True,
-                )
-                if t < VECTOR_DC_PLANES and h == 0:
-                    nc.vector.tensor_copy(out=dc[t][:, tokens], in_=dc_ps[:])
-                else:
-                    nc.scalar.copy(out=dc[t][:, tokens], in_=dc_ps[:])
-            gather_plane(0, t)
-            if t < PACK - SCALAR_PLANES:
-                gather_plane(PLAIN, t)
-
-        for t in range(PACK):
-            nc.scalar.activation(out=sg_pair[1][:, t, :], in_=a_pair[1][:, t, :], func=ACT.Sigmoid)
-            gather_plane(2, t)
+                gather_plane(0, t)
+            gather_plane(1, t)
+            if t < 2:
+                gather_plane(2, t)
+        nc.scalar.activation(out=sg[:, 2:4, 2 * C : 3 * C], in_=a_sb[:, 2:4, 2 * C : 3 * C], func=ACT.Sigmoid)
+        for t in range(0, PACK, 2):
+            nc.scalar.activation(
+                out=sg[:, t : t + 2, 3 * C : SLOTS], in_=a_sb[:, t : t + 2, 3 * C : SLOTS], func=ACT.Sigmoid
+            )
+        for t in (0, 2, 3):
             gather_plane(3, t)
 
         gate_ps = bank[GATE_BANK]
@@ -174,9 +199,9 @@ def tile_moe_sdb_silu_kernel(
         nc.scalar.copy(out=g_col[:], in_=gate_ps[:, 0 : SLOTS // P])
         nc.scalar.mul(out=neg_g_col[:], in_=gate_ps[:, 0 : SLOTS // P], mul=-1.0)
 
-        da_codes = {e: keep.tile([P, C], U32, name="da_codes%d" % e, align_bytes=64) for e in (TURNED[-1], PLAIN)}
+        da_codes = [keep.tile([P, C], U32, name="da_codes%d" % e, align_bytes=64) for e in range(E)]
         da_sc = [keep.tile([P, C], U8, name="da_sc%d" % e, align_bytes=64) for e in range(E)]
-        da = [keep.tile([P, C, PACK], BF16, name="da%d" % e, align_bytes=64) for e in range(E)]
+        da = {e: keep.tile([P, C, PACK], BF16, name="da%d" % e, tag="da%d" % e, align_bytes=64) for e in range(1, E)}
         dx = [keep.tile([P, SLOTS], F32, name="dx%d" % m) for m in range(ROW_BLOCKS)]
 
         def in_runs(planes_ap):
@@ -185,9 +210,6 @@ def tile_moe_sdb_silu_kernel(
         def planes_of(bank_tile):
             return bank_tile[:].rearrange("p (t s) -> p t s", t=PACK)
 
-        def back_bank(turn):
-            return bank[BACK_BANKS[turn % len(BACK_BANKS)]]
-
         def quantise(e, lo, hi):
             nc.vector.quantize_mx(
                 out=da_codes[e][:, lo:hi].bitcast(E5M2),
@@ -195,100 +217,55 @@ def tile_moe_sdb_silu_kernel(
                 in_=da[e][:, lo:hi, :].rearrange("p j t -> p (j t)"),
             )
 
-        def turned_block(n):
-            e, b = TURNED[n // BLOCKS], n % BLOCKS
-            cols = slice(b * P, (b + 1) * P)
-            a_bank = bank[n if n < BANKS else n - len(PRODUCT_BANKS)]
+        gated = {}
+
+        def turn_block(n, a_bank):
+            e, b = TURNED[n]
+            r = e * BLOCKS + b
             a_turned = planes_of(a_bank)
             for t in range(PACK):
-                nc.tensor.transpose(a_turned[:, t, :], a_sb[e][:, t, cols], ident[:])
-            u = u_tiles[n][:]
+                nc.tensor.transpose(a_turned[:, t, :], a_sb[:, t, r * P : (r + 1) * P], ident[:])
+            u = u_at[n]
             nc.scalar.activation(out=u, in_=a_bank[:], func=ACT.Silu, scale=-1.0)
+            if n in SCALAR_GATES:
+                gated[n] = own[n]
+                nc.scalar.activation(
+                    out=gated[n], in_=u, func=ACT.Identity, scale=neg_g_col[:, r : r + 1], bias=g_col[:, r : r + 1]
+                )
 
-        def gate_block(n):
-            e, b = TURNED[n // BLOCKS], n % BLOCKS
+        def gate_block(n, gw):
+            e, b = TURNED[n]
             r = e * BLOCKS + b
-            u = u_tiles[n][:]
-            if n < SCALAR_GATES or n >= len(TURNED) * BLOCKS - SCALAR_LAST_GATES:
-                gw = u
-                nc.scalar.activation(
-                    out=gw, in_=u, func=ACT.Identity, scale=neg_g_col[:, r : r + 1], bias=g_col[:, r : r + 1]
-                )
-            else:
-                gw = sg[E - 1][:, PACK - 1, :] if n == SCALAR_GATES else u
-                nc.gpsimd.tensor_scalar(
-                    out=gw,
-                    in0=u,
-                    scalar1=neg_g_col[:, r : r + 1],
-                    scalar2=g_col[:, r : r + 1],
-                    op0=ALU.mult,
-                    op1=ALU.add,
-                )
-            return gw
+            nc.gpsimd.tensor_scalar(
+                out=gw,
+                in0=u_at[n],
+                scalar1=neg_g_col[:, r : r + 1],
+                scalar2=g_col[:, r : r + 1],
+                op0=ALU.mult,
+                op1=ALU.add,
+            )
+            gated[n] = gw
 
-        def back_block(n, gw):
-            e, b = TURNED[n // BLOCKS], n % BLOCKS
-            gw_back = planes_of(back_bank(n))
+        def rounded(e, lo, hi):
+            return da[e][:, lo:hi, :].rearrange("p (c i) t -> p c t i", i=RUN)
+
+        def turn_back(n):
+            gw_back = planes_of(bank[BACK_BANKS[n]])
             for t in range(PACK):
-                nc.tensor.transpose(gw_back[:, t, :], gw[:, t * P : (t + 1) * P], ident[:])
-            round_block(e, b, in_runs(gw_back))
+                nc.tensor.transpose(gw_back[:, t, :], gated[n][:, t * P : (t + 1) * P], ident[:])
 
-        def round_block(e, b, factor_in_runs):
-            cols = slice(b * P, (b + 1) * P)
+        def round_block(n):
+            e, b = TURNED[n]
             nc.vector.tensor_tensor(
-                out=da[e][:, cols, :].rearrange("p (c i) t -> p c t i", i=RUN),
-                in0=in_runs(picked[e][:, :, cols]),
-                in1=factor_in_runs,
+                out=rounded(e, b * P, (b + 1) * P),
+                in0=in_runs(picked[e][:, :, b * P : (b + 1) * P]),
+                in1=in_runs(planes_of(bank[BACK_BANKS[n]])),
                 op=ALU.mult,
             )
 
-        fused = PACK - SCALAR_PLANES
-
-        def plain_on_scalar():
-            nc.scalar.activation(out=a_sb[PLAIN], in_=a_sb[PLAIN], func=ACT.Silu, scale=-1.0)
-            for t in range(fused, PACK):
-                nc.scalar.activation(
-                    out=picked_flat[PLAIN][:, t * C : (t + 1) * C],
-                    in_=dc[t][:].indirect(entries(offs_sb, PLAIN * C, C)),
-                    func=ACT.Copy,
-                )
-
-        def plain_factor():
-            u, rest = a_sb[PLAIN], picked[PLAIN]
-            nc.vector.scalar_tensor_tensor(
-                out=rest[:, 0:fused, :], in0=u[:, 0:fused, :], scalar=1.0, in1=rest[:, 0:fused, :],
-                op0=ALU.subtract, op1=ALU.mult,
-            )
-            nc.vector.scalar_tensor_tensor(
-                out=u[:, fused:PACK, :], in0=u[:, fused:PACK, :], scalar=1.0, in1=sg[PLAIN][:, fused:PACK, :],
-                op0=ALU.subtract, op1=ALU.mult,
-            )
-
-        def plain_gathers():
-            rest = picked[PLAIN][:, fused:PACK, :]
-            nc.vector.tensor_tensor(out=rest, in0=rest, in1=a_sb[PLAIN][:, fused:PACK, :], op=ALU.mult)
-
-        def spread_gate(neg_g):
-            for b in range(BLOCKS):
-                r = PLAIN * BLOCKS + b
-                nc.tensor.transpose(
-                    neg_g[:, b * P : (b + 1) * P], neg_g_col[:, r : r + 1].to_broadcast([P, P]), ident[:]
-                )
-
-        def round_plain(neg_g, lo, hi):
-            runs = neg_g[:, lo:hi].rearrange("p (c i) -> p c i", i=RUN).unsqueeze(2)
-            nc.vector.tensor_tensor(
-                out=da[PLAIN][:, lo:hi, :].rearrange("p (c i) t -> p c t i", i=RUN),
-                in0=in_runs(picked[PLAIN][:, :, lo:hi]),
-                in1=runs.to_broadcast([P, (hi - lo) // RUN, PACK, RUN]),
-                op=ALU.mult,
-            )
-
-        def expert_product(e, m, lo, hi, on_vector, dx_ps=None):
-            if dx_ps is None:
-                dx_ps = bank[PRODUCT_BANKS[m]]
+        def product(e, m, lo, hi, dx_ps):
             nc.tensor.matmul_mx(
-                out=dx_ps[:, lo:hi],
+                out=dx_ps,
                 lhsT=w1_codes[:, e, PACK * P * m : PACK * P * (m + 1)].bitcast(E4M3),
                 lhsT_scale=w1_sc[:, e * K + P * m : e * K + P * (m + 1)],
                 rhs=da_codes[e][:, lo:hi].bitcast(E5M2),
@@ -296,60 +273,97 @@ def tile_moe_sdb_silu_kernel(
                 start=True,
                 stop=True,
             )
-            if on_vector:
-                nc.vector.tensor_copy(out=dx[m][:, e * C + lo : e * C + hi], in_=dx_ps[:, lo:hi])
-            else:
-                nc.scalar.copy(out=dx[m][:, e * C + lo : e * C + hi], in_=dx_ps[:, lo:hi])
 
-        def late_quantise(e, n):
-            da_codes[e] = keep.tile([P, C], U32, name="da_codes%d" % e, tag="u%d" % n, align_bytes=64)
-            quantise(e, 0, C)
+        def copy_out(engine_copy, e, m, lo, hi, dx_ps):
+            engine_copy(out=dx[m][:, e * C + lo : e * C + hi], in_=dx_ps)
 
-        last = PLAIN
-        turned_blocks = len(TURNED) * BLOCKS
-        gated = {}
-        for n in range(turned_blocks):
-            turned_block(n)
-            if n < SCALAR_GATES - 1:
-                gated[n] = gate_block(n)
-            if n == SCALAR_GATES:
-                gated[n - 1] = gate_block(n - 1)
-        plain_on_scalar()
-        for n in range(turned_blocks):
-            back_block(n, gated[n] if n in gated else gate_block(n))
-            if n == FIRST_QUANTISE:
-                late_quantise(TURNED[0], n)
-        neg_g = back_bank(turned_blocks)
-        spread_gate(neg_g)
-        for e in TURNED:
-            if e == TURNED[-1]:
-                plain_factor()
-                quantise(e, 0, C)
-            elif e != TURNED[0]:
-                late_quantise(e, turned_blocks - 1)
+        neg_g = bank[SPREAD_BANK]
+        for n in range(12):
+            turn_block(n, bank[SILU_BANKS[n]])
+            if n == PACE_BLOCK:
+                gather_plane(E - 1, 1)
+            if n == SPREAD_BANK:
+                for b in range(EARLY // P):
+                    nc.tensor.transpose(
+                        neg_g[:, b * P : (b + 1) * P], neg_g_col[:, b : b + 1].to_broadcast([P, P]), ident[:]
+                    )
+
+        da[0] = keep.tile([P, C, PACK], BF16, name="da0", tag="dc1", align_bytes=64)
+        runs = neg_g[:, 0:EARLY].rearrange("p (c i) -> p c i", i=RUN).unsqueeze(2)
+        nc.vector.tensor_tensor(
+            out=rounded(0, 0, EARLY),
+            in0=in_runs(picked[0][:, :, 0:EARLY]),
+            in1=runs.to_broadcast([P, EARLY // RUN, PACK, RUN]),
+            op=ALU.mult,
+        )
+
+        def whole(e, m, bank_index):
+            product(e, m, 0, C, bank[PRODUCT_BANKS[bank_index]][:])
+            copy_out(nc.scalar.copy, e, m, 0, C, bank[PRODUCT_BANKS[bank_index]][:])
+
+        def first_products():
             for m in range(ROW_BLOCKS):
-                expert_product(e, m, 0, C, False)
-        plain_gathers()
-        round_plain(neg_g, 0, C // 2)
-        round_plain(neg_g, C // 2, C - P)
-        quantise(last, 0, C // 2)
-        expert_product(last, 0, 0, C // 2, False, back_bank(turned_blocks + 1))
-        round_plain(neg_g, C - P, C)
-        quantise(last, C // 2, C - P)
-        quantise(last, C - P, C)
-        expert_product(last, 0, C // 2, C - P, False, bank[PRODUCT_BANKS[3]])
-        expert_product(last, 0, C - P, C, True, back_bank(turned_blocks + 2))
+                whole(3, m, m)
+
+        def second_products():
+            for m in range(ROW_BLOCKS):
+                whole(1, m, 2 * m % ROW_BLOCKS)
+                whole(0, m, (2 * m + 1) % ROW_BLOCKS)
+
+        due = {9: first_products, 13: second_products}
+        for n in range(len(TURNED)):
+            e, b = TURNED[n]
+            if n not in gated:
+                if n == 2:
+                    gw = sg[:, 1, (E - 1) * C : E * C]
+                elif n == 9:
+                    gw = keep.tile([P, PACK * P], F32, name="held", tag="da3", align_bytes=64)[:]
+                elif n == 13:
+                    gw = late_dc[:, 0, :]
+                else:
+                    gw = u_at[n - 1]
+                gate_block(n, gw)
+            turn_back(n)
+            if n in due:
+                due[n]()
+            if n < 10 or n > 11:
+                round_block(n)
+            if n == 0:
+                turn_block(12, bank[SILU_BANKS[12]])
+                turn_block(13, bank[SILU_BANKS[13]])
+                for t in (2, 3):
+                    nc.scalar.activation(
+                        out=late_dc[:, t - 2, :], in_=dc[t][:].indirect(entries(offs_sb, LATE * C, C)), func=ACT.Copy
+                    )
+            if n == 3:
+                quantise(3, 0, C)
+            if n == 9:
+                quantise(1, 0, C)
+                quantise(0, 0, C)
+            if n == 11:
+                nc.vector.tensor_tensor(
+                    out=picked[LATE][:, 2:4, :], in0=late_dc[:], in1=sg[:, 2:4, LATE * C : (LATE + 1) * C], op=ALU.mult
+                )
+                round_block(10)
+                round_block(11)
+            if n == 12:
+                quantise(LATE, 0, C // 2)
+                product(LATE, 0, 0, C // 2, bank[2][:, 0 : C // 2])
+        quantise(LATE, C // 2, C)
+        product(LATE, 0, C // 2, C, bank[1][:, 0 : C // 2])
+        copy_out(nc.vector.tensor_copy, LATE, 0, 0, C // 2, bank[2][:, 0 : C // 2])
+        copy_out(nc.vector.tensor_copy, LATE, 0, C // 2, C, bank[1][:, 0 : C // 2])
+        last_places = {1: bank[5][:], 2: bank[4][:], 3: bank[PRODUCT_BANKS[0]][:]}
         for m in range(1, ROW_BLOCKS):
-            expert_product(last, m, 0, C // 2, False, bank[PRODUCT_BANKS[m - 1]])
-        expert_product(last, 1, C // 2, C, False, back_bank(turned_blocks + 3))
+            product(LATE, m, 0, C, last_places[m])
 
         half = T // 2
-        first = [a_pair[0][:, m, :] for m in range(ROW_BLOCKS)]
-        both = [a_pair[1][:, m, :] for m in range(ROW_BLOCKS)]
+        first = [a_sb[:, m, 0:T] for m in range(ROW_BLOCKS)]
+        both = [a_sb[:, m, T : 2 * T] for m in range(ROW_BLOCKS)]
         for m in range(ROW_BLOCKS):
             final = m + 1 == ROW_BLOCKS
             if m == 0:
-                cuts = (0, VECTOR_FIRST, half, T)
+                cuts = (0, VECTOR_FIRST, T)
             elif final:
                 cuts = (0, half, half + half // 2, T)
             else:
@@ -360,15 +374,13 @@ def tile_moe_sdb_silu_kernel(
                     nc.vector.tensor_copy(out=first[m][:, lo:hi], in_=window)
                 else:
                     nc.scalar.activation(out=first[m][:, lo:hi], in_=window, func=ACT.Copy)
-                if lo == 0 and 0 < m < ROW_BLOCKS - 1:
-                    expert_product(last, m + 1, C // 2, C, False, bank[PRODUCT_BANKS[m + 1]] if m == 2 else neg_g)
-            lo = 0
-            for width in (half, half // 2, half // 2) if final else (VECTOR_FIRST, half - VECTOR_FIRST, half) if m == 0 else (half, half):
+                if hi == T and m < ROW_BLOCKS - 1:
+                    copy_out(nc.scalar.copy, LATE, m + 1, 0, C, last_places[m + 1])
+            for lo, hi in zip(cuts, cuts[1:]):
                 nc.vector.tensor_tensor(
-                    out=both[m][:, lo : lo + width],
-                    in0=dx[m][:].indirect(entries(pos2_sb, lo, width)),
-                    in1=first[m][:, lo : lo + width],
+                    out=both[m][:, lo:hi],
+                    in0=dx[m][:].indirect(entries(pos2_sb, lo, hi - lo)),
+                    in1=first[m][:, lo:hi],
                     op=ALU.add,
                 )
-                nc.sync.dma_start(out=out[m * P : (m + 1) * P, lo : lo + width], in_=both[m][:, lo : lo + width])
-                lo = lo + width
+                nc.sync.dma_start(out=out[m * P : (m + 1) * P, lo:hi], in_=both[m][:, lo:hi])

@@ -38,11 +38,11 @@ TURNED = (
     + [(0, b) for b in range(EARLY // P, BLOCKS)]
     + [(LATE, b) for b in range(BLOCKS)]
 )
-SILU_BANKS = (0, 1, 2, 3, 4, 5, 6, 7, 0, 1, 5, 7, 3, 0)
+SILU_BANKS = (0, 1, 2, 3, 4, 5, 6, 7, 0, 1, 2, 3, 7, 0)
 GATE_BANK = 7
-SPREAD_BANK = 2
-BACK_BANKS = (3, 4, 6, 2, 4, 6, 2, 1, 5, 4, 2, 1, 5, 4)
-PRODUCT_BANKS = (7, 3, 0, 6)
+SPREAD_BANK = 4
+BACK_BANKS = (5, 6, 4, 5, 6, 1, 2, 4, 5, 6, 2, 4, 5, 6)
+PRODUCT_BANKS = (3, 7, 0, 1)
 SCALAR_GATES = (0, 1, 7, 8, 12)
 PACE_BLOCK = 1
 VECTOR_FIRST = 512
@@ -278,7 +278,7 @@ def tile_moe_sdb_silu_kernel(
             engine_copy(out=dx[m][:, e * C + lo : e * C + hi], in_=dx_ps)
 
         neg_g = bank[SPREAD_BANK]
-        for n in range(12):
+        for n in range(len(TURNED)):
             turn_block(n, bank[SILU_BANKS[n]])
             if n == PACE_BLOCK:
                 gather_plane(E - 1, 1)
@@ -329,8 +329,6 @@ def tile_moe_sdb_silu_kernel(
             if n < 10 or n > 11:
                 round_block(n)
             if n == 0:
-                turn_block(12, bank[SILU_BANKS[12]])
-                turn_block(13, bank[SILU_BANKS[13]])
                 for t in (2, 3):
                     nc.scalar.activation(
                         out=late_dc[:, t - 2, :], in_=dc[t][:].indirect(entries(offs_sb, LATE * C, C)), func=ACT.Copy
@@ -350,10 +348,10 @@ def tile_moe_sdb_silu_kernel(
                 quantise(LATE, 0, C // 2)
                 product(LATE, 0, 0, C // 2, bank[2][:, 0 : C // 2])
         quantise(LATE, C // 2, C)
-        product(LATE, 0, C // 2, C, bank[1][:, 0 : C // 2])
+        product(LATE, 0, C // 2, C, bank[4][:, 0 : C // 2])
         copy_out(nc.vector.tensor_copy, LATE, 0, 0, C // 2, bank[2][:, 0 : C // 2])
-        copy_out(nc.vector.tensor_copy, LATE, 0, C // 2, C, bank[1][:, 0 : C // 2])
-        last_places = {1: bank[5][:], 2: bank[4][:], 3: bank[PRODUCT_BANKS[0]][:]}
+        copy_out(nc.vector.tensor_copy, LATE, 0, C // 2, C, bank[4][:, 0 : C // 2])
+        last_places = {1: bank[5][:], 2: bank[6][:], 3: bank[PRODUCT_BANKS[0]][:]}
         for m in range(1, ROW_BLOCKS):
             product(LATE, m, 0, C, last_places[m])
 

@@ -38,13 +38,14 @@ TURNED = (
     + [(0, b) for b in range(EARLY // P, BLOCKS)]
     + [(LATE, b) for b in range(BLOCKS)]
 )
-SILU_BANKS = (0, 1, 2, 3, 4, 5, 6, 7, 0, 1, 2, 3, 7, 0)
+SILU_ORDER = (0, 1, 7, 2, 3, 4, 5, 6, 8, 9, 10, 11, 12, 13)
+SILU_BANKS = (0, 1, 2, 3, 4, 5, 6, 7, 0, 1, 2, 4, 7, 0)
 GATE_BANK = 7
-SPREAD_BANK = 4
-BACK_BANKS = (5, 6, 4, 5, 6, 1, 2, 4, 5, 6, 2, 4, 5, 6)
-PRODUCT_BANKS = (3, 7, 0, 1)
+SPREAD_BANK = 3
+BACK_BANKS = (5, 6, 3, 5, 6, 1, 2, 3, 5, 6, 2, 3, 5, 6)
+PRODUCT_BANKS = (4, 1, 7, 0)
 SCALAR_GATES = (0, 1, 7, 8, 12)
-PACE_BLOCK = 1
+PACE_BLOCK = 7
 VECTOR_FIRST = 512
 
 
@@ -129,7 +130,7 @@ def tile_moe_sdb_silu_kernel(
         late_dc = keep.tile([P, 2, C], F32, name="late_dc")
         places = {
             PACE_BLOCK: picked[3][:, 1, :],
-            7: late_dc[:, 0, :],
+            12: late_dc[:, 0, :],
             8: late_dc[:, 1, :],
             9: picked[LATE][:, 3, :],
             10: picked[LATE][:, 2, :],
@@ -278,11 +279,11 @@ def tile_moe_sdb_silu_kernel(
             engine_copy(out=dx[m][:, e * C + lo : e * C + hi], in_=dx_ps)
 
         neg_g = bank[SPREAD_BANK]
-        for n in range(len(TURNED)):
-            turn_block(n, bank[SILU_BANKS[n]])
+        for n, bank_index in zip(SILU_ORDER, SILU_BANKS):
+            turn_block(n, bank[bank_index])
             if n == PACE_BLOCK:
                 gather_plane(E - 1, 1)
-            if n == SPREAD_BANK:
+            if bank_index == SPREAD_BANK:
                 for b in range(EARLY // P):
                     nc.tensor.transpose(
                         neg_g[:, b * P : (b + 1) * P], neg_g_col[:, b : b + 1].to_broadcast([P, P]), ident[:]
@@ -310,7 +311,7 @@ def tile_moe_sdb_silu_kernel(
                 whole(1, m, 2 * m % ROW_BLOCKS)
                 whole(0, m, (2 * m + 1) % ROW_BLOCKS)
 
-        due = {9: first_products, 13: second_products}
+        due = {8: first_products, 13: second_products}
         for n in range(len(TURNED)):
             e, b = TURNED[n]
             if n not in gated:
@@ -348,9 +349,9 @@ def tile_moe_sdb_silu_kernel(
                 quantise(LATE, 0, C // 2)
                 product(LATE, 0, 0, C // 2, bank[2][:, 0 : C // 2])
         quantise(LATE, C // 2, C)
-        product(LATE, 0, C // 2, C, bank[4][:, 0 : C // 2])
+        product(LATE, 0, C // 2, C, bank[3][:, 0 : C // 2])
         copy_out(nc.vector.tensor_copy, LATE, 0, 0, C // 2, bank[2][:, 0 : C // 2])
-        copy_out(nc.vector.tensor_copy, LATE, 0, C // 2, C, bank[4][:, 0 : C // 2])
+        copy_out(nc.vector.tensor_copy, LATE, 0, C // 2, C, bank[3][:, 0 : C // 2])
         last_places = {1: bank[5][:], 2: bank[6][:], 3: bank[PRODUCT_BANKS[0]][:]}
         for m in range(1, ROW_BLOCKS):
             product(LATE, m, 0, C, last_places[m])

@@ -46,7 +46,7 @@ BACK_BANKS = (5, 6, 3, 5, 6, 1, 2, 3, 5, 6, 2, 3, 5, 6)
 PRODUCT_BANKS = (4, 1, 7, 0)
 SCALAR_GATES = (0, 1, 7, 8, 12)
 PACE_BLOCK = 7
-VECTOR_FIRST = 512
+VECTOR_FIRST = 384
 
 
 def tile_moe_sdb_silu_kernel(
@@ -348,11 +348,14 @@ def tile_moe_sdb_silu_kernel(
             if n == 12:
                 quantise(LATE, 0, C // 2)
                 product(LATE, 0, 0, C // 2, bank[2][:, 0 : C // 2])
-        quantise(LATE, C // 2, C)
-        product(LATE, 0, C // 2, C, bank[3][:, 0 : C // 2])
+        quantise(LATE, C // 2, C - P)
+        product(LATE, 0, C // 2, C - P, bank[3][:, 0:P])
+        quantise(LATE, C - P, C)
+        product(LATE, 0, C - P, C, bank[5][:, 0:P])
         copy_out(nc.vector.tensor_copy, LATE, 0, 0, C // 2, bank[2][:, 0 : C // 2])
-        copy_out(nc.vector.tensor_copy, LATE, 0, C // 2, C, bank[3][:, 0 : C // 2])
-        last_places = {1: bank[5][:], 2: bank[6][:], 3: bank[PRODUCT_BANKS[0]][:]}
+        copy_out(nc.vector.tensor_copy, LATE, 0, C // 2, C - P, bank[3][:, 0:P])
+        copy_out(nc.vector.tensor_copy, LATE, 0, C - P, C, bank[5][:, 0:P])
+        last_places = {1: bank[6][:], 2: bank[PRODUCT_BANKS[0]][:], 3: bank[PRODUCT_BANKS[1]][:]}
         for m in range(1, ROW_BLOCKS):
             product(LATE, m, 0, C, last_places[m])
 

@@ -38,15 +38,8 @@ TURNED = (
     + [(0, b) for b in range(EARLY // P, BLOCKS)]
     + [(LATE, b) for b in range(BLOCKS)]
 )
-SILU_ORDER = (0, 1, 7, 2, 3, 4, 5, 6, 8, 9, 10, 11, 12, 13)
-SILU_BANKS = (0, 1, 2, 3, 4, 5, 6, 7, 0, 1, 2, 4, 7, 0)
 GATE_BANK = 7
-SPREAD_BANK = 3
-BACK_BANKS = (5, 6, 3, 5, 6, 1, 2, 3, 5, 6, 2, 3, 5, 6)
-PRODUCT_BANKS = (4, 1, 7, 0)
-SCALAR_GATES = (0, 1, 7, 8, 12)
-PACE_BLOCK = 7
-VECTOR_FIRST = 384
+VECTOR_FIRST = 512
 
 
 def tile_moe_sdb_silu_kernel(
@@ -125,19 +118,20 @@ def tile_moe_sdb_silu_kernel(
         )
 
         dc = [keep.tile([P, T], F32, name="dc%d" % t, tag="dc%d" % t, align_bytes=64) for t in range(PACK)]
-        picked_flat = [keep.tile([P, PACK * C], F32, name="picked%d" % e) for e in range(E)]
-        picked = [x[:].rearrange("p (t j) -> p t j", t=PACK) for x in picked_flat]
-        late_dc = keep.tile([P, 2, C], F32, name="late_dc")
+        picked = [keep.tile([P, PACK, C], F32, name="picked%d" % e)[:] for e in range(E)]
+        late_dc = keep.tile([P, PACK - 1, C], F32, name="late_dc")
         places = {
-            PACE_BLOCK: picked[3][:, 1, :],
-            12: late_dc[:, 0, :],
-            8: late_dc[:, 1, :],
-            9: picked[LATE][:, 3, :],
-            10: picked[LATE][:, 2, :],
+            1: picked[3][:, 0, :],
+            4: late_dc[:, 0, :],
+            5: late_dc[:, 1, :],
+            6: late_dc[:, 2, :],
+            10: picked[LATE][:, 3, :],
+            11: picked[LATE][:, 2, :],
         }
-        own = [keep.tile([P, PACK * P], F32, name="u%d" % n)[:] for n in range(len(TURNED)) if n not in (9, 10)]
-        own = own[:9] + [None, None] + own[9:]
-        u_at = [places.get(n, own[n]) for n in range(len(TURNED))]
+        u_at = [
+            places[n] if n in places else keep.tile([P, PACK * P], F32, name="u%d" % n, tag="u%d" % n, align_bytes=64)[:]
+            for n in range(len(TURNED))
+        ]
         bank = [psum.tile([P, BANK], F32, name="bank%d" % n) for n in range(BANKS)]
 
         def entries(list_sb, first, count):
@@ -151,7 +145,7 @@ def tile_moe_sdb_silu_kernel(
 
         def gather_plane(e, t, lo=0, hi=C):
             nc.vector.tensor_tensor(
-                out=picked_flat[e][:, t * C + lo : t * C + hi],
+                out=picked[e][:, t, lo:hi],
                 in0=dc[t][:].indirect(entries(offs_sb, e * C + lo, hi - lo)),
                 in1=sg[:, t, e * C + lo : e * C + hi],
                 op=ALU.mult,
@@ -183,14 +177,14 @@ def tile_moe_sdb_silu_kernel(
             else:
                 gather_plane(0, t)
             gather_plane(1, t)
-            if t < 2:
-                gather_plane(2, t)
+            if t == 0:
+                gather_plane(LATE, t)
         nc.scalar.activation(out=sg[:, 2:4, 2 * C : 3 * C], in_=a_sb[:, 2:4, 2 * C : 3 * C], func=ACT.Sigmoid)
         for t in range(0, PACK, 2):
             nc.scalar.activation(
                 out=sg[:, t : t + 2, 3 * C : SLOTS], in_=a_sb[:, t : t + 2, 3 * C : SLOTS], func=ACT.Sigmoid
             )
-        for t in (0, 2, 3):
+        for t in (1, 2, 3):
             gather_plane(3, t)
 
         gate_ps = bank[GATE_BANK]
@@ -200,7 +194,7 @@ def tile_moe_sdb_silu_kernel(
         nc.scalar.copy(out=g_col[:], in_=gate_ps[:, 0 : SLOTS // P])
         nc.scalar.mul(out=neg_g_col[:], in_=gate_ps[:, 0 : SLOTS // P], mul=-1.0)
 
-        da_codes = [keep.tile([P, C], U32, name="da_codes%d" % e, align_bytes=64) for e in range(E)]
+        da_codes = {e: keep.tile([P, C], U32, name="da_codes%d" % e, align_bytes=64) for e in (0, LATE)}
         da_sc = [keep.tile([P, C], U8, name="da_sc%d" % e, align_bytes=64) for e in range(E)]
         da = {e: keep.tile([P, C, PACK], BF16, name="da%d" % e, tag="da%d" % e, align_bytes=64) for e in range(1, E)}
         dx = [keep.tile([P, SLOTS], F32, name="dx%d" % m) for m in range(ROW_BLOCKS)]
@@ -219,39 +213,46 @@ def tile_moe_sdb_silu_kernel(
             )
 
         gated = {}
+        at = {}
+        freed = []
+        taken = []
 
-        def turn_block(n, a_bank):
+        def take(key):
+            at[key] = freed[len(taken)]
+            taken.append(key)
+            return at[key]
+
+        def columns(n):
             e, b = TURNED[n]
             r = e * BLOCKS + b
-            a_turned = planes_of(a_bank)
+            return neg_g_col[:, r : r + 1], g_col[:, r : r + 1]
+
+        def turn(n):
+            e, b = TURNED[n]
+            r = e * BLOCKS + b
+            a_turned = planes_of(take(("a", n)))
             for t in range(PACK):
                 nc.tensor.transpose(a_turned[:, t, :], a_sb[:, t, r * P : (r + 1) * P], ident[:])
-            u = u_at[n]
-            nc.scalar.activation(out=u, in_=a_bank[:], func=ACT.Silu, scale=-1.0)
-            if n in SCALAR_GATES:
-                gated[n] = own[n]
-                nc.scalar.activation(
-                    out=gated[n], in_=u, func=ACT.Identity, scale=neg_g_col[:, r : r + 1], bias=g_col[:, r : r + 1]
-                )
 
-        def gate_block(n, gw):
-            e, b = TURNED[n]
-            r = e * BLOCKS + b
-            nc.gpsimd.tensor_scalar(
-                out=gw,
-                in0=u_at[n],
-                scalar1=neg_g_col[:, r : r + 1],
-                scalar2=g_col[:, r : r + 1],
-                op0=ALU.mult,
-                op1=ALU.add,
-            )
-            gated[n] = gw
+        def silu(n):
+            nc.scalar.activation(out=u_at[n], in_=at["a", n][:], func=ACT.Silu, scale=-1.0)
+            freed.append(at["a", n])
+
+        def gate_scalar(n):
+            neg_g, g = columns(n)
+            gated[n] = keep.tile([P, PACK * P], F32, name="gated%d" % n)[:]
+            nc.scalar.activation(out=gated[n], in_=u_at[n], func=ACT.Identity, scale=neg_g, bias=g)
+
+        def gate_gpsimd(n, place=None):
+            neg_g, g = columns(n)
+            gated[n] = u_at[n] if place is None else place
+            nc.gpsimd.tensor_scalar(out=gated[n], in0=u_at[n], scalar1=neg_g, scalar2=g, op0=ALU.mult, op1=ALU.add)
 
         def rounded(e, lo, hi):
             return da[e][:, lo:hi, :].rearrange("p (c i) t -> p c t i", i=RUN)
 
         def turn_back(n):
-            gw_back = planes_of(bank[BACK_BANKS[n]])
+            gw_back = planes_of(take(("back", n)))
             for t in range(PACK):
                 nc.tensor.transpose(gw_back[:, t, :], gated[n][:, t * P : (t + 1) * P], ident[:])
 
@@ -260,13 +261,14 @@ def tile_moe_sdb_silu_kernel(
             nc.vector.tensor_tensor(
                 out=rounded(e, b * P, (b + 1) * P),
                 in0=in_runs(picked[e][:, :, b * P : (b + 1) * P]),
-                in1=in_runs(planes_of(bank[BACK_BANKS[n]])),
+                in1=in_runs(planes_of(at["back", n])),
                 op=ALU.mult,
             )
+            freed.append(at["back", n])
 
-        def product(e, m, lo, hi, dx_ps):
+        def product(e, m, lo, hi):
             nc.tensor.matmul_mx(
-                out=dx_ps,
+                out=take(("dx", e, m, lo))[:, 0 : hi - lo],
                 lhsT=w1_codes[:, e, PACK * P * m : PACK * P * (m + 1)].bitcast(E4M3),
                 lhsT_scale=w1_sc[:, e * K + P * m : e * K + P * (m + 1)],
                 rhs=da_codes[e][:, lo:hi].bitcast(E5M2),
@@ -275,89 +277,109 @@ def tile_moe_sdb_silu_kernel(
                 stop=True,
             )
 
-        def copy_out(engine_copy, e, m, lo, hi, dx_ps):
-            engine_copy(out=dx[m][:, e * C + lo : e * C + hi], in_=dx_ps)
+        def copy_out(engine_copy, e, m, lo, hi):
+            engine_copy(out=dx[m][:, e * C + lo : e * C + hi], in_=at["dx", e, m, lo][:, 0 : hi - lo])
+            freed.append(at["dx", e, m, lo])
 
-        neg_g = bank[SPREAD_BANK]
-        for n, bank_index in zip(SILU_ORDER, SILU_BANKS):
-            turn_block(n, bank[bank_index])
-            if n == PACE_BLOCK:
-                gather_plane(E - 1, 1)
-            if bank_index == SPREAD_BANK:
-                for b in range(EARLY // P):
-                    nc.tensor.transpose(
-                        neg_g[:, b * P : (b + 1) * P], neg_g_col[:, b : b + 1].to_broadcast([P, P]), ident[:]
-                    )
-
-        da[0] = keep.tile([P, C, PACK], BF16, name="da0", tag="dc1", align_bytes=64)
-        runs = neg_g[:, 0:EARLY].rearrange("p (c i) -> p c i", i=RUN).unsqueeze(2)
-        nc.vector.tensor_tensor(
-            out=rounded(0, 0, EARLY),
-            in0=in_runs(picked[0][:, :, 0:EARLY]),
-            in1=runs.to_broadcast([P, EARLY // RUN, PACK, RUN]),
-            op=ALU.mult,
-        )
-
-        def whole(e, m, bank_index):
-            product(e, m, 0, C, bank[PRODUCT_BANKS[bank_index]][:])
-            copy_out(nc.scalar.copy, e, m, 0, C, bank[PRODUCT_BANKS[bank_index]][:])
-
-        def first_products():
-            for m in range(ROW_BLOCKS):
-                whole(3, m, m)
-
-        def second_products():
-            for m in range(ROW_BLOCKS):
-                whole(1, m, 2 * m % ROW_BLOCKS)
-                whole(0, m, (2 * m + 1) % ROW_BLOCKS)
-
-        due = {8: first_products, 13: second_products}
-        for n in range(len(TURNED)):
-            e, b = TURNED[n]
-            if n not in gated:
-                if n == 2:
-                    gw = sg[:, 1, (E - 1) * C : E * C]
-                elif n == 9:
-                    gw = keep.tile([P, PACK * P], F32, name="held", tag="da3", align_bytes=64)[:]
-                elif n == 13:
-                    gw = late_dc[:, 0, :]
-                else:
-                    gw = u_at[n - 1]
-                gate_block(n, gw)
-            turn_back(n)
-            if n in due:
-                due[n]()
-            if n < 10 or n > 11:
-                round_block(n)
-            if n == 0:
-                for t in (2, 3):
-                    nc.scalar.activation(
-                        out=late_dc[:, t - 2, :], in_=dc[t][:].indirect(entries(offs_sb, LATE * C, C)), func=ACT.Copy
-                    )
-            if n == 3:
-                quantise(3, 0, C)
-            if n == 9:
-                quantise(1, 0, C)
-                quantise(0, 0, C)
-            if n == 11:
-                nc.vector.tensor_tensor(
-                    out=picked[LATE][:, 2:4, :], in0=late_dc[:], in1=sg[:, 2:4, LATE * C : (LATE + 1) * C], op=ALU.mult
+        def spread_gate():
+            neg_g = take("spread")
+            for b in range(EARLY // P):
+                nc.tensor.transpose(
+                    neg_g[:, b * P : (b + 1) * P], neg_g_col[:, b : b + 1].to_broadcast([P, P]), ident[:]
                 )
-                round_block(10)
-                round_block(11)
-            if n == 12:
-                quantise(LATE, 0, C // 2)
-                product(LATE, 0, 0, C // 2, bank[2][:, 0 : C // 2])
-        quantise(LATE, C // 2, C - P)
-        product(LATE, 0, C // 2, C - P, bank[3][:, 0:P])
-        quantise(LATE, C - P, C)
-        product(LATE, 0, C - P, C, bank[5][:, 0:P])
-        copy_out(nc.vector.tensor_copy, LATE, 0, 0, C // 2, bank[2][:, 0 : C // 2])
-        copy_out(nc.vector.tensor_copy, LATE, 0, C // 2, C - P, bank[3][:, 0:P])
-        copy_out(nc.vector.tensor_copy, LATE, 0, C - P, C, bank[5][:, 0:P])
-        last_places = {1: bank[6][:], 2: bank[PRODUCT_BANKS[0]][:], 3: bank[PRODUCT_BANKS[1]][:]}
+
+        def round_early():
+            da[0] = keep.tile([P, C, PACK], BF16, name="da0", tag="dc0", align_bytes=64)
+            runs = at["spread"][:, 0:EARLY].rearrange("p (c i) -> p c i", i=RUN).unsqueeze(2)
+            nc.vector.tensor_tensor(
+                out=rounded(0, 0, EARLY),
+                in0=in_runs(picked[0][:, :, 0:EARLY]),
+                in1=runs.to_broadcast([P, EARLY // RUN, PACK, RUN]),
+                op=ALU.mult,
+            )
+            freed.append(at["spread"])
+
+        freed.extend(bank)
+        for n in range(BANKS):
+            turn(n)
+        silu(0)
+        gate_scalar(0)
+        spread_gate()
+        silu(1)
+        gate_scalar(1)
+        gather_plane(E - 1, 0)
+        turn_back(0)
+        silu(2)
+        turn(8)
+        silu(3)
+        turn(9)
+        silu(4)
+        turn_back(1)
+        silu(5)
+        turn(10)
+        gate_gpsimd(2, sg[:, 0, (E - 1) * C : E * C])
+        silu(6)
+        turn(11)
+        round_early()
+        turn_back(2)
+        silu(7)
+        turn(12)
+        gate_gpsimd(3, u_at[2])
+        round_block(0)
+        turn_back(3)
+        silu(8)
+        turn(13)
+        round_block(1)
+        for n in range(4, 12):
+            gate_gpsimd(n)
+            turn_back(n)
+            if n + 5 < len(TURNED):
+                silu(n + 5)
+            if n > 4:
+                round_block(n - 3)
+        for t in range(1, PACK):
+            nc.scalar.activation(
+                out=late_dc[:, t - 1, :], in_=dc[t][:].indirect(entries(offs_sb, LATE * C, C)), func=ACT.Copy
+            )
+        gate_gpsimd(12)
+        round_block(9)
+        da_codes[3] = keep.tile([P, C], U32, name="da_codes3", tag="u9", align_bytes=64)
+        quantise(3, 0, C)
+        for m in range(ROW_BLOCKS):
+            product(3, m, 0, C)
+        da_codes[1] = keep.tile([P, C], U32, name="da_codes1", tag="da3", align_bytes=64)
+        quantise(1, 0, C)
+        quantise(0, 0, C)
+        for m in range(ROW_BLOCKS):
+            product(1, m, 0, C)
+            copy_out(nc.scalar.copy, 3, m, 0, C)
+            if m == 1:
+                turn_back(12)
+        nc.vector.tensor_tensor(
+            out=picked[LATE][:, 1:PACK, :], in0=late_dc[:], in1=sg[:, 1:PACK, LATE * C : (LATE + 1) * C], op=ALU.mult
+        )
+        product(0, 0, 0, C)
+        round_block(10)
+        gate_gpsimd(13, late_dc[:, 0, :])
+        turn_back(13)
+        round_block(11)
+        for m in range(ROW_BLOCKS):
+            copy_out(nc.scalar.copy, 1, m, 0, C)
         for m in range(1, ROW_BLOCKS):
-            product(LATE, m, 0, C, last_places[m])
+            product(0, m, 0, C)
+        round_block(12)
+        pieces_late = ((0, C // 2), (C // 2, C - P), (C - P, C))
+        for x, (lo, hi) in enumerate(pieces_late):
+            quantise(LATE, lo, hi)
+            product(LATE, 0, lo, hi)
+            if x == 0:
+                round_block(13)
+        for m in range(ROW_BLOCKS):
+            copy_out(nc.scalar.copy, 0, m, 0, C)
+        for m in range(1, ROW_BLOCKS):
+            product(LATE, m, 0, C)
+        for lo, hi in pieces_late:
+            copy_out(nc.vector.tensor_copy, LATE, 0, lo, hi)
 
         half = T // 2
         first = [a_sb[:, m, 0:T] for m in range(ROW_BLOCKS)]
@@ -377,7 +399,7 @@ def tile_moe_sdb_silu_kernel(
                 else:
                     nc.scalar.activation(out=first[m][:, lo:hi], in_=window, func=ACT.Copy)
                 if hi == T and m < ROW_BLOCKS - 1:
-                    copy_out(nc.scalar.copy, LATE, m + 1, 0, C, last_places[m + 1])
+                    copy_out(nc.scalar.copy, LATE, m + 1, 0, C)
             for lo, hi in zip(cuts, cuts[1:]):
                 nc.vector.tensor_tensor(
                     out=both[m][:, lo:hi],

@@ -39,7 +39,7 @@ TURNED = (
     + [(LATE, b) for b in range(BLOCKS)]
 )
 GATE_BANK = 7
-VECTOR_FIRST = 512
+VECTOR_FIRST = 640
 
 
 def tile_moe_sdb_silu_kernel(
@@ -310,6 +310,7 @@ def tile_moe_sdb_silu_kernel(
         gather_plane(E - 1, 0)
         turn_back(0)
         silu(2)
+        gate_scalar(2)
         turn(8)
         silu(3)
         turn(9)
@@ -317,21 +318,20 @@ def tile_moe_sdb_silu_kernel(
         turn_back(1)
         silu(5)
         turn(10)
-        gate_gpsimd(2, sg[:, 0, (E - 1) * C : E * C])
+        gate_gpsimd(3, sg[:, 0, (E - 1) * C : E * C])
         silu(6)
         turn(11)
         round_early()
         turn_back(2)
         silu(7)
         turn(12)
-        gate_gpsimd(3, u_at[2])
         round_block(0)
         turn_back(3)
         silu(8)
         turn(13)
         round_block(1)
         for n in range(4, 12):
-            gate_gpsimd(n)
+            gate_gpsimd(n, u_at[3] if n == 4 else None)
             turn_back(n)
             if n + 5 < len(TURNED):
                 silu(n + 5)
@@ -389,7 +389,7 @@ def tile_moe_sdb_silu_kernel(
             if m == 0:
                 cuts = (0, VECTOR_FIRST, T)
             elif final:
-                cuts = (0, half, half + half // 2, T)
+                cuts = tuple(range(0, T + 1, half // 2))
             else:
                 cuts = (0, half, T)
             for lo, hi in zip(cuts, cuts[1:]):

@@ -121,7 +121,7 @@ def tile_moe_sdb_silu_kernel(
         picked = [keep.tile([P, PACK, C], F32, name="picked%d" % e)[:] for e in range(E)]
         late_dc = keep.tile([P, PACK - 1, C], F32, name="late_dc")
         places = {
-            1: picked[3][:, 0, :],
+            0: picked[3][:, 0, :],
             4: late_dc[:, 0, :],
             5: late_dc[:, 1, :],
             6: late_dc[:, 2, :],
@@ -243,10 +243,10 @@ def tile_moe_sdb_silu_kernel(
             gated[n] = keep.tile([P, PACK * P], F32, name="gated%d" % n)[:]
             nc.scalar.activation(out=gated[n], in_=u_at[n], func=ACT.Identity, scale=neg_g, bias=g)
 
-        def gate_gpsimd(n, place=None):
+        def gate_gpsimd(n, place=None, engine=nc.gpsimd):
             neg_g, g = columns(n)
             gated[n] = u_at[n] if place is None else place
-            nc.gpsimd.tensor_scalar(out=gated[n], in0=u_at[n], scalar1=neg_g, scalar2=g, op0=ALU.mult, op1=ALU.add)
+            engine.tensor_scalar(out=gated[n], in0=u_at[n], scalar1=neg_g, scalar2=g, op0=ALU.mult, op1=ALU.add)
 
         def rounded(e, lo, hi):
             return da[e][:, lo:hi, :].rearrange("p (c i) t -> p c t i", i=RUN)
@@ -268,7 +268,7 @@ def tile_moe_sdb_silu_kernel(
 
         def product(e, m, lo, hi):
             nc.tensor.matmul_mx(
-                out=take(("dx", e, m, lo))[:, 0 : hi - lo],
+                out=(at["dx", e, m, lo] if ("dx", e, m, lo) in at else take(("dx", e, m, lo)))[:, 0 : hi - lo],
                 lhsT=w1_codes[:, e, PACK * P * m : PACK * P * (m + 1)].bitcast(E4M3),
                 lhsT_scale=w1_sc[:, e * K + P * m : e * K + P * (m + 1)],
                 rhs=da_codes[e][:, lo:hi].bitcast(E5M2),
@@ -303,62 +303,65 @@ def tile_moe_sdb_silu_kernel(
         for n in range(BANKS):
             turn(n)
         silu(0)
-        gate_scalar(0)
         spread_gate()
-        silu(1)
-        gate_scalar(1)
+        for n in range(1, 3):
+            silu(n)
+            turn(n + 7)
+        gate_scalar(0)
         gather_plane(E - 1, 0)
-        turn_back(0)
-        silu(2)
-        gate_scalar(2)
-        turn(8)
         silu(3)
-        turn(9)
-        silu(4)
-        turn_back(1)
-        silu(5)
         turn(10)
+        gate_scalar(1)
+        gate_scalar(2)
+        for n in range(2):
+            silu(n + 4)
+            turn_back(n)
         gate_gpsimd(3, sg[:, 0, (E - 1) * C : E * C])
-        silu(6)
-        turn(11)
         round_early()
         turn_back(2)
-        silu(7)
-        turn(12)
-        round_block(0)
+        silu(6)
         turn_back(3)
-        silu(8)
-        turn(13)
-        round_block(1)
-        for n in range(4, 12):
-            gate_gpsimd(n, u_at[3] if n == 4 else None)
-            turn_back(n)
-            if n + 5 < len(TURNED):
-                silu(n + 5)
-            if n > 4:
-                round_block(n - 3)
+        round_block(0)
+        gate_gpsimd(4, u_at[3])
+        turn_back(4)
+        silu(7)
+        turn(11)
+        for n in range(5, 12):
+            round_block(n - 4)
+            gate_gpsimd(n)
+            if n < 11:
+                turn_back(n)
+            if n + 3 < 12:
+                silu(n + 3)
         for t in range(1, PACK):
             nc.scalar.activation(
                 out=late_dc[:, t - 1, :], in_=dc[t][:].indirect(entries(offs_sb, LATE * C, C)), func=ACT.Copy
             )
-        gate_gpsimd(12)
+        for m in range(ROW_BLOCKS):
+            take(("dx", 3, m, 0))
+        turn(12)
+        round_block(8)
+        turn(13)
         round_block(9)
+        turn_back(11)
+        silu(12)
+        silu(13)
         da_codes[3] = keep.tile([P, C], U32, name="da_codes3", tag="u9", align_bytes=64)
         quantise(3, 0, C)
         for m in range(ROW_BLOCKS):
             product(3, m, 0, C)
         da_codes[1] = keep.tile([P, C], U32, name="da_codes1", tag="da3", align_bytes=64)
         quantise(1, 0, C)
+        gate_gpsimd(12, u_at[8], nc.vector)
         quantise(0, 0, C)
-        for m in range(ROW_BLOCKS):
-            product(1, m, 0, C)
+        turn_back(12)
+        product(1, 0, 0, C)
+        for m, (e_next, m_next) in enumerate(((1, 1), (1, 2), (1, 3), (0, 0))):
             copy_out(nc.scalar.copy, 3, m, 0, C)
-            if m == 1:
-                turn_back(12)
+            product(e_next, m_next, 0, C)
         nc.vector.tensor_tensor(
             out=picked[LATE][:, 1:PACK, :], in0=late_dc[:], in1=sg[:, 1:PACK, LATE * C : (LATE + 1) * C], op=ALU.mult
         )
-        product(0, 0, 0, C)
         round_block(10)
         gate_gpsimd(13, late_dc[:, 0, :])
         turn_back(13)

@@ -126,7 +126,6 @@ def tile_moe_sdb_silu_kernel(
             5: late_dc[:, 1, :],
             6: late_dc[:, 2, :],
             10: picked[LATE][:, 3, :],
-            11: picked[LATE][:, 2, :],
         }
         u_at = [
             places[n] if n in places else keep.tile([P, PACK * P], F32, name="u%d" % n, tag="u%d" % n, align_bytes=64)[:]
@@ -311,11 +310,10 @@ def tile_moe_sdb_silu_kernel(
         gather_plane(E - 1, 0)
         silu(3)
         turn(10)
-        gate_scalar(1)
-        gate_scalar(2)
         for n in range(2):
             silu(n + 4)
             turn_back(n)
+            gate_scalar(n + 1)
         gate_gpsimd(3, sg[:, 0, (E - 1) * C : E * C])
         round_early()
         turn_back(2)
@@ -343,7 +341,6 @@ def tile_moe_sdb_silu_kernel(
         round_block(8)
         turn(13)
         round_block(9)
-        turn_back(11)
         silu(12)
         silu(13)
         da_codes[3] = keep.tile([P, C], U32, name="da_codes3", tag="u9", align_bytes=64)
@@ -352,13 +349,18 @@ def tile_moe_sdb_silu_kernel(
             product(3, m, 0, C)
         da_codes[1] = keep.tile([P, C], U32, name="da_codes1", tag="da3", align_bytes=64)
         quantise(1, 0, C)
-        gate_gpsimd(12, u_at[8], nc.vector)
         quantise(0, 0, C)
+        gate_gpsimd(12, keep.tile([P, PACK * P], F32, name="gated12", tag="da1", align_bytes=64)[:], nc.vector)
+        for m in range(3):
+            product(1, m, 0, C)
+        copy_out(nc.scalar.copy, 3, 0, 0, C)
+        turn_back(11)
+        copy_out(nc.scalar.copy, 3, 1, 0, C)
         turn_back(12)
-        product(1, 0, 0, C)
-        for m, (e_next, m_next) in enumerate(((1, 1), (1, 2), (1, 3), (0, 0))):
-            copy_out(nc.scalar.copy, 3, m, 0, C)
-            product(e_next, m_next, 0, C)
+        copy_out(nc.scalar.copy, 3, 2, 0, C)
+        product(1, 3, 0, C)
+        copy_out(nc.scalar.copy, 3, 3, 0, C)
+        product(0, 0, 0, C)
         nc.vector.tensor_tensor(
             out=picked[LATE][:, 1:PACK, :], in0=late_dc[:], in1=sg[:, 1:PACK, LATE * C : (LATE + 1) * C], op=ALU.mult
         )

@@ -31,7 +31,7 @@ SCALE_ROWS = 16
 RUN = 4
 
 BANKS = 8
-EARLY = 256
+EARLY = 384
 LATE = 2
 TURNED = (
     [(e, b) for e in (3, 1) for b in range(BLOCKS)]
@@ -55,7 +55,7 @@ def tile_moe_sdb_silu_kernel(
         pos2_sb = keep.tile([P, T // PER_COLUMN], U16, name="pos2_sb")
 
         w2_raw = keep.tile([P, 2 * H], U8, name="w2_raw", align_bytes=64)
-        w2_sc_raw = keep.tile([P, H], U8, name="w2_sc_raw", align_bytes=64)
+        w2_sc_raw = keep.tile([P, H], U8, name="w2_sc_raw", tag="w2_sc_raw", align_bytes=64)
         w2_codes = keep.tile([P, 2 * H], U8, name="w2_codes", align_bytes=64)
         w2_sc = keep.tile([P, H], U8, name="w2_sc", align_bytes=64)
         dy_codes = keep.tile([P, PACK * T], U8, name="dy_codes", align_bytes=64)
@@ -125,7 +125,7 @@ def tile_moe_sdb_silu_kernel(
             4: late_dc[:, 0, :],
             5: late_dc[:, 1, :],
             6: late_dc[:, 2, :],
-            10: picked[LATE][:, 3, :],
+            9: picked[LATE][:, 3, :],
         }
         u_at = [
             places[n] if n in places else keep.tile([P, PACK * P], F32, name="u%d" % n, tag="u%d" % n, align_bytes=64)[:]
@@ -139,8 +139,11 @@ def tile_moe_sdb_silu_kernel(
         for x in range(2):
             a_x, s_x = a_sb[:, 2 * x : 2 * x + 2, 0:EARLY], sg[:, 2 * x : 2 * x + 2, 0:EARLY]
             nc.scalar.activation(out=s_x, in_=a_x, func=ACT.Sigmoid)
-            nc.vector.scalar_tensor_tensor(out=a_x, in0=s_x, scalar=1.0, in1=a_x, op0=ALU.subtract, op1=ALU.mult)
-            nc.vector.scalar_tensor_tensor(out=s_x, in0=a_x, scalar=1.0, in1=s_x, op0=ALU.subtract, op1=ALU.mult)
+            u_x = a_x
+            if x == 0:
+                u_x = keep.tile([P, 2, EARLY], F32, name="u_early", tag="w2_sc_raw", align_bytes=64)[:]
+            nc.vector.scalar_tensor_tensor(out=u_x, in0=s_x, scalar=1.0, in1=a_x, op0=ALU.subtract, op1=ALU.mult)
+            nc.vector.scalar_tensor_tensor(out=s_x, in0=u_x, scalar=1.0, in1=s_x, op0=ALU.subtract, op1=ALU.mult)
 
         def gather_plane(e, t, lo=0, hi=C):
             nc.vector.tensor_tensor(
@@ -165,10 +168,7 @@ def tile_moe_sdb_silu_kernel(
                             start=True,
                             stop=True,
                         )
-                        if (t, h) == (0, 1):
-                            nc.vector.tensor_copy(out=dc[t][:, tokens], in_=dc_ps[:])
-                        else:
-                            nc.scalar.copy(out=dc[t][:, tokens], in_=dc_ps[:])
+                        nc.scalar.copy(out=dc[t][:, tokens], in_=dc_ps[:])
                 nc.scalar.activation(out=sg[:, t, lo:hi], in_=a_sb[:, t, lo:hi], func=ACT.Sigmoid)
             if t == 0:
                 gather_plane(0, t, 0, EARLY)
@@ -323,13 +323,12 @@ def tile_moe_sdb_silu_kernel(
         gate_gpsimd(4, u_at[3])
         turn_back(4)
         silu(7)
-        turn(11)
-        for n in range(5, 12):
+        for n in range(5, 11):
             round_block(n - 4)
             gate_gpsimd(n)
-            if n < 11:
+            if n < 10:
                 turn_back(n)
-            if n + 3 < 12:
+            if n + 3 < 11:
                 silu(n + 3)
         for t in range(1, PACK):
             nc.scalar.activation(
@@ -337,26 +336,26 @@ def tile_moe_sdb_silu_kernel(
             )
         for m in range(ROW_BLOCKS):
             take(("dx", 3, m, 0))
+        turn(11)
+        round_block(7)
         turn(12)
         round_block(8)
-        turn(13)
-        round_block(9)
+        silu(11)
         silu(12)
-        silu(13)
-        da_codes[3] = keep.tile([P, C], U32, name="da_codes3", tag="u9", align_bytes=64)
+        da_codes[3] = keep.tile([P, C], U32, name="da_codes3", tag="u8", align_bytes=64)
         quantise(3, 0, C)
         for m in range(ROW_BLOCKS):
             product(3, m, 0, C)
         da_codes[1] = keep.tile([P, C], U32, name="da_codes1", tag="da3", align_bytes=64)
         quantise(1, 0, C)
         quantise(0, 0, C)
-        gate_gpsimd(12, keep.tile([P, PACK * P], F32, name="gated12", tag="da1", align_bytes=64)[:], nc.vector)
+        gate_gpsimd(11, keep.tile([P, PACK * P], F32, name="gated11", tag="da1", align_bytes=64)[:], nc.vector)
         for m in range(3):
             product(1, m, 0, C)
         copy_out(nc.scalar.copy, 3, 0, 0, C)
-        turn_back(11)
+        turn_back(10)
         copy_out(nc.scalar.copy, 3, 1, 0, C)
-        turn_back(12)
+        turn_back(11)
         copy_out(nc.scalar.copy, 3, 2, 0, C)
         product(1, 3, 0, C)
         copy_out(nc.scalar.copy, 3, 3, 0, C)
@@ -364,21 +363,21 @@ def tile_moe_sdb_silu_kernel(
         nc.vector.tensor_tensor(
             out=picked[LATE][:, 1:PACK, :], in0=late_dc[:], in1=sg[:, 1:PACK, LATE * C : (LATE + 1) * C], op=ALU.mult
         )
+        round_block(9)
+        gate_gpsimd(12, late_dc[:, 0, :])
+        turn_back(12)
         round_block(10)
-        gate_gpsimd(13, late_dc[:, 0, :])
-        turn_back(13)
-        round_block(11)
         for m in range(ROW_BLOCKS):
             copy_out(nc.scalar.copy, 1, m, 0, C)
         for m in range(1, ROW_BLOCKS):
             product(0, m, 0, C)
-        round_block(12)
+        round_block(11)
         pieces_late = ((0, C // 2), (C // 2, C - P), (C - P, C))
         for x, (lo, hi) in enumerate(pieces_late):
             quantise(LATE, lo, hi)
             product(LATE, 0, lo, hi)
             if x == 0:
-                round_block(13)
+                round_block(12)
         for m in range(ROW_BLOCKS):
             copy_out(nc.scalar.copy, 0, m, 0, C)
         for m in range(1, ROW_BLOCKS):

@@ -32,9 +32,12 @@ RUN = 4
 
 BANKS = 8
 EARLY = 384
-LATE = 2
+FIRST = 2
+WIDE = 3 * C
+SPARE = WIDE + 16 - T
+LATE = 3
 TURNED = (
-    [(e, b) for e in (3, 1) for b in range(BLOCKS)]
+    [(e, b) for e in (FIRST, 1) for b in range(BLOCKS)]
     + [(0, b) for b in range(EARLY // P, BLOCKS)]
     + [(LATE, b) for b in range(BLOCKS)]
 )
@@ -86,15 +89,14 @@ def tile_moe_sdb_silu_kernel(
         load_scale_rows(dy_sc[:].bitcast(I32), dy_scales[0].bitcast(I32))
 
         def pieces(t):
-            cuts = (EARLY, 2 * C, 3 * C) if t < 2 else (EARLY, 2 * C)
+            cuts = (EARLY, 2 * C, WIDE) if t < 2 else (EARLY, WIDE)
             return list(zip(cuts, cuts[1:]))
 
         for t in range(PACK):
-            for lo, hi in pieces(t) if t != 1 else [(EARLY, 3 * C)]:
+            for lo, hi in pieces(t) if t != 1 else [(EARLY, WIDE)]:
                 nc.sync.dma_start(out=a_sb[:, t, lo:hi], in_=a_planes[:, t, lo:hi])
                 if t == 0 and lo == EARLY:
                     nc.sync.dma_start(offs_sb[:], offs)
-        nc.sync.dma_start(out=a_sb[:, 2:4, 2 * C : 3 * C], in_=a_planes[:, 2:4, 2 * C : 3 * C])
         for t in range(0, PACK, 2):
             nc.sync.dma_start(out=a_sb[:, t : t + 2, 3 * C : SLOTS], in_=a_planes[:, t : t + 2, 3 * C : SLOTS])
         nc.sync.dma_start(out=gate_rows[0 : SLOTS // P, :], in_=gate[0].rearrange("(r c) -> r c", c=P))
@@ -117,11 +119,13 @@ def tile_moe_sdb_silu_kernel(
             in_=w2_sc_raw[:].rearrange("p (m t) -> p t m", t=PACK),
         )
 
-        dc = [keep.tile([P, T], F32, name="dc%d" % t, tag="dc%d" % t, align_bytes=64) for t in range(PACK)]
-        picked = [keep.tile([P, PACK, C], F32, name="picked%d" % e)[:] for e in range(E)]
+        dc = [keep.tile([P, T + SPARE], F32, name="dc%d" % t, tag="dc%d" % t, align_bytes=64) for t in range(PACK)]
+        picked_wide = keep.tile([P, PACK, WIDE], F32, name="picked_wide")
+        picked = [picked_wide[:, :, e * C : (e + 1) * C] for e in range(LATE)]
+        picked = picked + [keep.tile([P, PACK, C], F32, name="picked_late")[:]]
         late_dc = keep.tile([P, PACK - 1, C], F32, name="late_dc")
         places = {
-            0: picked[3][:, 0, :],
+            0: picked[LATE][:, 0, :],
             4: late_dc[:, 0, :],
             5: late_dc[:, 1, :],
             6: late_dc[:, 2, :],
@@ -147,7 +151,7 @@ def tile_moe_sdb_silu_kernel(
 
         def gather_plane(e, t, lo=0, hi=C):
             nc.vector.tensor_tensor(
-                out=picked[e][:, t, lo:hi],
+                out=(picked_wide if e == 0 else picked[e])[:, t, lo:hi],
                 in0=dc[t][:].indirect(entries(offs_sb, e * C + lo, hi - lo)),
                 in1=sg[:, t, e * C + lo : e * C + hi],
                 op=ALU.mult,
@@ -172,19 +176,17 @@ def tile_moe_sdb_silu_kernel(
                 nc.scalar.activation(out=sg[:, t, lo:hi], in_=a_sb[:, t, lo:hi], func=ACT.Sigmoid)
             if t == 0:
                 gather_plane(0, t, 0, EARLY)
-                gather_plane(0, t, EARLY, C)
+                for lo, hi in pieces(t):
+                    gather_plane(0, t, lo, hi)
+            elif t == 1:
+                gather_plane(0, t, 0, 2 * C)
+                gather_plane(0, t, 2 * C, WIDE)
             else:
-                gather_plane(0, t)
-            gather_plane(1, t)
-            if t == 0:
-                gather_plane(LATE, t)
-        nc.scalar.activation(out=sg[:, 2:4, 2 * C : 3 * C], in_=a_sb[:, 2:4, 2 * C : 3 * C], func=ACT.Sigmoid)
+                gather_plane(0, t, 0, WIDE)
         for t in range(0, PACK, 2):
             nc.scalar.activation(
                 out=sg[:, t : t + 2, 3 * C : SLOTS], in_=a_sb[:, t : t + 2, 3 * C : SLOTS], func=ACT.Sigmoid
             )
-        for t in (1, 2, 3):
-            gather_plane(3, t)
 
         gate_ps = bank[GATE_BANK]
         nc.tensor.transpose(gate_ps[:, 0:P], gate_rows[:], ident[:])
@@ -335,30 +337,30 @@ def tile_moe_sdb_silu_kernel(
                 out=late_dc[:, t - 1, :], in_=dc[t][:].indirect(entries(offs_sb, LATE * C, C)), func=ACT.Copy
             )
         for m in range(ROW_BLOCKS):
-            take(("dx", 3, m, 0))
+            take(("dx", FIRST, m, 0))
         turn(11)
         round_block(7)
         turn(12)
         round_block(8)
         silu(11)
         silu(12)
-        da_codes[3] = keep.tile([P, C], U32, name="da_codes3", tag="u8", align_bytes=64)
-        quantise(3, 0, C)
+        da_codes[FIRST] = keep.tile([P, C], U32, name="da_codes_first", tag="u8", align_bytes=64)
+        quantise(FIRST, 0, C)
         for m in range(ROW_BLOCKS):
-            product(3, m, 0, C)
-        da_codes[1] = keep.tile([P, C], U32, name="da_codes1", tag="da3", align_bytes=64)
+            product(FIRST, m, 0, C)
+        da_codes[1] = keep.tile([P, C], U32, name="da_codes1", tag="da%d" % FIRST, align_bytes=64)
         quantise(1, 0, C)
         quantise(0, 0, C)
         gate_gpsimd(11, keep.tile([P, PACK * P], F32, name="gated11", tag="da1", align_bytes=64)[:], nc.vector)
         for m in range(3):
             product(1, m, 0, C)
-        copy_out(nc.scalar.copy, 3, 0, 0, C)
+        copy_out(nc.scalar.copy, FIRST, 0, 0, C)
         turn_back(10)
-        copy_out(nc.scalar.copy, 3, 1, 0, C)
+        copy_out(nc.scalar.copy, FIRST, 1, 0, C)
         turn_back(11)
-        copy_out(nc.scalar.copy, 3, 2, 0, C)
+        copy_out(nc.scalar.copy, FIRST, 2, 0, C)
         product(1, 3, 0, C)
-        copy_out(nc.scalar.copy, 3, 3, 0, C)
+        copy_out(nc.scalar.copy, FIRST, 3, 0, C)
         product(0, 0, 0, C)
         nc.vector.tensor_tensor(
             out=picked[LATE][:, 1:PACK, :], in0=late_dc[:], in1=sg[:, 1:PACK, LATE * C : (LATE + 1) * C], op=ALU.mult

@@ -309,13 +309,15 @@ def tile_moe_sdb_silu_kernel(
             silu(n)
             turn(n + 7)
         gate_scalar(0)
+        gate_gpsimd(2, None, nc.vector)
         gather_plane(E - 1, 0)
         silu(3)
         turn(10)
         for n in range(2):
             silu(n + 4)
             turn_back(n)
-            gate_scalar(n + 1)
+            if n == 0:
+                gate_scalar(1)
         gate_gpsimd(3, sg[:, 0, (E - 1) * C : E * C])
         round_early()
         turn_back(2)

@@ -42,7 +42,7 @@ TURNED = (
     + [(LATE, b) for b in range(BLOCKS)]
 )
 GATE_BANK = 7
-VECTOR_FIRST = 640
+VECTOR_FIRST = 128
 
 
 def tile_moe_sdb_silu_kernel(
@@ -395,7 +395,7 @@ def tile_moe_sdb_silu_kernel(
         for m in range(ROW_BLOCKS):
             final = m + 1 == ROW_BLOCKS
             if m == 0:
-                cuts = (0, VECTOR_FIRST, T)
+                cuts = (0, VECTOR_FIRST, (VECTOR_FIRST + T) // 2, T)
             elif final:
                 cuts = tuple(range(0, T + 1, half // 2))
             else:
@@ -406,7 +406,10 @@ def tile_moe_sdb_silu_kernel(
                     nc.vector.tensor_copy(out=first[m][:, lo:hi], in_=window)
                 else:
                     nc.scalar.activation(out=first[m][:, lo:hi], in_=window, func=ACT.Copy)
-                if hi == T and m < ROW_BLOCKS - 1:
+                if lo == 0 and m == 0:
+                    for x in (1, 2):
+                        copy_out(nc.vector.tensor_copy, LATE, x, 0, C)
+                if hi == T and m == ROW_BLOCKS - 2:
                     copy_out(nc.scalar.copy, LATE, m + 1, 0, C)
             for lo, hi in zip(cuts, cuts[1:]):
                 nc.vector.tensor_tensor(

@@ -42,7 +42,6 @@ TURNED = (
     + [(LATE, b) for b in range(BLOCKS)]
 )
 GATE_BANK = 7
-VECTOR_FIRST = 128
 
 
 def tile_moe_sdb_silu_kernel(
@@ -388,34 +387,22 @@ def tile_moe_sdb_silu_kernel(
             product(LATE, m, 0, C)
         for lo, hi in pieces_late:
             copy_out(nc.vector.tensor_copy, LATE, 0, lo, hi)
+        for m in range(1, ROW_BLOCKS):
+            copy_out(nc.vector.tensor_copy, LATE, m, 0, C)
 
-        half = T // 2
+        half, quarter = T // 2, T // 4
         first = [a_sb[:, m, 0:T] for m in range(ROW_BLOCKS)]
         both = [a_sb[:, m, T : 2 * T] for m in range(ROW_BLOCKS)]
+        second = keep.tile([P, quarter], F32, name="second")
         for m in range(ROW_BLOCKS):
-            final = m + 1 == ROW_BLOCKS
-            if m == 0:
-                cuts = (0, VECTOR_FIRST, (VECTOR_FIRST + T) // 2, T)
-            elif final:
-                cuts = tuple(range(0, T + 1, half // 2))
-            else:
-                cuts = (0, half, T)
+            cuts = (0, half, T - quarter, T) if m + 1 == ROW_BLOCKS else (0, half, T)
             for lo, hi in zip(cuts, cuts[1:]):
-                window = dx[m][:].indirect(entries(pos1_sb, lo, hi - lo))
-                if m == 0 and lo == 0:
-                    nc.vector.tensor_copy(out=first[m][:, lo:hi], in_=window)
-                else:
-                    nc.scalar.activation(out=first[m][:, lo:hi], in_=window, func=ACT.Copy)
-                if lo == 0 and m == 0:
-                    for x in (1, 2):
-                        copy_out(nc.vector.tensor_copy, LATE, x, 0, C)
-                if hi == T and m == ROW_BLOCKS - 2:
-                    copy_out(nc.scalar.copy, LATE, m + 1, 0, C)
-            for lo, hi in zip(cuts, cuts[1:]):
-                nc.vector.tensor_tensor(
-                    out=both[m][:, lo:hi],
-                    in0=dx[m][:].indirect(entries(pos2_sb, lo, hi - lo)),
-                    in1=first[m][:, lo:hi],
-                    op=ALU.add,
+                nc.scalar.activation(
+                    out=first[m][:, lo:hi], in_=dx[m][:].indirect(entries(pos1_sb, lo, hi - lo)), func=ACT.Copy
                 )
+                window = dx[m][:].indirect(entries(pos2_sb, lo, hi - lo))
+                if (m + 1, hi) == (ROW_BLOCKS, T):
+                    nc.scalar.activation(out=second[:], in_=window, func=ACT.Copy)
+                    window = second[:]
+                nc.vector.tensor_tensor(out=both[m][:, lo:hi], in0=window, in1=first[m][:, lo:hi], op=ALU.add)
                 nc.sync.dma_start(out=out[m * P : (m + 1) * P, lo:hi], in_=both[m][:, lo:hi])

@@ -381,14 +381,17 @@ def tile_moe_sdb_silu_kernel(
             product(LATE, 0, lo, hi)
             if x == 0:
                 round_block(12)
-        for m in range(ROW_BLOCKS):
+        for m in range(ROW_BLOCKS - 1):
             copy_out(nc.scalar.copy, 0, m, 0, C)
+        shared = at["dx", 0, ROW_BLOCKS - 1, 0]
+        nc.scalar.copy(out=dx[ROW_BLOCKS - 1][:, 0 : C // 2], in_=shared[:, 0 : C // 2])
         for m in range(1, ROW_BLOCKS):
             product(LATE, m, 0, C)
         for lo, hi in pieces_late:
             copy_out(nc.vector.tensor_copy, LATE, 0, lo, hi)
         for m in range(1, ROW_BLOCKS):
             copy_out(nc.vector.tensor_copy, LATE, m, 0, C)
+        nc.vector.tensor_copy(out=dx[ROW_BLOCKS - 1][:, C // 2 : C], in_=shared[:, C // 2 : C])
 
         half, quarter = T // 2, T // 4
         first = [a_sb[:, m, 0:T] for m in range(ROW_BLOCKS)]

from contextlib import ExitStack

import concourse.mybir as mybir
from concourse.masks import make_identity

K, T, E, C, H, N = 512, 1024, 4, 512, 512, 512
SLOTS = E * C
FLOPS = 2 * N * H * T + 2 * H * K * SLOTS

F32 = mybir.dt.float32
BF16 = mybir.dt.bfloat16
I32 = mybir.dt.int32
U32 = mybir.dt.uint32
U16 = mybir.dt.uint16
U8 = mybir.dt.uint8
E2M1 = mybir.dt.float4_e2m1fn_x4
E4M3 = mybir.dt.float8_e4m3fn_x4
E5M2 = mybir.dt.float8_e5m2_x4
ACT = mybir.ActivationFunctionType
ALU = mybir.AluOpType

P = 128
PACK = 4
BANK = 512
BLOCKS = C // P
ROW_BLOCKS = K // P
PER_COLUMN = 16
QUADRANT = 32
GROUP = 4
SCALE_ROWS = 16
RUN = 4

BANKS = 8
EARLY = 384
FIRST = 2
WIDE = 3 * C
SPARE = WIDE + 16 - T
LATE = 3
TURNED = (
    [(e, b) for e in (FIRST, 1) for b in range(BLOCKS)]
    + [(0, b) for b in range(EARLY // P, BLOCKS)]
    + [(LATE, b) for b in range(BLOCKS)]
)
GATE_BANK = 7


def tile_moe_sdb_silu_kernel(
    tc, dy_words, dy_scales, w2t_words, w2t_scales, w1t_words, w1t_scales, a, gate, offs, pos1, pos2, out
):
    nc = tc.nc
    with ExitStack() as ctx:
        keep = ctx.enter_context(tc.tile_pool(name="keep", bufs=1))
        psum = ctx.enter_context(tc.psum_pool(name="psum", bufs=1))

        offs_sb = keep.tile([P, SLOTS // PER_COLUMN], U16, name="offs_sb")
        pos1_sb = keep.tile([P, T // PER_COLUMN], U16, name="pos1_sb")
        pos2_sb = keep.tile([P, T // PER_COLUMN], U16, name="pos2_sb")

        w2_raw = keep.tile([P, 2 * H], U8, name="w2_raw", align_bytes=64)
        w2_sc_raw = keep.tile([P, H], U8, name="w2_sc_raw", tag="w2_sc_raw", align_bytes=64)
        w2_codes = keep.tile([P, 2 * H], U8, name="w2_codes", align_bytes=64)
        w2_sc = keep.tile([P, H], U8, name="w2_sc", align_bytes=64)
        dy_codes = keep.tile([P, PACK * T], U8, name="dy_codes", align_bytes=64)
        dy_sc = keep.tile([P, T], U8, name="dy_sc", align_bytes=64)
        w1_codes = keep.tile([P, E, PACK * K], U8, name="w1_codes", align_bytes=64)
        w1_sc = keep.tile([P, E * K], U8, name="w1_sc", align_bytes=64)
        a_sb = keep.tile([P, PACK, SLOTS], F32, name="a_sb")
        sg = keep.tile([P, PACK, SLOTS], F32, name="sg")
        ident = keep.tile([P, P], F32, name="ident")
        gate_rows = keep.tile([P, P], F32, name="gate_rows")

        nc.gpsimd.memset(w2_sc_raw[:].bitcast(I32), 0)
        nc.gpsimd.memset(dy_sc[:].bitcast(I32), 0)
        nc.vector.memset(w1_sc[:].bitcast(I32), 0)
        nc.gpsimd.memset(gate_rows[:], 0.0)
        make_identity(nc, ident[:])

        def load_scale_rows(plane, rows):
            for r in range(GROUP):
                nc.sync.dma_start(out=plane[r:P:QUADRANT], in_=rows[r:SCALE_ROWS:GROUP])

        a_planes = a.rearrange("(p t) j -> p t j", t=PACK)
        nc.sync.dma_start(out=a_sb[:, 0:2, 0:EARLY], in_=a_planes[:, 0:2, 0:EARLY])
        nc.sync.dma_start(out=w2_raw[:].bitcast(I32), in_=w2t_words[0].bitcast(I32))
        load_scale_rows(w2_sc_raw[:].bitcast(I32), w2t_scales[0].bitcast(I32))
        nc.sync.dma_start(out=a_sb[:, 2:4, 0:EARLY], in_=a_planes[:, 2:4, 0:EARLY])
        nc.sync.dma_start(out=dy_codes[:].bitcast(I32), in_=dy_words[0].rearrange("p n d -> p (n d)").bitcast(I32))
        load_scale_rows(dy_sc[:].bitcast(I32), dy_scales[0].bitcast(I32))

        def pieces(t):
            cuts = (EARLY, 2 * C, WIDE) if t < 2 else (EARLY, WIDE)
            return list(zip(cuts, cuts[1:]))

        for t in range(PACK):
            for lo, hi in pieces(t) if t != 1 else [(EARLY, WIDE)]:
                nc.sync.dma_start(out=a_sb[:, t, lo:hi], in_=a_planes[:, t, lo:hi])
                if t == 0 and lo == EARLY:
                    nc.sync.dma_start(offs_sb[:], offs)
        for t in range(0, PACK, 2):
            nc.sync.dma_start(out=a_sb[:, t : t + 2, 3 * C : SLOTS], in_=a_planes[:, t : t + 2, 3 * C : SLOTS])
        nc.sync.dma_start(out=gate_rows[0 : SLOTS // P, :], in_=gate[0].rearrange("(r c) -> r c", c=P))
        nc.sync.dma_start(
            out=w1_codes[:].bitcast(I32), in_=w1t_words[:, 0].rearrange("e p k d -> p e (k d)").bitcast(I32)
        )
        load_scale_rows(
            w1_sc[:].bitcast(I32).rearrange("p (e k) -> p e k", e=E),
            w1t_scales[:, 0].bitcast(I32).rearrange("e b k -> b e k"),
        )
        nc.sync.dma_start(pos1_sb[:], pos1)
        nc.sync.dma_start(pos2_sb[:], pos2)

        nc.vector.tensor_copy(
            out=w2_codes[:].bitcast(U16).rearrange("p (t m) -> p t m", t=PACK),
            in_=w2_raw[:].bitcast(U16).rearrange("p (m t) -> p t m", t=PACK),
        )
        nc.vector.tensor_copy(
            out=w2_sc[:].rearrange("p (t m) -> p t m", t=PACK),
            in_=w2_sc_raw[:].rearrange("p (m t) -> p t m", t=PACK),
        )

        dc = [keep.tile([P, T + SPARE], F32, name="dc%d" % t, tag="dc%d" % t, align_bytes=64) for t in range(PACK)]
        picked_wide = keep.tile([P, PACK, WIDE], F32, name="picked_wide")
        picked = [picked_wide[:, :, e * C : (e + 1) * C] for e in range(LATE)]
        picked = picked + [keep.tile([P, PACK, C], F32, name="picked_late")[:]]
        late_dc = keep.tile([P, PACK - 1, C], F32, name="late_dc")
        places = {
            0: picked[LATE][:, 0, :],
            4: late_dc[:, 0, :],
            5: late_dc[:, 1, :],
            6: late_dc[:, 2, :],
            9: picked[LATE][:, 3, :],
        }
        u_at = [
            places[n] if n in places else keep.tile([P, PACK * P], F32, name="u%d" % n, tag="u%d" % n, align_bytes=64)[:]
            for n in range(len(TURNED))
        ]
        bank = [psum.tile([P, BANK], F32, name="bank%d" % n) for n in range(BANKS)]

        def entries(list_sb, first, count):
            return list_sb[:, first // PER_COLUMN : (first + count) // PER_COLUMN]

        for x in range(2):
            a_x, s_x = a_sb[:, 2 * x : 2 * x + 2, 0:EARLY], sg[:, 2 * x : 2 * x + 2, 0:EARLY]
            nc.scalar.activation(out=s_x, in_=a_x, func=ACT.Sigmoid)
            u_x = a_x
            if x == 0:
                u_x = keep.tile([P, 2, EARLY], F32, name="u_early", tag="w2_sc_raw", align_bytes=64)[:]
            nc.vector.scalar_tensor_tensor(out=u_x, in0=s_x, scalar=1.0, in1=a_x, op0=ALU.subtract, op1=ALU.mult)
            nc.vector.scalar_tensor_tensor(out=s_x, in0=u_x, scalar=1.0, in1=s_x, op0=ALU.subtract, op1=ALU.mult)

        def gather_plane(e, t, lo=0, hi=C):
            nc.vector.tensor_tensor(
                out=(picked_wide if e == 0 else picked[e])[:, t, lo:hi],
                in0=dc[t][:].indirect(entries(offs_sb, e * C + lo, hi - lo)),
                in1=sg[:, t, e * C + lo : e * C + hi],
                op=ALU.mult,
            )

        for t in range(PACK):
            for x, (lo, hi) in enumerate(pieces(t)):
                if x == 0:
                    for h in range(T // BANK):
                        tokens = slice(BANK * h, BANK * (h + 1))
                        dc_ps = bank[2 * t + h]
                        nc.tensor.matmul_mx(
                            out=dc_ps[:],
                            lhsT=w2_codes[:, 2 * P * t : 2 * P * (t + 1)].bitcast(E2M1),
                            lhsT_scale=w2_sc[:, P * t : P * (t + 1)],
                            rhs=dy_codes[:, PACK * BANK * h : PACK * BANK * (h + 1)].bitcast(E5M2),
                            rhs_scale=dy_sc[:, tokens],
                            start=True,
                            stop=True,
                        )
                        nc.scalar.copy(out=dc[t][:, tokens], in_=dc_ps[:])
                nc.scalar.activation(out=sg[:, t, lo:hi], in_=a_sb[:, t, lo:hi], func=ACT.Sigmoid)
            if t == 0:
                gather_plane(0, t, 0, EARLY)
                for lo, hi in pieces(t):
                    gather_plane(0, t, lo, hi)
            elif t == 1:
                gather_plane(0, t, 0, 2 * C)
                gather_plane(0, t, 2 * C, WIDE)
            else:
                gather_plane(0, t, 0, WIDE)
        for t in range(0, PACK, 2):
            nc.scalar.activation(
                out=sg[:, t : t + 2, 3 * C : SLOTS], in_=a_sb[:, t : t + 2, 3 * C : SLOTS], func=ACT.Sigmoid
            )

        gate_ps = bank[GATE_BANK]
        nc.tensor.transpose(gate_ps[:, 0:P], gate_rows[:], ident[:])
        g_col = keep.tile([P, SLOTS // P], F32, name="g_col")
        neg_g_col = keep.tile([P, SLOTS // P], F32, name="neg_g_col")
        nc.scalar.copy(out=g_col[:], in_=gate_ps[:, 0 : SLOTS // P])
        nc.scalar.mul(out=neg_g_col[:], in_=gate_ps[:, 0 : SLOTS // P], mul=-1.0)

        da_codes = {e: keep.tile([P, C], U32, name="da_codes%d" % e, align_bytes=64) for e in (0, LATE)}
        da_sc = [keep.tile([P, C], U8, name="da_sc%d" % e, align_bytes=64) for e in range(E)]
        da = {e: keep.tile([P, C, PACK], BF16, name="da%d" % e, tag="da%d" % e, align_bytes=64) for e in range(1, E)}
        dx = [keep.tile([P, SLOTS], F32, name="dx%d" % m) for m in range(ROW_BLOCKS)]

        def in_runs(planes_ap):
            return planes_ap.rearrange("p t (c i) -> p c t i", i=RUN)

        def planes_of(bank_tile):
            return bank_tile[:].rearrange("p (t s) -> p t s", t=PACK)

        def quantise(e, lo, hi):
            nc.vector.quantize_mx(
                out=da_codes[e][:, lo:hi].bitcast(E5M2),
                scales=da_sc[e][:, lo:hi],
                in_=da[e][:, lo:hi, :].rearrange("p j t -> p (j t)"),
            )

        gated = {}
        at = {}
        freed = []
        taken = []

        def take(key):
            at[key] = freed[len(taken)]
            taken.append(key)
            return at[key]

        def columns(n):
            e, b = TURNED[n]
            r = e * BLOCKS + b
            return neg_g_col[:, r : r + 1], g_col[:, r : r + 1]

        def turn(n):
            e, b = TURNED[n]
            r = e * BLOCKS + b
            a_turned = planes_of(take(("a", n)))
            for t in range(PACK):
                nc.tensor.transpose(a_turned[:, t, :], a_sb[:, t, r * P : (r + 1) * P], ident[:])

        def silu(n):
            nc.scalar.activation(out=u_at[n], in_=at["a", n][:], func=ACT.Silu, scale=-1.0)
            freed.append(at["a", n])

        def gate_scalar(n):
            neg_g, g = columns(n)
            gated[n] = keep.tile([P, PACK * P], F32, name="gated%d" % n)[:]
            nc.scalar.activation(out=gated[n], in_=u_at[n], func=ACT.Identity, scale=neg_g, bias=g)

        def gate_gpsimd(n, place=None, engine=nc.gpsimd):
            neg_g, g = columns(n)
            gated[n] = u_at[n] if place is None else place
            engine.tensor_scalar(out=gated[n], in0=u_at[n], scalar1=neg_g, scalar2=g, op0=ALU.mult, op1=ALU.add)

        def rounded(e, lo, hi):
            return da[e][:, lo:hi, :].rearrange("p (c i) t -> p c t i", i=RUN)

        def turn_back(n):
            gw_back = planes_of(take(("back", n)))
            for t in range(PACK):
                nc.tensor.transpose(gw_back[:, t, :], gated[n][:, t * P : (t + 1) * P], ident[:])

        def round_block(n):
            e, b = TURNED[n]
            nc.vector.tensor_tensor(
                out=rounded(e, b * P, (b + 1) * P),
                in0=in_runs(picked[e][:, :, b * P : (b + 1) * P]),
                in1=in_runs(planes_of(at["back", n])),
                op=ALU.mult,
            )
            freed.append(at["back", n])

        def product(e, m, lo, hi):
            nc.tensor.matmul_mx(
                out=(at["dx", e, m, lo] if ("dx", e, m, lo) in at else take(("dx", e, m, lo)))[:, 0 : hi - lo],
                lhsT=w1_codes[:, e, PACK * P * m : PACK * P * (m + 1)].bitcast(E4M3),
                lhsT_scale=w1_sc[:, e * K + P * m : e * K + P * (m + 1)],
                rhs=da_codes[e][:, lo:hi].bitcast(E5M2),
                rhs_scale=da_sc[e][:, lo:hi],
                start=True,
                stop=True,
            )

        def copy_out(engine_copy, e, m, lo, hi):
            engine_copy(out=dx[m][:, e * C + lo : e * C + hi], in_=at["dx", e, m, lo][:, 0 : hi - lo])
            freed.append(at["dx", e, m, lo])

        def spread_gate():
            neg_g = take("spread")
            for b in range(EARLY // P):
                nc.tensor.transpose(
                    neg_g[:, b * P : (b + 1) * P], neg_g_col[:, b : b + 1].to_broadcast([P, P]), ident[:]
                )

        def round_early():
            da[0] = keep.tile([P, C, PACK], BF16, name="da0", tag="dc0", align_bytes=64)
            runs = at["spread"][:, 0:EARLY].rearrange("p (c i) -> p c i", i=RUN).unsqueeze(2)
            nc.vector.tensor_tensor(
                out=rounded(0, 0, EARLY),
                in0=in_runs(picked[0][:, :, 0:EARLY]),
                in1=runs.to_broadcast([P, EARLY // RUN, PACK, RUN]),
                op=ALU.mult,
            )
            freed.append(at["spread"])

        freed.extend(bank)
        for n in range(BANKS):
            turn(n)
        silu(0)
        spread_gate()
        for n in range(1, 3):
            silu(n)
            turn(n + 7)
        gate_scalar(0)
        gate_gpsimd(2, None, nc.vector)
        gather_plane(E - 1, 0)
        silu(3)
        turn(10)
        for n in range(2):
            silu(n + 4)
            turn_back(n)
            if n == 0:
                gate_scalar(1)
        gate_gpsimd(3, sg[:, 0, (E - 1) * C : E * C])
        round_early()
        turn_back(2)
        silu(6)
        turn_back(3)
        round_block(0)
        gate_gpsimd(4, u_at[3])
        turn_back(4)
        silu(7)
        for n in range(5, 11):
            round_block(n - 4)
            gate_gpsimd(n)
            if n < 10:
                turn_back(n)
            if n + 3 < 11:
                silu(n + 3)
        for t in range(1, PACK):
            nc.scalar.activation(
                out=late_dc[:, t - 1, :], in_=dc[t][:].indirect(entries(offs_sb, LATE * C, C)), func=ACT.Copy
            )
        for m in range(ROW_BLOCKS):
            take(("dx", FIRST, m, 0))
        turn(11)
        round_block(7)
        turn(12)
        round_block(8)
        silu(11)
        silu(12)
        da_codes[FIRST] = keep.tile([P, C], U32, name="da_codes_first", tag="u8", align_bytes=64)
        quantise(FIRST, 0, C)
        for m in range(ROW_BLOCKS):
            product(FIRST, m, 0, C)
        da_codes[1] = keep.tile([P, C], U32, name="da_codes1", tag="da%d" % FIRST, align_bytes=64)
        quantise(1, 0, C)
        quantise(0, 0, C)
        gate_gpsimd(11, keep.tile([P, PACK * P], F32, name="gated11", tag="da1", align_bytes=64)[:], nc.vector)
        for m in range(3):
            product(1, m, 0, C)
        copy_out(nc.scalar.copy, FIRST, 0, 0, C)
        turn_back(10)
        copy_out(nc.scalar.copy, FIRST, 1, 0, C)
        turn_back(11)
        copy_out(nc.scalar.copy, FIRST, 2, 0, C)
        product(1, 3, 0, C)
        copy_out(nc.scalar.copy, FIRST, 3, 0, C)
        product(0, 0, 0, C)
        nc.vector.tensor_tensor(
            out=picked[LATE][:, 1:PACK, :], in0=late_dc[:], in1=sg[:, 1:PACK, LATE * C : (LATE + 1) * C], op=ALU.mult
        )
        round_block(9)
        gate_gpsimd(12, late_dc[:, 0, :])
        turn_back(12)
        round_block(10)
        for m in range(ROW_BLOCKS):
            copy_out(nc.scalar.copy, 1, m, 0, C)
        for m in range(1, ROW_BLOCKS):
            product(0, m, 0, C)
        round_block(11)
        pieces_late = ((0, C // 2), (C // 2, C - P), (C - P, C))
        for x, (lo, hi) in enumerate(pieces_late):
            quantise(LATE, lo, hi)
            product(LATE, 0, lo, hi)
            if x == 0:
                round_block(12)
        for m in range(ROW_BLOCKS - 1):
            copy_out(nc.scalar.copy, 0, m, 0, C)
        shared = at["dx", 0, ROW_BLOCKS - 1, 0]
        nc.scalar.copy(out=dx[ROW_BLOCKS - 1][:, 0 : C // 2], in_=shared[:, 0 : C // 2])
        for m in range(1, ROW_BLOCKS):
            product(LATE, m, 0, C)
        for lo, hi in pieces_late:
            copy_out(nc.vector.tensor_copy, LATE, 0, lo, hi)
        for m in range(1, ROW_BLOCKS):
            copy_out(nc.vector.tensor_copy, LATE, m, 0, C)
        nc.vector.tensor_copy(out=dx[ROW_BLOCKS - 1][:, C // 2 : C], in_=shared[:, C // 2 : C])

        half, quarter = T // 2, T // 4
        first = [a_sb[:, m, 0:T] for m in range(ROW_BLOCKS)]
        both = [a_sb[:, m, T : 2 * T] for m in range(ROW_BLOCKS)]
        second = keep.tile([P, quarter], F32, name="second")
        for m in range(ROW_BLOCKS):
            cuts = (0, half, T - quarter, T) if m + 1 == ROW_BLOCKS else (0, half, T)
            for lo, hi in zip(cuts, cuts[1:]):
                nc.scalar.activation(
                    out=first[m][:, lo:hi], in_=dx[m][:].indirect(entries(pos1_sb, lo, hi - lo)), func=ACT.Copy
                )
                window = dx[m][:].indirect(entries(pos2_sb, lo, hi - lo))
                if (m + 1, hi) == (ROW_BLOCKS, T):
                    nc.scalar.activation(out=second[:], in_=window, func=ACT.Copy)
                    window = second[:]
                nc.vector.tensor_tensor(out=both[m][:, lo:hi], in0=window, in1=first[m][:, lo:hi], op=ALU.add)
                nc.sync.dma_start(out=out[m * P : (m + 1) * P, lo:hi], in_=both[m][:, lo:hi])
